import numpy as np, ml_dtypes
CORES = [16,17,18,19,32,33,34,35]
N = 8
BF = ml_dtypes.bfloat16
def gentries(a):
    return np.ascontiguousarray(a.reshape(8, 16, -1).transpose(0, 2, 1)).reshape(8, -1)
def gtable(e):
    e = np.asarray(e); return np.ascontiguousarray(e.reshape(8, -1, 16).transpose(0, 2, 1)).reshape(128, -1).astype(np.int32)
W, C, PB, R, INC, RO = 3840, 4, 256, 12, 128, 8
V = C * PB
TOP = 4080
def procs():
    return np.ascontiguousarray(np.broadcast_to(np.arange(V).reshape(C, 1, PB), (C, R, PB))).reshape(-1)
def rows():
    return np.ascontiguousarray(np.broadcast_to(np.arange(R).reshape(1, R, 1), (C, R, PB))).reshape(-1)
def owners(rng, E, share, rich):
    P = procs(); O = rng.integers(0, V, (N, 2, 8, W))
    for q in range(N):
        for g in range(8):
            e = E[q, g].reshape(-1); w = rng.random(V) < rich
            for s in range(2):
                p = rng.permutation(R * V); o = O[q, s, g].copy(); o[e[p]] = P[p]
                o = np.where(rng.random(W) < share[q, g], o, O[q, s, g])
                i = np.nonzero(w[P] & (P % 2 == s))[0]; o[e[i]] = P[i]
                O[q, s, g] = o
    return O
def parts(rng):
    M = rng.integers(0, 256, (N, 8, 16, W)); Z = rng.integers(0, 256, (N, 8, 16, V)); K = rng.integers(0, W, (N, 8, W)); E = rng.integers(0, W, (N, 8, C, R, PB))
    O = owners(rng, E, rng.choice(np.array([0.25, 0.5, 0.75, 0.95]), (N, 8)), 0.06); T = rng.integers(500, 1500, (N, 8, V))
    return M, K, O, E, Z, T
def least(M, O, E, Z):
    P = procs(); out = np.zeros((N, 8, V), np.int64)
    for q in range(N):
        for g in range(8):
            e = E[q, g].reshape(-1); y = M[q, g][:, e].reshape(16, C, R, PB)
            d = np.add.reduce(np.abs(y - Z[q, g].reshape(16, C, 1, PB)), axis=0)
            live = ((O[q, 0, g][e] == P) | (O[q, 1, g][e] == P)).reshape(C, R, PB)
            out[q, g] = np.min(np.where(live, d, TOP), axis=1).reshape(V)
    return out
def pack(M, K, O, E, Z, T):
    return {"msg": np.ascontiguousarray(M.reshape(N, 128, W)).astype(np.float32).astype(BF), "enc": K.astype(np.int32), "own": np.ascontiguousarray(O.reshape(N, 16, W)).astype(np.int32),
            "ends": np.stack([gtable(a.reshape(8, -1)) for a in E]), "st": np.ascontiguousarray(Z.reshape(N, 128, V)).astype(np.float32).astype(BF), "th": T.astype(np.int32)}
def setup_inputs(rng):
    return pack(*parts(rng))
def setup_inputs_corners(rng):
    M, K, O, E, Z, T = parts(rng); P = procs(); k = rows(); ee = np.arange(W); c = W // V
    x = rng.random(K.shape); K = np.where(x < 0.2, ee, np.where(x < 0.35, 0, np.where(x < 0.5, W - 1, np.where(x < 0.8, (ee + 1) % W, K))))
    for q in range(N):
        for g in range(8):
            w = (q + g) % 4
            if w == 0:
                x = rng.random(W); O[q, 0, g] = np.where(x < 0.1, 0, np.where(x < 0.2, V - 1, O[q, 0, g])); O[q, 1, g] = np.where(x > 0.85, O[q, 0, g], O[q, 1, g])
                continue
            O[q, :, g, :c * V] = np.tile(np.arange(V), c)
            mine = P + V * rng.integers(0, c, P.shape); other = (P + rng.integers(1, V, P.shape)) % V + V * rng.integers(0, c, P.shape)
            pos = rng.choice(np.array([0, R - 1, int(rng.integers(0, R))]), V)[P]; full = (rng.random(V) < 0.5)[P]
            hit = full if w == 1 else (k == pos if w == 2 else k != pos)
            E[q, g] = np.where(hit, mine, other).reshape(C, R, PB)
            if w == 1 and g >= 4:
                M[q, g] = 160 + ((M[q, g] * 3) >> 3); Z[q, g] = Z[q, g] >> 3
    low = least(M, O, E, Z); x = rng.integers(0, 5, T.shape)
    T = np.where(x == 0, low, np.where(x == 1, np.minimum(low + 1, TOP), np.where(x == 2, 0, np.where(x == 3, TOP, T))))
    for q in range(N):
        g = 4 + (1 - q) % 4; T[q, g] = low[q, g] + rng.integers(0, 2, V) - INC
    return pack(M, K, O, E, Z, T)
def setup_inputs_crowd(rng):
    M, K, O, E, Z, T = parts(rng); P = procs(); k = rows(); O = rng.integers(0, V, O.shape); a = np.arange(V); u = a - a % 2
    for q in range(N):
        for g in range(8):
            w = g % 4; e = E[q, g].reshape(-1).copy(); pos = rng.integers(0, R, V); hit = k == pos[P]; one = (0, W - 1, int(rng.integers(0, W)))[(q + g // 4) % 3]
            T[q, g] = TOP
            if w == 2:
                e[hit] = u[P[hit]]; O[q, 0, g, :V] = u; O[q, 1, g, :V] = u + 1; K[q, g] = rng.choice(np.array([0, W - 1, W // 2]), W)
            elif w == 3:
                m = rng.random(e.shape) < 0.5; e = np.where(m, rng.choice(np.array([V, V + 1, W - 1]), e.shape), e)
                e[hit] = P[hit]; O[q, 0, g] = (0, V - 1)[(q + g // 4) % 2]; O[q, 1, g, :V] = a; T[q, g] = TOP * rng.integers(0, 2, V)
            else:
                e[hit] = P[hit]; O[q, 0, g, :V] = a; K[q, g] = one
                if w == 1:
                    for b in range(C): T[q, g, b * PB + (0 if g == 1 else int(rng.integers(0, PB)))] = 0
            E[q, g] = e.reshape(C, R, PB)
    return pack(M, K, O, E, Z, T)
def setup_inputs_ends(rng):
    x = rng.random((N, 8, 1, W)); M = np.where(x < 0.4, 255, np.where(x < 0.8, 0, 255 * rng.integers(0, 2, (N, 8, 16, W))))
    x = rng.random((N, 8, 1, V)); Z = np.where(x < 0.35, 255, np.where(x < 0.7, 0, 255 * rng.integers(0, 2, (N, 8, 16, V))))
    E = rng.integers(0, W, (N, 8, C, R, PB)); E = np.where(rng.random(E.shape) < 0.68, (W - 1) * rng.integers(0, 2, E.shape), E)
    O = owners(rng, E, np.ones((N, 8)), 0.0); O = np.where(rng.random(O.shape) < 0.65, (V - 1) * rng.integers(0, 2, O.shape), O)
    K = rng.integers(0, W, (N, 8, W)); K = np.where(rng.random(K.shape) < 0.7, (W - 1) * rng.integers(0, 2, K.shape), K)
    T = TOP * rng.integers(0, 2, (N, 8, V))
    T[:, 7, :V - PB] = 0; T[:, 7, V - 1] = TOP
    M[:, 7, :, W - 1] = 255; M[:, 7, :, 0] = 0; Z[:, 7, :, V - 1] = 0
    O[:, 0, 7, W - 1] = 0; O[:, 1, 7, W - 1] = V - 1; O[:, 0, 7, 0] = V - 1; O[:, 1, 7, 0] = 0
    k = np.arange(R); both = np.where((k % 2 == 1) | (k == R - 2), W - 1, 0)
    for q in range(N): E[q, 7, C - 1, :, PB - 1] = both if (N - 1 - q) % 2 == 0 else W - 1
    T[:, 6] = 0; T[:, 6, 0] = TOP
    M[:, 6, :, W - 1] = 255; M[:, 6, :, 0] = 0; Z[:, 6, :, 0] = 0; Z[:, 6, :, 1] = 0
    O[:, 0, 6, W - 1] = V - 1; O[:, 1, 6, W - 1] = 0; E[:, 6, 0, :, 0] = W - 1
    O[:, 0, 6, 0] = 1; E[:, 6, 0, :, 1] = 0; E[:, 6, 0, R - 1, 1] = W - 1
    return pack(M, K, O, E, Z, T)
def setup_inputs_spread(rng):
    M, K, O, E, Z, T = parts(rng)
    M = np.minimum((np.exp2(8.5 * rng.random((N, 8, 1, W))) * rng.random(M.shape)).astype(np.int64), 255)
    Z = np.minimum((np.exp2(8.5 * rng.random((N, 8, 1, V))) * rng.random(Z.shape)).astype(np.int64), 255)
    K = np.minimum((W * rng.random(K.shape) ** 3).astype(np.int64), W - 1); E = np.minimum((W * rng.random(E.shape) ** 2).astype(np.int64), W - 1)
    O = owners(rng, E, rng.choice(np.array([0.5, 0.8, 1.0]), (N, 8)), 0.03)
    O = np.where(rng.random(O.shape) < 0.15, np.minimum((V * rng.random(O.shape) ** 3).astype(np.int64), V - 1), O)
    T = np.minimum(np.exp2(12 * rng.random(T.shape)).astype(np.int64) - 1, TOP)
    return pack(M, K, O, E, Z, T)
def setup_inputs_ties(rng):
    M, K, O, E, Z, T = parts(rng); base = rng.integers(0, 3, (N, 8, 16, W)); top = (np.arange(8) % 2).reshape(1, 8, 1, 1)
    for q in range(N):
        for g in range(8):
            M[q, g] = base[q, g][:, rng.integers(0, 24, W)]
            z = M[q, g][:, rng.integers(0, W, V)]; Z[q, g] = np.where(rng.random(V) < 0.5, z, rng.integers(0, 3, (16, V)))
    E[:, ::3, :, 1::2] = E[:, ::3, :, 0::2]
    O = owners(rng, E, rng.choice(np.array([0.6, 0.9]), (N, 8)), 0.05)
    M = np.where(top == 1, 255 - M, M); Z = np.where(top == 1, 255 - Z, Z); T = rng.integers(0, 24, T.shape)
    T = np.where(rng.random(T.shape) < 0.2, rng.integers(0, 2, T.shape), T)
    return pack(M, K, O, E, Z, T)
def check_inputs(d):
    bad = []
    for k, hi in (("msg", 255), ("enc", W - 1), ("own", V - 1), ("ends", W - 1), ("st", 255), ("th", TOP)):
        a = np.asarray(d[k]).astype(np.float64)
        if not (np.min(a) >= 0 and np.max(a) <= hi): bad.append("range of " + k)
        elif np.any(a != np.floor(a)): bad.append("whole numbers of " + k)
    return bad
def first(name, ok):
    qi = np.arange(N)[:, None, None]; gi = np.arange(8)[None, :, None]; lane = np.arange(PB)
    low = np.full((N, 8, W), PB, np.int64); np.minimum.at(low, (qi, gi, name), np.where(ok, lane, PB))
    return ok & (low[qi, gi, name] == lane)
def pick(a, k):
    return np.take_along_axis(a, k[:, :, None, :], 2)[:, :, 0]
def reference(msg, enc, own, ends, st, th):
    M = msg.astype(np.float32).astype(np.int64).reshape(N, 8, 16, W); K = enc.astype(np.int64); O = own.astype(np.int64).reshape(N, 2, 8, W)
    E = np.stack([gentries(a) for a in ends]).astype(np.int64).reshape(N, 8, C, R, PB)
    Z = st.astype(np.float32).astype(np.int64).reshape(N, 8, 16, V); T = th.astype(np.int64)
    qi = np.arange(N)[:, None, None]; gi = np.arange(8)[None, :, None]; lane = np.arange(PB); far = 2 ** 20
    for t in range(RO):
        b = t % C; lo = b * PB; v = lo + lane
        e = E[:, :, b].copy(); z = Z[..., lo:lo + PB].copy(); flat = e.reshape(N, 8, R * PB)
        y = np.take_along_axis(M, flat[:, :, None, :], 3).reshape(N, 8, 16, R, PB)
        d = np.add.reduce(np.abs(y - z[:, :, :, None, :]), axis=2)
        o0 = np.take_along_axis(O[:, 0], flat, 2).reshape(e.shape); o1 = np.take_along_axis(O[:, 1], flat, 2).reshape(e.shape)
        live = (o0 == v) | (o1 == v); stale = np.logical_not(live); has = np.any(stale, axis=2)
        dl = np.where(live, d, far); f = np.argmin(dl, axis=2); fire = np.min(dl, axis=2) < T[..., lo:lo + PB]
        m = np.argmax(np.where(live, d, -1), axis=2); s = np.argmin(np.where(stale, d, far), axis=2); j = np.where(has, np.argmax(stale, axis=2), f)
        ef = pick(e, f); em = pick(e, m); es = pick(e, s)
        yf = np.take_along_axis(M, ef[:, :, None, :], 3); ys = np.take_along_axis(M, es[:, :, None, :], 3)
        c = np.take_along_axis(K, ef, 2); hop = np.take_along_axis(O[:, 0], es, 2); hint = E[qi, gi, hop // PB, s, hop % PB]
        fb = fire[:, :, None, :]; hb = has[:, :, None, :]
        zn = np.where(fb, np.abs(z - yf), np.where(hb, (z + ys) >> 1, z))
        E[qi, gi, b, np.where(fire, j, s), lane] = np.where(fire, c, np.where(has, hint, es))
        Z[..., lo:lo + PB] = zn; T[..., lo:lo + PB] += np.where(fire, 0, INC)
        q, g, i = np.nonzero(first(c, fire)); O[q, t & 1, g, c[q, g, i]] = lo + i
        q, g, i = np.nonzero(first(ef, fire)); to = (q + 1 + t % (N - 1)) % N; a = ef[q, g, i]
        M[to, g, :, a] = zn[q, g, :, i]; K[to, g, a] = em[q, g, i]
    return {"ym": M.reshape(N, 128, W).astype(np.float32).astype(BF), "yk": K.astype(np.float32), "yo": O.reshape(N, 16, W).astype(np.float32),
            "ye": np.stack([gtable(a.reshape(8, -1)) for a in E]).astype(np.float32), "yz": Z.reshape(N, 128, V).astype(np.float32).astype(BF), "yt": T.astype(np.float32)}

@@ -1,0 +1,481 @@
+from concourse.mybir import dt, AluOpType as ALU, ActivationFunctionType as AF
+from concourse.bass import DstId, RemoteDMATransfer
+
+W, PB, RO, NR = 3840, 256, 8, 8
+B = 1 << 21
+MAGIC = 12582912.0
+HDT = "float16"
+LASTM = 2
+OGV0 = 64
+OGV = 16
+CH = ((0, 4), (4, 8), (8, 10), (10, 11), (11, 12))
+
+F, BF, I, U = "float32", "bfloat16", "int32", "uint16"
+SCRATCH = {
+    "mt": ("sbuf", [128, 4096], BF), "ot": ("sbuf", [128, 3872], F), "kt": ("sbuf", [128, 4096], F),
+    "xx": ("sbuf", [128, 3072], BF), "wx": ("sbuf", [128, 5376], BF), "oa": ("sbuf", [128, 3072], BF),
+    "zt": ("sbuf", [128, 4096], BF),
+    "zo": ("sbuf", [128, 1024], BF), "ec": ("sbuf", [128, 768], F), "eo": ("sbuf", [128, 768], U),
+    "ei": ("sbuf", [128, 768], I), "eout": ("sbuf", [128, 768], F),
+    "oi": ("sbuf", [128, 720], I), "stg": ("sbuf", [128, 2160], F), "sti": ("sbuf", [128, 720], I), "hb": ("sbuf", [128, 480], BF),
+    "ti": ("sbuf", [128, 128], I), "tf": ("sbuf", [128, 128], F), "thb": ("sbuf", [128, 64], F), "tho": ("sbuf", [128, 64], F),
+    "ip": ("sbuf", [128, 4], I), "pc": ("sbuf", [128, 16], F), "cs": ("sbuf", [128, 16], F),
+    "mk": ("sbuf", [128, 16], F), "mk2": ("sbuf", [128, 4], F),
+    "i143": ("sbuf", [128, 144], F), "b128": ("sbuf", [128, 128], F), "x240": ("sbuf", [128, 256], F),
+    "h256": ("sbuf", [128, 256], F), "r256": ("sbuf", [128, 256], F), "lc0": ("sbuf", [128, 384], F), "bo0": ("sbuf", [128, 4], F),
+    "d20": ("sbuf", [128, 16], F), "bc0": ("sbuf", [128, 8], F),
+    "ww": ("sbuf", [128, 7 * 144], BF), "wh": ("sbuf", [128, 144], HDT), "wm": ("sbuf", [128, 8 * 128], BF), "idf": ("sbuf", [128, 128], F),
+    "lanec": ("sbuf", [128, 384], BF), "kc2": ("sbuf", [128, 192], BF), "kcn": ("sbuf", [128, 192], BF),
+    "cwc": ("sbuf", [128, 400], BF), "hc": ("sbuf", [128, 272], BF), "qc": ("sbuf", [128, 256], BF),
+    "dm": ("sbuf", [128, 16], F), "ch": ("sbuf", [128, 16], F), "bck": ("sbuf", [128, 12], U), "bcc": ("sbuf", [128, 24], U),
+    "vl": ("sbuf", [128, 512], F), "vt": ("sbuf", [128, 512], F),
+    "u0": ("sbuf", [128, 192], F), "uu": ("sbuf", [128, 192], F), "sc": ("sbuf", [128, 192], BF), "d0": ("sbuf", [128, 192], F),
+    "vq": ("sbuf", [128, 16], F),
+    "d1": ("sbuf", [128, 192], F), "d2": ("sbuf", [128, 192], F), "lead": ("sbuf", [128, 192], BF), "la": ("sbuf", [128, 192], BF),
+    "kb": ("sbuf", [128, 3, 192], F), "t1": ("sbuf", [128, 3, 96], F), "t2": ("sbuf", [128, 3, 48], F), "t3": ("sbuf", [128, 3, 16], F),
+    "rr": ("sbuf", [128, 3, 16], I), "rk": ("sbuf", [128, 3, 16], I), "off": ("sbuf", [128, 48], U),
+    "nf_": ("sbuf", [128, 512], BF),
+    "sb": ("sbuf", [128, 256], BF), "kg": ("sbuf", [128, 256], BF), "xs": ("sbuf", [128, 256], BF),
+    "crow": ("sbuf", [128, 384], F), "erow": ("sbuf", [128, 256], F), "keepv": ("sbuf", [128, 256], F),
+    "ma": ("sbuf", [128, 256], BF), "mm": ("sbuf", [128, 256], BF),
+    "ht": ("sbuf", [128, 256], F), "eq": ("sbuf", [128, 384], BF), "eq2": ("sbuf", [128, 256], BF),
+    "hs": ("sbuf", [128, 256], HDT), "emr": ("sbuf", [128, 256], F),
+    "sm": ("sbuf", [128, 28 * 16], F), "si": ("sbuf", [128, 16], I), "su": ("sbuf", [128, 5 * 16], U), "oc": ("sbuf", [128, 16], U),
+    "rowb": ("sbuf", [128, 16], BF), "so": ("sbuf", [128, 32], F), "ld": ("sbuf", [128, 192], F),
+    "sz": ("sbuf", [128, RO * 256], BF), "sn": ("sbuf", [128, RO * 32], U),
+    "lz": ("sbuf", [128, RO * 256], BF), "ln": ("sbuf", [128, RO * 32], U),
+}
+for _i in range(8):
+    SCRATCH["p%d" % _i] = ("psum", [128, 512], F)
+DSEMS = ["d%d" % i for i in range(48)]
+SEMAPHORES = ["cv", "cs", "cp", "cg", "sent"] + DSEMS + ["az%d" % t for t in range(RO)] + ["an%d" % t for t in range(RO)]
+
+
+def rank_program(g, core, T, topo):
+    rank = T.rank_of(core)
+    if rank is None:
+        return
+    ops, lastw, readers, nd = [], {}, {}, [0]
+
+    def deps(e, R, Wr):
+        d = set()
+        for k in R:
+            if k in lastw: d.add(lastw[k])
+            if k[0] == "P": d.update(x for x in readers.get(k, ()) if ops[x]["e"] != e)
+        for k in Wr:
+            for x in ([lastw[k]] if k in lastw else []) + readers.get(k, []):
+                if e != "p" or ops[x]["e"] != e: d.add(x)
+        return d
+
+    def add(e, fn, R, Wr, tok=None, ext=None):
+        ops.append({"e": e, "fn": fn, "d": deps(e, R, Wr), "tok": tok, "ext": ext})
+        n = len(ops) - 1
+        for k in R: readers.setdefault(k, []).append(n)
+        for k in Wr:
+            lastw[k] = n; readers[k] = []
+        return n
+
+    def dma(e, pairs, R, Wr):
+        name = DSEMS[nd[0]]; nd[0] += 1
+        q = g.sync if e == "y" else g.scalar
+        def fn():
+            for o, i in pairs: q.dma_start(o, i).then_inc(T.sem[name], 16)
+        return add(e, fn, R, Wr, tok=(name, 16 * len(pairs)))
+
+    V, S, P = g.vector, g.scalar, g.tensor
+    def ts(o, i, a, b, o0, o1, R, Wr):
+        add("v", (lambda: V.tensor_scalar(o, i, a, None, o0)) if o1 is None else (lambda: V.tensor_scalar(o, i, a, b, o0, o1)), R, Wr)
+    def tt(o, a, b, op, R, Wr, ext=None): add("v", lambda: V.tensor_tensor(o, a, b, op), R, Wr, ext=ext)
+    def cp(o, i, R, Wr, ext=None): add("v", lambda: V.tensor_copy(o, i), R, Wr, ext=ext)
+    def ms(o, c, Wr): add("v", lambda: V.memset(o, c), [], Wr)
+    def act(o, i, f, R, Wr, bias=0.0, scale=1.0, ext=None): add("s", lambda: S.activation(o, i, f, bias=bias, scale=scale), R, Wr, ext=ext)
+    def iota(o, pat, base, cm, Wr, isint=False):
+        add("g", (lambda: g.iota(o, pat, base, cm)) if isint else (lambda: g.iota(o, pat, base, cm, allow_small_or_imprecise_dtypes=True)), [], Wr)
+    def mm(lst, R, Wr):
+        def fn():
+            for x in lst: last = P.matmul(*x)
+            return last
+        add("p", fn, R, Wr)
+    def wrap(out, w, src, lo, hi, start, stop):
+        return [(out, w(r), src[:, lo + r:hi:16], start and r == 0, stop and r == 15) for r in range(16)]
+    def wset(i): return lambda r: T.ww[:, 144 * i + 15 - r:144 * i + 143 - r]
+    WD, WBIG, WU0, WU1, WN, WC, WP = [wset(i) for i in range(7)]
+    WH = lambda r: T.wh[:, 15 - r:143 - r]
+    ID, NID, BID, HID, RN, R3, I16, I16R = [T.wm[:, 128 * i:128 * i + 128] for i in range(8)]
+    pcol, rcol, p16, r2, r240, dcol, dcol2 = [T.pc[:, i:i + 1] for i in range(7)]
+    mk = lambda f: T.mk[:, f:f + 1]
+    mk2 = lambda f: T.mk2[:, f:f + 1]
+    sm = lambda i, n=1: T.sm[:, 16 * i:16 * (i + n)]
+    su = lambda i: T.su[:, 16 * i:16 * i + 16]
+    st = lambda a, b: T.stg[:, 240 * a:240 * b]
+    P0, P1, P2, P3, P4, P5, P6, P7 = [T["p%d" % i] for i in range(8)]
+    HCOL, Z0, Z1 = 3072, 3328, 4352
+    AK = ["A%d" % k for k in range(12)]; XK = ["X%d" % k for k in range(12)]; OAK = ["OA0", "OA1", "OA2"]
+    EK = ["E%d" % b for b in range(4)]; Z0K = ["Z0"]
+    ident, absf, relu, sign = AF.Identity, AF.Abs, AF.Relu, AF.Sign
+
+    dma("y", [(T.oi[:, 0:240], T.own[0:8, :]), (T.oi[:, 240:480], T.own[8:16, :])], [], ["oi"])
+    dma("y", [(T.ei[:, 0:192], T.ends[:, 0:192])], [], ["ei0"])
+    dma("y", [(T.zt[:, 256 * j:256 * j + 256], T.st[:, 0:256]) for j in range(4)], [], ["zt0"])
+    dma("y", [(T.mt[:, 0:W], T.msg[:])], [], ["M"])
+    iota(T.ip[:, 0:1], [[0, 1]], 0, 1, ["ip"], True)
+    iota(T.x240[:], [[1, 256]], 0, 0, ["x240"])
+    iota(T.i143[:], [[1, 144]], -15, 0, ["i143"])
+    iota(T.bo0[:], [[-256, 4]], -128, 0, ["bo0"])
+    iota(T.lc0[:], [[0, 24], [-16, 16]], 128, 0, ["lc0"])
+    iota(T.kcn[:], [[-1, 192]], 0, 0, ["kcn"])
+    iota(T.kc2[:], [[2, 192]], 0, 0, ["kc2"])
+    iota(T.b128[:], [[16, 8], [0, 16]], 0, 0, ["b128"])
+    iota(T.d20[:], [[16, 16]], W, 0, ["d20"])
+    iota(T.r256[:], [[0, 16], [1, 16]], 0, 0, ["r256"])
+    iota(T.h256[:], [[1, 16], [0, 16]], 0, 0, ["h256"])
+    iota(T.hc[:, 0:16], [[-1, 16]], 0, 0, ["hc0"])
+    iota(T.ch[:], [[1, 16]], 192, 0, ["ch"])
+    iota(T.bc0[:], [[2, 8]], 0, 0, ["bc0"])
+    ms(T.wx[:, 0:960], 0.0, AK[:4])
+    for j in range(4):
+        act(T.ot[:, 960 * j:960 * j + 960], T.wx[:, 0:960], AF.Copy, AK[:4], ["Of%d" % j])
+    OF = ["Of%d" % j for j in range(4)]; KF = ["Kf%d" % j for j in range(4)]
+    dma("s", [(T.oi[:, 480:720], T.enc[:])], [], ["ki"])
+    dma("s", [(T.ti[0:64, 16 * q:16 * q + 16], T.th[q, :]) for q in range(8)], [], ["ti"])
+    for j in range(4):
+        act(T.kt[:, 960 * j:960 * j + 960], T.wx[:, 0:960], AF.Copy, AK[:4], ["Kf%d" % j])
+    ts(T.ip[:, 1:2], T.ip[:, 0:1], 15, None, ALU.bitwise_and, None, ["ip"], ["ip1"])
+    ts(T.ip[:, 2:3], T.ip[:, 0:1], 112, None, ALU.bitwise_and, None, ["ip"], ["ip2"])
+    ts(T.ip[:, 3:4], T.ip[:, 0:1], 1, 7, ALU.arith_shift_right, ALU.bitwise_and, ["ip"], ["ip3"])
+    cp(T.pc[:, 0:4], T.ip[:], ["ip", "ip1", "ip2", "ip3"], ["pc"])
+    ts(r240, rcol, 240.0, None, ALU.mult, None, ["pc"], ["r240"])
+    ts(st(3, 4), T.x240[:, 0:240], r240, None, ALU.add, None, ["x240", "r240"], ["s3"])
+    ts(T.mk[:], T.x240[:, 0:16], rcol, None, ALU.is_equal, None, ["x240", "pc"], ["mk"])
+    cp(T.hb[:, 240:480], st(3, 4), ["s3"], ["hb1"])
+    ts(T.mk2[:], T.x240[:, 0:4], r2, None, ALU.is_equal, None, ["x240", "pc"], ["mk2"])
+    tt(st(5, 6), st(3, 4), T.hb[:, 240:480], ALU.subtract, ["s3", "hb1"], ["s5"])
+    cp(st(0, 2), T.oi[:, 0:480], ["oi"], ["s0"])
+    ts(T.sti[:, 0:240], T.oi[:, 0:240], 8, None, ALU.arith_shift_right, None, ["oi"], ["sti0"])
+    ts(T.sti[:, 240:480], T.oi[:, 0:240], 4, 15, ALU.arith_shift_right, ALU.bitwise_and, ["oi"], ["sti1"])
+    ts(T.sti[:, 480:720], T.oi[:, 0:240], 15, None, ALU.bitwise_and, None, ["oi"], ["sti2"])
+    dma("y", [(T.ot[f::16, 0:W], st(s, s + 1)) for f, s in ((2, 3), (3, 5), (0, 0), (1, 1))], ["s0", "s3", "s5"] + OF, ["Oa"])
+    ts(st(6, 7), T.sti[:, 0:240], 192.0, None, ALU.mult, None, ["sti0"], ["s6"])
+    cp(st(7, 9), T.sti[:, 240:720], ["sti1", "sti2"], ["s7"])
+    dma("y", [(T.ot[f::16, 0:W], st(s, s + 1)) for f, s in ((4, 6), (5, 7), (6, 8))], ["s6", "s7"] + OF, ["O"])
+    dma("y", [(T.wx[:, Z0:Z0 + 1024], T.st[:])], [], Z0K)
+    dma("y", [(T.ei[:, 192:768], T.ends[:, 192:768])], [], ["ei1"])
+    cp(T.eo[:, 0:192], T.ei[:, 0:192], ["ei0"], ["eo0"])
+    ts(T.cs[:, 0:4], T.bo0[:], mk2(0), None, ALU.mult, None, ["bo0", "mk2"], ["bo"])
+    def weights(i, w, w2=None):
+        ts(T.ww[:, 144 * i:144 * i + 144], T.i143[:], p16, w, ALU.is_equal, ALU.mult, ["i143", "pc", "mk", "mk2", "wp"], ["w%d" % i])
+    def diag(i, w):
+        ts(T.wm[:, 128 * i:128 * i + 128], T.x240[:, 0:128], pcol, w, ALU.is_equal, ALU.mult, ["x240", "pc"], ["m%d" % i])
+    weights(2, mk(0)); weights(3, mk(1)); weights(0, 256.0)
+    diag(0, 1.0); diag(1, -1.0)
+    ts(T.lanec[:], T.lc0[:], rcol, None, ALU.subtract, None, ["lc0", "pc"], ["lanec"])
+    mm([(P5[:, 272:464], ID, T.kc2[:], True, True)], ["m0", "kc2"], ["P5"])
+    ts(T.idf[:], T.x240[:, 0:128], pcol, None, ALU.is_equal, None, ["x240", "pc"], ["idf"])
+    ts(T.cs[:, 12:13], mk2(0), 1.0 / 16, None, ALU.mult, None, ["mk2"], ["wp"])
+    diag(3, 0.5); diag(6, 16.0); diag(7, 1.0 / 16)
+    weights(4, mk2(1)); weights(6, T.cs[:, 12:13]); weights(5, mk2(2)); weights(1, 4096.0)
+
+    def late_constants():
+        cp(st(2, 3), T.oi[:, 480:720], ["ki"], ["s2"])
+        cp(T.hb[:, 0:240], st(2, 3), ["s2"], ["hb0"])
+        tt(st(4, 5), st(2, 3), T.hb[:, 0:240], ALU.subtract, ["s2", "hb0"], ["s4"])
+        dma("y", [(T.kt[f::16, 0:W], st(s, s + 1)) for f, s in ((2, 2), (3, 4))], ["s2", "s4"] + KF, ["K"])
+        for b in range(1, 4):
+            dma("y", [(T.zt[:, 1024 * b + 256 * j:1024 * b + 256 * j + 256], T.st[:, 256 * b:256 * b + 256]) for j in range(4)], [], ["zt%d" % b])
+        ts(T.thb[:], P7[:, 0:64], 256.0, None, ALU.mult, None, ["P7"], ["th0", "th1", "th2", "th3"])
+        ts(T.vq[:], T.lanec[:, 0:16], -1.0 / 16, None, ALU.mult, None, ["lanec"], ["vq"])
+        ts(T.dm[:], T.d20[:], rcol, None, ALU.add, None, ["d20", "pc"], ["dm"])
+        ts(dcol, rcol, float(W), None, ALU.add, None, ["pc"], ["dcol"])
+        ts(dcol2, rcol, float(W + 16), None, ALU.add, None, ["pc"], ["dcol2"])
+        ms(T.qc[:], -0.25, ["qc"])
+        ms(T.cwc[:, 0:16], -2048.0, ["cwc0"])
+        ms(T.cwc[:, 272:400], -2048.0, ["cwc1"])
+        ts(T.eq2[:], T.r256[:], rcol, 8192.0, ALU.is_le, ALU.mult, ["r256", "pc"], ["eq2"])
+        ts(T.hc[:, 16:272], T.r256[:], 0.0, rcol, ALU.mult, ALU.subtract, ["r256", "pc"], ["hc"])
+        ts(T.cwc[:, 16:272], T.eq2[:], -2048.0, None, ALU.add, None, ["eq2"], ["cwc"])
+        ts(T.wm[:, 512:640], T.b128[:], p16, mk2(1), ALU.is_equal, ALU.mult, ["b128", "pc", "mk2"], ["m4"])
+        ts(T.wm[:, 640:768], T.b128[:], p16, mk(6), ALU.is_equal, ALU.mult, ["b128", "pc", "mk"], ["m5"])
+        ts(T.wh[:], T.i143[:], p16, None, ALU.is_equal, None, ["i143", "pc"], ["wh"])
+        ts(T.bck[:], T.x240[:, 0:12], 0.0, rcol, ALU.mult, ALU.add, ["x240", "pc"], ["bck"])
+        cp(T.bcc[:, 0:16], T.x240[:, 0:16], ["x240"], ["bcc"])
+        cp(T.bcc[:, 16:24], T.bc0[:], ["bc0"], ["bcc1"])
+        act(T.vl[:, 0:256], T.x240[:], ident, ["x240", "mk"], ["vl0"], scale=mk(0))
+        act(T.vl[:, 256:512], T.x240[:], ident, ["x240", "mk"], ["vl1"], scale=mk(1))
+        act(T.vt[:, 0:256], T.h256[:], ident, ["h256", "mk"], ["vt0"], scale=mk(5))
+        act(T.vt[:, 256:512], T.r256[:], ident, ["r256", "mk"], ["vt1"], scale=mk(6))
+        ts(T.cs[:, 10:11], mk(0), mk2(2), mk(6), ALU.add, ALU.add, ["mk", "mk2"], ["cs10"])
+        ts(T.cs[:, 5:6], mk(1), -1.0, 1.0, ALU.mult, ALU.add, ["mk"], ["keep5"])
+        ms(T.cs[:, 6:7], 0.0, ["keep6"])
+        ts(T.cs[:, 11:12], mk(4), 384.0, None, ALU.mult, None, ["mk"], ["cs11"])
+        ts(T.cs[:, 7:8], mk(1), 256.0, None, ALU.mult, None, ["mk"], ["keep7"])
+        ts(T.cs[:, 9:10], mk(1), 768.0, None, ALU.mult, None, ["mk"], ["keep9"])
+        ts(T.cs[:, 4:5], T.cs[:, 10:11], -1.0, 1.0, ALU.mult, ALU.add, ["cs10"], ["keep4"])
+        ts(T.cs[:, 8:9], mk(0), 512.0, T.cs[:, 11:12], ALU.mult, ALU.add, ["mk", "cs11"], ["keep8"])
+
+    def later_constants():
+        tt(T.vl[:, 0:256], T.vl[:, 0:256], T.vt[:, 0:256], ALU.add, ["vl0", "vt0"], ["vl0"])
+        tt(T.vl[:, 0:256], T.vl[:, 0:256], T.vt[:, 256:512], ALU.add, ["vl0", "vt1"], ["vl0"])
+
+    def owners(t, ogv):
+        b = t % 4
+        mm([(P1[:, 0:384], ID, T.lanec[:], True, False)], ["m0", "lanec"], ["P1"])
+        def part(e, lo, hi, key):
+            o, i = T.oa[:, 16 * lo:16 * hi], T.ot[:, 0:W].indirect(T.eo[:, 192 * b + lo:192 * b + hi])
+            R = ["O", "Oa", "eo%d" % b, "bo"]
+            if e == "s": act(o, i, ident, R, [key], bias=T.cs[:, b:b + 1])
+            else: ts(o, i, T.cs[:, b:b + 1], None, ALU.add, None, R, [key])
+        if ogv: part("v", 192 - ogv, 192, "OA3")
+        for j in ((2, 0, 1) if ogv == 64 else (0, 1, 2)):
+            if 64 * j < 192 - ogv: part("s", 64 * j, min(64 * j + 64, 192 - ogv), OAK[j])
+            mm(wrap(P1[:, 64 * j:64 * j + 64], WU0, T.oa, 1024 * j, 1024 * j + 1024, False, False)
+               + wrap(P1[:, 192 + 64 * j:256 + 64 * j], WU1, T.oa, 1024 * j, 1024 * j + 1024, False, j == (1 if ogv == 64 else 2)),
+               [OAK[j], "w2", "w3"] + (["OA3"] if j == 2 else []), ["P1"])
+    OAK = OAK + ["OA3"]
+
+    def arrive(t):
+        cp(T.mt[:].indirect(T.ln[:, 32 * t:32 * t + 16]), T.lz[:, 256 * t:256 * t + 256], [], ["M"],
+           ext=[("az%d" % t, cnt_in[t]), ("an%d" % t, cnt_in[t])])
+
+    def arrive_em(t):
+        act(T.emr[:], T.ot[:, 0:W].indirect(T.ln[:, 32 * t + 16:32 * t + 32]), ident, ["O", "Oa"], ["emr"], ext=[("an%d" % t, cnt_in[t])])
+
+    def arrive_k(t):
+        cp(T.kt[:].indirect(T.ln[:, 32 * t:32 * t + 16]), T.emr[:], ["emr"], ["K"])
+
+    dst = [T.cores[(rank + 1 + t % (NR - 1)) % NR] for t in range(RO)]
+    src = [T.cores[(rank - 1 - t % (NR - 1)) % NR] for t in range(RO)]
+    cnt_in = [len(topo.engines(s, core)) for s in src]
+    sent = [0]
+
+    def send(t, o, i, sem, R):
+        rid, pid, _ = topo.addr(dst[t]); m = topo.mask(core, dst[t])
+        sent[0] += len(topo.engines(core, dst[t]))
+        add("g", lambda: g.remote_dma(o, i, T.sem[sem], T.sem.sent, pid, rid, m), R, [], tok=("sent", 0))
+
+    nf, cm, colf, tc, hp, new, fa, jj, nhd, clb, tab, fav, f0, pu1, t1, nhs = [sm(i) for i in range(16)]
+    nfb, fb, hasp, nhp, k0p, sn_, ra, rb = [sm(16 + i) for i in range(8)]
+
+    def list_mask():
+        act(T.la[:], P4[:, 0:192], absf, ["P4"], ["la"])
+        act(P4[:, 192:384], T.la[:], relu, ["la"], ["P4"], bias=1.0, scale=-1.0)
+
+    def hints(t):
+        cp(su(2), colf, ["colf"], ["colu"])
+        ts(fb, nfb, -1.0, 32768.0, ALU.mult, ALU.add, ["nfb"], ["fb"])
+        tt(T.hs[:], T.ec[:].indirect(su(2)), T.mm[:], ALU.mult, EK + ["colu", "mm"], ["hs"])
+        tt(k0p, k0p, jj, ALU.min, ["k0p", "jj"], ["k0p"])
+        tt(sm(22, 2), sm(20, 2), sm(16, 2), ALU.add, ["k0p", "sn_", "nfb", "fb"], ["rab"])
+        tt(T.rowb[:], ra, rb, ALU.min, ["rab"], ["rowb"])
+
+    def hints_p():
+        mm([(P4[:, 0:192], ID, T.kcn[:], True, False)]
+           + [(P4[:, 16 * k:16 * k + 16], ID, T.rowb[:], False, k == 11) for k in range(12)], ["rowb", "m0", "kcn"], ["P4"])
+        mm(wrap(P7[:, 0:16], WH, T.hs, 0, 256, True, True), ["hs", "wh"], ["P7"])
+
+    def hints_b():
+        tt(hp, P7[:, 0:16], fb, ALU.add, ["P7", "fb"], ["hp"])
+        tt(new, hp, cm, ALU.min, ["hp", "cm"], ["new"])
+
+    def list_update(t):
+        b = t % 4; eb = T.ec[:, 192 * b:192 * b + 192]
+        yield tt(T.ld[:], new.indirect(T.bck[:]), eb, ALU.subtract, ["new", "bck", EK[b]], ["ld"])
+        yield tt(P4[:, 0:192], T.ld[:], P4[:, 192:384], ALU.mult, ["P4", "ld"], ["P4"])
+        yield tt(eb, eb, P4[:, 0:192], ALU.add, [EK[b], "P4"], [EK[b]])
+        if t < 4:
+            yield ts(T.eo[:, 192 * b:192 * b + 192], eb, 2048.0, None, ALU.add, None, [EK[b]], ["eo%d" % b])
+
+    def list_out(t):
+        b = t % 4
+        act(T.eout[:, 192 * b:192 * b + 192], T.ec[:, 192 * b:192 * b + 192], ident, [EK[b]], ["eout%d" % b], bias=2048.0)
+        dma("y", [(T.ye[:, 192 * b:192 * b + 192], T.eout[:, 192 * b:192 * b + 192])], ["eout%d" % b], [])
+
+    def live():
+        act(T.u0[:], P1[:, 0:192], ident, ["P1"], ["u0"])
+        tt(T.uu[:], T.u0[:], P1[:, 192:384], ALU.mult, ["u0", "P1"], ["uu"])
+        ts(T.d0[:], T.uu[:], 0.0, float(B), ALU.not_equal, ALU.mult, ["uu"], ["d0"])
+        ts(T.d1[:], T.uu[:], 0.0, float(B), ALU.is_equal, ALU.mult, ["uu"], ["d1"])
+        tt(T.d2[:], T.d0[:], P5[:, 272:464], ALU.add, ["d0", "P5"], ["d2"])
+
+    for t in range(RO):
+        b = t % 4; lo = 256 * b
+        zb = (Z0 if t < 4 else Z1) + lo; zk = "Z0" if t < 4 else "Z1_%d" % b
+        zc = T.wx[:, zb:zb + 256]
+        if t:
+            arrive(t - 1)
+        mm([(P0[:, 0:192], NID, T.kcn[:], True, False)], ["m1", "kcn"], ["P0"])
+        for a, e in CH:
+            tt(T.xx[:, 256 * a:256 * e], T.mt[:, 0:W].indirect(T.eo[:, 192 * b + 16 * a:192 * b + 16 * e]),
+               T.zt[:, 1024 * b:1024 * b + 256 * (e - a)], ALU.subtract, ["M", "eo%d" % b, "zt%d" % b], XK[a:e])
+        if t: hints(t - 1)
+        for a, e in CH:
+            act(T.wx[:, 256 * a:256 * e], T.xx[:, 256 * a:256 * e], absf, XK[a:e], AK[a:e])
+            if a == 0 and t: live()
+            if e % 4 == 0:
+                j = e // 4 - 1
+                mm(wrap(P0[:, 64 * j:64 * j + 64], WD, T.wx, 1024 * j, 1024 * j + 1024, False, j == 2), AK[4 * j:4 * j + 4] + ["w0"], ["P0"])
+        if t:
+            hints_p(); arrive_em(t - 1)
+        else:
+            cp(T.tf[0:64, :], T.ti[0:64, :], ["ti"], ["tf"])
+            add("p", lambda: P.transpose(P7[:, 0:64], T.tf[0:64, :], T.idf[0:64, 0:64]), ["tf", "idf"], ["P7"])
+            owners(0, OGV0); late_constants(); live()
+        act(T.sc[:], T.d0[:], ident, ["d0"], ["stale"], scale=1.0 / B)
+        mm([(P6[:, 16 * s:192], ID, T.sc[:, 0:192 - 16 * s], s == 0, s == 11) for s in range(12)], ["stale", "m0"], ["P6"])
+        if t: list_mask()
+        act(T.lead[:], P6[:, 0:192], relu, ["P6"], ["lead"], bias=1.0, scale=-1.0)
+        mm([(P6[:, 192:208], NID, T.kcn[:, 0:16], True, False)]
+           + [(P6[:, 192:208], I16, T.lead[:, 16 * k:16 * k + 16], False, k == 11) for k in range(12)], ["lead", "m1", "m6", "kcn"], ["P6"])
+        tt(T.kb[:, 0, :], P0[:, 0:192], T.d0[:], ALU.add, ["P0", "d0"], ["kb0"])
+        tt(T.kb[:, 1, :], P0[:, 0:192], T.d1[:], ALU.add, ["P0", "d1"], ["kb1"])
+        tt(T.kb[:, 2, :], T.d2[:], P0[:, 0:192], ALU.subtract, ["P0", "d2"], ["kb2"])
+        tt(T.t1[:], T.kb[:, :, 0:96], T.kb[:, :, 96:192], ALU.min, ["kb0", "kb1", "kb2"], ["t1"])
+        tt(T.t2[:], T.t1[:, :, 0:48], T.t1[:, :, 48:96], ALU.min, ["t1"], ["t2"])
+        tt(T.t3[:], T.t2[:, :, 0:16], T.t2[:, :, 16:32], ALU.min, ["t2"], ["t3"])
+        tt(T.rr[:], T.t3[:], T.t2[:, :, 32:48], ALU.min, ["t2", "t3"], ["rr"])
+        ts(T.rk[:], T.rr[:], 255, None, ALU.bitwise_and, None, ["rr"], ["rk"])
+        ts(T.off[:], T.rk[:], 16.0, rcol, ALU.mult, ALU.add, ["rk", "pc"], ["off"])
+        R0, K0, K1 = T.rr[:, 0, :], T.rk[:, 0, :], T.rk[:, 1, :]
+        of, os_, om = T.off[:, 0:16], T.off[:, 16:32], T.off[:, 32:48]
+        thb = T.thb[:, 16 * b:16 * b + 16]; tk = "th%d" % b
+        lu = list_update(t - 1) if t else iter(())
+        mm([(P2[:, 0:384], ID, T.cwc[:, 16:400], True, False)], ["m0", "cwc", "cwc1"], ["P2"])
+        mm([(P1[:, 0:16], ID, T.cwc[:, 0:16], True, False)], ["m0", "cwc0"], ["P1"])
+        act(T.nf_[:, 0:256], T.oa[:].indirect(of), ident, OAK + ["off"], ["nbf"])
+        act(T.nf_[:, 256:512], T.oa[:].indirect(om), ident, OAK + ["off"], ["nbm"])
+        mm([(P0[:, 0:16], I16R, T.lanec[:, 0:16], True, False)] + wrap(P0[:, 0:16], WP, T.nf_, 0, 256, False, True),
+           ["nbf", "w6", "m7", "lanec"], ["P0"])
+        mm(wrap(P3[:, 0:32], WN, T.nf_, 0, 512, True, True), ["nbf", "nbm", "w4"], ["P3"])
+        mm([(P5[:, 16:272], RN, T.nf_[:, 0:256], True, True)], ["nbf", "m4"], ["P5"])
+        act(T.sz[:, 256 * t:256 * t + 256], T.wx[:, 0:3072].indirect(of), ident, AK + ["off"], ["sz%d" % t])
+        send(t, T.lz[:, 256 * t:256 * t + 256], T.sz[:, 256 * t:256 * t + 256], "az%d" % t, ["sz%d" % t])
+        act(nhp, P6[:, 192:208], relu, ["P6"], ["nhp"], bias=-256.0 * 191, scale=256.0)
+        act(jj, P6[:, 192:208], ident, ["P6"], ["jj"])
+        act(nhs, nhp, sign, ["nhp"], ["nhs"])
+        act(hasp, P6[:, 192:208], relu, ["P6"], ["hasp"], bias=256.0 * 192, scale=-256.0)
+        act(nhd, nhs, ident, ["nhs"], ["nhd"], scale=float((zb - HCOL) // 16))
+        tt(nf, R0, thb, ALU.is_ge, ["rr", tk], ["nf"])
+        if t: arrive_k(t - 1)
+        else:
+            cp(T.eo[:, 192:768], T.ei[:, 192:768], ["ei1"], ["eo1", "eo2", "eo3"])
+            ts(T.ec[:], T.ei[:], -2048.0, None, ALU.add, None, ["ei0", "ei1"], EK)
+        ts(nfb, nf, 32768.0, None, ALU.mult, None, ["nf"], ["nfb"])
+        cp(su(0), P3[:, 0:16], ["P3"], ["efu"])
+        act(T.kg[:], T.kt[:, 0:W].indirect(su(0)), ident, ["K", "efu"], ["kg"])
+        tt(f0, P3[:, 0:16], nfb, ALU.add, ["P3", "nfb"], ["f0"])
+        cp(T.sn[:, 32 * t + 16:32 * t + 32], P3[:, 16:32], ["P3"], ["sm%d" % t])
+        if t: hints_b()
+        mm([(P2[:, 0:256], RN, T.kg[:], False, False)]
+           + [(P2[:, 256 + 16 * m:272 + 16 * m], RN, T.kg[:, 32 * m + 16:32 * m + 32], False, m == 7) for m in range(8)], ["kg", "m4"], ["P2"])
+        mm(wrap(P1[:, 0:16], WN, T.kg, 0, 256, False, True), ["kg", "w4"], ["P1"])
+        act(T.erow[:], P5[:, 16:272], ident, ["P5"], ["erow"])
+        act(T.crow[:], P2[:, 0:384], ident, ["P2"], ["crow"])
+        tt(clb, P0[:, 0:16], T.vq[:], ALU.is_lt, ["P0", "vq"], ["clb"])
+        ts(pu1, P0[:, 0:16], 7.53125, MAGIC, ALU.add, ALU.add, ["P0"], ["pu1"])
+        ts(clb, clb, 4096.0, None, ALU.mult, None, ["clb"], ["clb"])
+        ts(su(4), pu1, -MAGIC, 15.0, ALU.add, ALU.min, ["pu1"], ["pu"])
+        tt(fav, f0, clb, ALU.add, ["f0", "clb"], ["fav"])
+        tt(thb, thb, nfb, ALU.add, [tk, "nfb"], [tk])
+        tt(T.eq2[:], fav.indirect(su(4)), T.erow[:], ALU.is_equal, ["fav", "pu", "erow"], ["eq2"])
+        mm(wrap(P0[:, 16:32], WBIG, T.eq2, 0, 256, True, True), ["eq2", "w1"], ["P0"])
+        tt(cm, P1[:, 0:16], nfb, ALU.add, ["P1", "nfb"], ["cm"])
+        ts(su(1), P1[:, 0:16], 2048.0, None, ALU.add, None, ["P1"], ["cu"])
+        tt(T.eq[:], cm.indirect(T.bcc[:]), T.crow[:], ALU.is_equal, ["cm", "bcc", "bcc1", "crow"], ["eq"])
+        mm(wrap(P1[:, 32:56], WBIG, T.eq, 0, 384, True, True), ["eq", "w1"], ["P1"])
+        tt(t1, P0[:, 16:32], clb, ALU.min, ["P0", "clb"], ["t1_"])
+        tt(fa, nhd, T.ch[:], ALU.add, ["nhd", "ch"], ["fa"])
+        tt(t1, t1, f0, ALU.add, ["t1_", "f0"], ["t1_"])
+        tt(fa, fa, nf, ALU.mult, ["fa", "nf"], ["fa"])
+        tt(T.so[:, 0:16], t1, T.dm[:], ALU.min, ["t1_", "dm"], ["soa"])
+        tt(fa, fa, K0, ALU.max, ["fa", "rk"], ["fa"])
+        cp(T.sn[:, 32 * t:32 * t + 16], T.so[:, 0:16], ["soa"], ["sn%d" % t])
+        send(t, T.ln[:, 32 * t:32 * t + 32], T.sn[:, 32 * t:32 * t + 32], "an%d" % t, ["sn%d" % t, "sm%d" % t])
+        if t == 0: later_constants()
+        act(T.keepv[:], T.ot[:, 0:W].indirect(su(1)), ident, ["O", "Oa", "cu", "keep%d" % (4 + b % 2), "keep%d" % (6 + b)], ["keepv"],
+            bias=T.cs[:, 6 + b:7 + b], scale=T.cs[:, 4 + b % 2:5 + b % 2])
+        act(T.sb[:], T.oa[:].indirect(os_), ident, OAK + ["off"], ["sb"])
+        mm([(P7[:, 0:272], ID, T.hc[:], True, False), (P7[:, 16:272], R3, T.sb[:], False, False)]
+           + wrap(P7[:, 0:16], WC, T.sb, 0, 256, False, True), ["sb", "w5", "m0", "m5", "hc", "hc0"], ["P7"])
+        act(T.xs[:], T.xx[:].indirect(os_), ident, XK + ["off"], ["xs"])
+        mm([(P6[:, 0:256], ID, T.qc[:], True, False), (P6[:, 0:256], ID, zc, False, False), (P6[:, 0:256], HID, T.xs[:], False, True)],
+           ["xs", zk, "qc", "m0", "m3"], ["P6"])
+        tt(tc, P1[:, 32:48], cm, ALU.add, ["P1", "cm"], ["tc"])
+        tco = T.sm[:, 16 * 3 + 1:16 * 4:2]; tce = T.sm[:, 16 * 3:16 * 4:2]
+        tt(tco, tco, P1[:, 48:56], ALU.add, ["P1", "tc"], ["tco"])
+        ts(T.oc[:, 0:16:2], tce, 2048.0, dcol, ALU.add, ALU.min, ["tc", "dcol"], ["oce"])
+        ts(T.oc[:, 1:16:2], tco, 2048.0, dcol2, ALU.add, ALU.min, ["tco", "dcol2"], ["oco"])
+        act(T.ma[:], P7[:, 16:272], absf, ["P7"], ["ma"])
+        act(T.mm[:], T.ma[:], relu, ["ma"], ["mm"], bias=1.0, scale=-1.0)
+        act(T.ht[:], P6[:, 0:256], ident, ["P6"], ["ht"], bias=MAGIC)
+        act(T.wx[:, HCOL:HCOL + 256], T.ht[:], ident, ["ht"], ["H"], bias=-MAGIC)
+        fill = [
+            lambda: ts(su(3), fa, 16.0, rcol, ALU.mult, ALU.add, ["fa", "pc"], ["fo"]),
+            lambda: next(lu, None), lambda: next(lu, None), lambda: next(lu, None), lambda: next(lu, None),
+            lambda: tt(colf, P7[:, 0:16], K1, ALU.add, ["P7", "rk"], ["colf"]),
+            lambda: tt(sm(20, 2), T.rk[:, 0:2, :], sm(18, 2), ALU.add, ["rk", "hasp", "nhp"], ["k0p", "sn_"]),
+        ]
+        vb = 256 * (b % 2)
+        for m in range(7, -1, -1):
+            tt(T.ot[:].indirect(T.oc[:, 2 * m:2 * m + 2]), T.keepv[:, 32 * m:32 * m + 32], T.vl[:, vb + 32 * m:vb + 32 * m + 32], ALU.add,
+               ["oce", "oco", "keepv", "vl0", "vl1"], ["O", "Oa"])
+            if fill: fill.pop(0)()
+            if t == RO - 1 and m == LASTM:
+                arrive(t)
+                dma("y", [(T.ym[:], T.mt[:, 0:W])], ["M"], [])
+        if t < 4:
+            act(T.wx[:, Z1 + lo:Z1 + lo + 256], T.wx[:, 0:Z1].indirect(su(3)), ident, AK + ["H", "fo", "Z0"], ["Z1_%d" % b])
+            dma("y", [(T.zt[:, 1024 * b + 256 * j:1024 * b + 256 * j + 256], T.wx[:, Z1 + lo:Z1 + lo + 256]) for j in range(4)],
+                ["Z1_%d" % b], ["zt%d" % b])
+        else:
+            act(T.zo[:, lo:lo + 256], T.wx[:].indirect(su(3)), ident, AK + ["H", "fo", zk], ["zo%d" % b])
+            dma("y", [(T.yz[:, lo:lo + 256], T.zo[:, lo:lo + 256])], ["zo%d" % b], [])
+        if t > 4: list_out(t - 1)
+        if t == RO - 2: dma("y", [(T.yo[0:8, :], T.ot[0::16, 0:W])], ["O", "Oa"], [])
+        if t == RO - 1: dma("y", [(T.yo[8:16, :], T.ot[1::16, 0:W])], ["O", "Oa"], [])
+        if t == RO - 1:
+            act(T.tho[:], T.thb[:], ident, ["th0", "th1", "th2", "th3"], ["tho"], scale=1.0 / 256)
+            add("p", lambda: P.transpose(P3[0:64, 0:128], T.tho[:], T.idf[:]), ["tho", "idf"], ["P3"])
+            arrive_em(t)
+            act(T.tf[0:64, :], P3[0:64, 0:128], ident, ["P3"], ["tf"])
+            dma("s", [(T.yt[q, :], T.tf[0:64, 16 * q:16 * q + 16]) for q in range(8)], ["tf"], [])
+            hints(t); hints_p()
+            arrive_k(t)
+            dma("y", [(T.yk[:], T.kt[2::16, 0:W])], ["K"], [])
+        if t + 1 < RO: owners(t + 1, OGV)
+    list_mask(); hints_b()
+    for _ in list_update(RO - 1): pass
+    list_out(RO - 1)
+
+    queue = {"v": V, "s": S, "p": P, "g": g, "y": g.sync}
+    csem = {"v": "cv", "s": "cs", "p": "cp", "g": "cg"}
+    needed = set()
+    for o in ops:
+        best = {}
+        for x in o["d"]:
+            if ops[x]["tok"] is None: best[ops[x]["e"]] = max(best.get(ops[x]["e"], -1), x)
+        o["d"] = [x for x in o["d"] if ops[x]["tok"] is not None] + list(best.values())
+    seen = {e: {} for e in queue}
+    for o in ops:
+        keep = []
+        for x in o["d"]:
+            if ops[x]["tok"] is None:
+                if seen[o["e"]].get(ops[x]["e"], -1) >= x: continue
+                seen[o["e"]][ops[x]["e"]] = x; needed.add(x)
+            keep.append(x)
+        o["d"] = keep
+    count = {e: 0 for e in csem}
+    waited = {e: {} for e in queue}
+    done = set()
+    for n, o in enumerate(ops):
+        e = o["e"]
+        for name, val in [ops[x]["tok"] for x in o["d"]] + list(o["ext"] or []):
+            if waited[e].get(name, 0) < val:
+                queue[e].wait_ge(T.sem[name], val); waited[e][name] = val; done.add(name)
+        ins = o["fn"]()
+        if n in needed:
+            count[e] += 1
+            ins.then_inc(T.sem[csem[e]], 1)
+            o["tok"] = (csem[e], count[e])
+    for o in ops:
+        if o["tok"] is not None and o["tok"][0] in DSEMS and o["tok"][0] not in done:
+            g.sync.wait_ge(T.sem[o["tok"][0]], o["tok"][1])
+    g.wait_ge(T.sem.sent, sent[0])

@@ -5,9 +5,12 @@ W, PB, RO, NR = 3840, 256, 8, 8
 B = 1 << 21
 MAGIC = 12582912.0
 HDT = "float16"
-LASTM = 2
+CYC, GATHER, SCATTER, WAKE, REM, SLACK = 0.95e-3, 1.56, 3.8, 0.1, 3.0, 0.03
+EMSPLIT = True
+EMSEND = False
+LIVES = 1
 OGV0 = 64
-OGV = 16
+OGV = 0
 CH = ((0, 4), (4, 8), (8, 10), (10, 11), (11, 12))
 
 F, BF, I, U = "float32", "bfloat16", "int32", "uint16"
@@ -27,7 +30,7 @@ SCRATCH = {
     "ww": ("sbuf", [128, 7 * 144], BF), "wh": ("sbuf", [128, 144], HDT), "wm": ("sbuf", [128, 8 * 128], BF), "idf": ("sbuf", [128, 128], F),
     "lanec": ("sbuf", [128, 384], BF), "kc2": ("sbuf", [128, 192], BF), "kcn": ("sbuf", [128, 192], BF),
     "cwc": ("sbuf", [128, 400], BF), "hc": ("sbuf", [128, 272], BF), "qc": ("sbuf", [128, 256], BF),
-    "dm": ("sbuf", [128, 16], F), "ch": ("sbuf", [128, 16], F), "bck": ("sbuf", [128, 12], U), "bcc": ("sbuf", [128, 24], U),
+    "dm": ("sbuf", [128, 16], F), "ch": ("sbuf", [128, 16], BF), "bck": ("sbuf", [128, 12], U), "bcc": ("sbuf", [128, 24], U),
     "vl": ("sbuf", [128, 512], F), "vt": ("sbuf", [128, 512], F),
     "u0": ("sbuf", [128, 192], F), "uu": ("sbuf", [128, 192], F), "sc": ("sbuf", [128, 192], BF), "d0": ("sbuf", [128, 192], F),
     "vq": ("sbuf", [128, 16], F),
@@ -41,6 +44,7 @@ SCRATCH = {
     "ht": ("sbuf", [128, 256], F), "eq": ("sbuf", [128, 384], BF), "eq2": ("sbuf", [128, 256], BF),
     "hs": ("sbuf", [128, 256], HDT), "emr": ("sbuf", [128, 256], F),
     "sm": ("sbuf", [128, 28 * 16], F), "si": ("sbuf", [128, 16], I), "su": ("sbuf", [128, 5 * 16], U), "oc": ("sbuf", [128, 16], U),
+    "fbb": ("sbuf", [128, 16], BF), "newh": ("sbuf", [128, 16], HDT), "idh": ("sbuf", [128, 128], HDT),
     "rowb": ("sbuf", [128, 16], BF), "so": ("sbuf", [128, 32], F), "ld": ("sbuf", [128, 192], F),
     "sz": ("sbuf", [128, RO * 256], BF), "sn": ("sbuf", [128, RO * 32], U),
     "lz": ("sbuf", [128, RO * 256], BF), "ln": ("sbuf", [128, RO * 32], U),
@@ -48,54 +52,69 @@ SCRATCH = {
 for _i in range(8):
     SCRATCH["p%d" % _i] = ("psum", [128, 512], F)
 DSEMS = ["d%d" % i for i in range(48)]
-SEMAPHORES = ["cv", "cs", "cp", "cg", "sent"] + DSEMS + ["az%d" % t for t in range(RO)] + ["an%d" % t for t in range(RO)]
+SEMAPHORES = ["cv", "cs", "cp", "cg", "sent"] + DSEMS + ["az%d" % t for t in range(RO)] + ["an%d" % t for t in range(RO)] + ["ae%d" % t for t in range(RO)]
 
 
 def rank_program(g, core, T, topo):
     rank = T.rank_of(core)
     if rank is None:
         return
-    ops, lastw, readers, nd = [], {}, {}, [0]
+    ops, lastw, readers, nd, own_send = [], {}, {}, [0], {}
+
+    def width(a):
+        n = 1
+        for x in a.shape[1:]: n *= x
+        return n
+
+    def cost(a, per, kind):
+        if kind: return 0.05 + width(a) * (GATHER if kind == "g" else SCATTER) * CYC
+        return 0.03 + max(64, width(a) * per) * CYC
 
     def deps(e, R, Wr):
-        d = set()
+        d, soft = set(), set()
         for k in R:
             if k in lastw: d.add(lastw[k])
             if k[0] == "P": d.update(x for x in readers.get(k, ()) if ops[x]["e"] != e)
         for k in Wr:
             for x in ([lastw[k]] if k in lastw else []) + readers.get(k, []):
-                if e != "p" or ops[x]["e"] != e: d.add(x)
-        return d
+                (d if e != "p" or ops[x]["e"] != e else soft).add(x)
+        return d, soft
 
-    def add(e, fn, R, Wr, tok=None, ext=None):
-        ops.append({"e": e, "fn": fn, "d": deps(e, R, Wr), "tok": tok, "ext": ext})
+    def add(e, fn, R, Wr, c, tok=None, ext=None, lat=0.0):
+        d, soft = deps(e, R, Wr)
+        ops.append({"e": e, "fn": fn, "d": d, "soft": soft, "tok": tok, "ext": ext, "c": c, "lat": lat,
+                    "far": [own_send[x[0]] for x in ext or ()]})
         n = len(ops) - 1
         for k in R: readers.setdefault(k, []).append(n)
         for k in Wr:
             lastw[k] = n; readers[k] = []
         return n
 
-    def dma(e, pairs, R, Wr):
+    def dma(e, pairs, R, Wr, lat=0.8):
         name = DSEMS[nd[0]]; nd[0] += 1
         q = g.sync if e == "y" else g.scalar
         def fn():
             for o, i in pairs: q.dma_start(o, i).then_inc(T.sem[name], 16)
-        return add(e, fn, R, Wr, tok=(name, 16 * len(pairs)))
+        return add(e, fn, R, Wr, 0.06 * len(pairs) + (lat if e == "y" else 0.0), tok=(name, 16 * len(pairs)), lat=2.0)
 
     V, S, P = g.vector, g.scalar, g.tensor
-    def ts(o, i, a, b, o0, o1, R, Wr):
-        add("v", (lambda: V.tensor_scalar(o, i, a, None, o0)) if o1 is None else (lambda: V.tensor_scalar(o, i, a, b, o0, o1)), R, Wr)
-    def tt(o, a, b, op, R, Wr, ext=None): add("v", lambda: V.tensor_tensor(o, a, b, op), R, Wr, ext=ext)
-    def cp(o, i, R, Wr, ext=None): add("v", lambda: V.tensor_copy(o, i), R, Wr, ext=ext)
-    def ms(o, c, Wr): add("v", lambda: V.memset(o, c), [], Wr)
-    def act(o, i, f, R, Wr, bias=0.0, scale=1.0, ext=None): add("s", lambda: S.activation(o, i, f, bias=bias, scale=scale), R, Wr, ext=ext)
+    def ts(o, i, a, b, o0, o1, R, Wr, k=None):
+        add("v", (lambda: V.tensor_scalar(o, i, a, None, o0)) if o1 is None else (lambda: V.tensor_scalar(o, i, a, b, o0, o1)), R, Wr, cost(o, 1, k))
+    def tt(o, a, b, op, R, Wr, k=None):
+        add("v", lambda: V.tensor_tensor(o, a, b, op), R, Wr, cost(b, 1 if any(x[0] == "P" for x in R) else 2, k))
+    def cp(o, i, R, Wr, ext=None, k=None): add("v", lambda: V.tensor_copy(o, i), R, Wr, cost(i, 1, k), ext=ext)
+    def ms(o, c, Wr): add("v", lambda: V.memset(o, c), [], Wr, cost(o, 0.5, None))
+    def act(o, i, f, R, Wr, bias=0.0, scale=1.0, ext=None, k=None):
+        add("s", lambda: S.activation(o, i, f, bias=bias, scale=scale), R, Wr, cost(o, 1, k), ext=ext)
+    def gat(o, i, R, Wr, bias=0.0, scale=1.0, ext=None): act(o, i, AF.Identity, R, Wr, bias, scale, ext, "g")
     def iota(o, pat, base, cm, Wr, isint=False):
-        add("g", (lambda: g.iota(o, pat, base, cm)) if isint else (lambda: g.iota(o, pat, base, cm, allow_small_or_imprecise_dtypes=True)), [], Wr)
+        add("g", (lambda: g.iota(o, pat, base, cm)) if isint else (lambda: g.iota(o, pat, base, cm, allow_small_or_imprecise_dtypes=True)), [], Wr,
+            0.13 + 2 * width(o) * CYC)
     def mm(lst, R, Wr):
         def fn():
             for x in lst: last = P.matmul(*x)
             return last
-        add("p", fn, R, Wr)
+        add("p", fn, R, Wr, sum(max(64, width(x[2])) for x in lst) * CYC / 2)
     def wrap(out, w, src, lo, hi, start, stop):
         return [(out, w(r), src[:, lo + r:hi:16], start and r == 0, stop and r == 15) for r in range(16)]
     def wset(i): return lambda r: T.ww[:, 144 * i + 15 - r:144 * i + 143 - r]
@@ -117,7 +136,7 @@ def rank_program(g, core, T, topo):
     dma("y", [(T.oi[:, 0:240], T.own[0:8, :]), (T.oi[:, 240:480], T.own[8:16, :])], [], ["oi"])
     dma("y", [(T.ei[:, 0:192], T.ends[:, 0:192])], [], ["ei0"])
     dma("y", [(T.zt[:, 256 * j:256 * j + 256], T.st[:, 0:256]) for j in range(4)], [], ["zt0"])
-    dma("y", [(T.mt[:, 0:W], T.msg[:])], [], ["M"])
+    dma("y", [(T.mt[:, 0:W], T.msg[:])], [], ["M"], 3.5)
     iota(T.ip[:, 0:1], [[0, 1]], 0, 1, ["ip"], True)
     iota(T.x240[:], [[1, 256]], 0, 0, ["x240"])
     iota(T.i143[:], [[1, 144]], -15, 0, ["i143"])
@@ -168,6 +187,7 @@ def rank_program(g, core, T, topo):
         ts(T.wm[:, 128 * i:128 * i + 128], T.x240[:, 0:128], pcol, w, ALU.is_equal, ALU.mult, ["x240", "pc"], ["m%d" % i])
     weights(2, mk(0)); weights(3, mk(1)); weights(0, 256.0)
     diag(0, 1.0); diag(1, -1.0)
+    if LIVES > 1: diag(2, float(B))
     ts(T.lanec[:], T.lc0[:], rcol, None, ALU.subtract, None, ["lc0", "pc"], ["lanec"])
     mm([(P5[:, 272:464], ID, T.kc2[:], True, True)], ["m0", "kc2"], ["P5"])
     ts(T.idf[:], T.x240[:, 0:128], pcol, None, ALU.is_equal, None, ["x240", "pc"], ["idf"])
@@ -196,7 +216,7 @@ def rank_program(g, core, T, topo):
         ts(T.wm[:, 512:640], T.b128[:], p16, mk2(1), ALU.is_equal, ALU.mult, ["b128", "pc", "mk2"], ["m4"])
         ts(T.wm[:, 640:768], T.b128[:], p16, mk(6), ALU.is_equal, ALU.mult, ["b128", "pc", "mk"], ["m5"])
         ts(T.wh[:], T.i143[:], p16, None, ALU.is_equal, None, ["i143", "pc"], ["wh"])
-        ts(T.bck[:], T.x240[:, 0:12], 0.0, rcol, ALU.mult, ALU.add, ["x240", "pc"], ["bck"])
+        cp(T.idh[:], ID, ["m0"], ["idh"])
         cp(T.bcc[:, 0:16], T.x240[:, 0:16], ["x240"], ["bcc"])
         cp(T.bcc[:, 16:24], T.bc0[:], ["bc0"], ["bcc1"])
         act(T.vl[:, 0:256], T.x240[:], ident, ["x240", "mk"], ["vl0"], scale=mk(0))
@@ -222,11 +242,13 @@ def rank_program(g, core, T, topo):
         def part(e, lo, hi, key):
             o, i = T.oa[:, 16 * lo:16 * hi], T.ot[:, 0:W].indirect(T.eo[:, 192 * b + lo:192 * b + hi])
             R = ["O", "Oa", "eo%d" % b, "bo"]
-            if e == "s": act(o, i, ident, R, [key], bias=T.cs[:, b:b + 1])
-            else: ts(o, i, T.cs[:, b:b + 1], None, ALU.add, None, R, [key])
+            if e == "s": gat(o, i, R, [key], bias=T.cs[:, b:b + 1])
+            else: ts(o, i, T.cs[:, b:b + 1], None, ALU.add, None, R, [key], "g")
         if ogv: part("v", 192 - ogv, 192, "OA3")
         for j in ((2, 0, 1) if ogv == 64 else (0, 1, 2)):
-            if 64 * j < 192 - ogv: part("s", 64 * j, min(64 * j + 64, 192 - ogv), OAK[j])
+            if 64 * j < 192 - ogv:
+                part("s", 64 * j, min(64 * j + 64, 192 - ogv), OAK[j])
+                if j: ops[-1]["soft"].add(lastw[OAK[j - 1]])
             mm(wrap(P1[:, 64 * j:64 * j + 64], WU0, T.oa, 1024 * j, 1024 * j + 1024, False, False)
                + wrap(P1[:, 192 + 64 * j:256 + 64 * j], WU1, T.oa, 1024 * j, 1024 * j + 1024, False, j == (1 if ogv == 64 else 2)),
                [OAK[j], "w2", "w3"] + (["OA3"] if j == 2 else []), ["P1"])
@@ -234,13 +256,13 @@ def rank_program(g, core, T, topo):
 
     def arrive(t):
         cp(T.mt[:].indirect(T.ln[:, 32 * t:32 * t + 16]), T.lz[:, 256 * t:256 * t + 256], [], ["M"],
-           ext=[("az%d" % t, cnt_in[t]), ("an%d" % t, cnt_in[t])])
+           ext=[("az%d" % t, cnt_in[t]), ("an%d" % t, cnt_in[t])], k="s")
 
     def arrive_em(t):
-        act(T.emr[:], T.ot[:, 0:W].indirect(T.ln[:, 32 * t + 16:32 * t + 32]), ident, ["O", "Oa"], ["emr"], ext=[("an%d" % t, cnt_in[t])])
+        gat(T.emr[:], T.ot[:, 0:W].indirect(T.ln[:, 32 * t + 16:32 * t + 32]), ["O", "Oa"], ["emr"], ext=[(("ae%d" if EMSEND else "an%d") % t, cnt_in[t])])
 
     def arrive_k(t):
-        cp(T.kt[:].indirect(T.ln[:, 32 * t:32 * t + 16]), T.emr[:], ["emr"], ["K"])
+        cp(T.kt[:].indirect(T.ln[:, 32 * t:32 * t + 16]), T.emr[:], ["emr"], ["K"], ext=[("an%d" % t, cnt_in[t])], k="s")
 
     dst = [T.cores[(rank + 1 + t % (NR - 1)) % NR] for t in range(RO)]
     src = [T.cores[(rank - 1 - t % (NR - 1)) % NR] for t in range(RO)]
@@ -250,37 +272,34 @@ def rank_program(g, core, T, topo):
     def send(t, o, i, sem, R):
         rid, pid, _ = topo.addr(dst[t]); m = topo.mask(core, dst[t])
         sent[0] += len(topo.engines(core, dst[t]))
-        add("g", lambda: g.remote_dma(o, i, T.sem[sem], T.sem.sent, pid, rid, m), R, [], tok=("sent", 0))
+        own_send[sem] = add("g", lambda: g.remote_dma(o, i, T.sem[sem], T.sem.sent, pid, rid, m), R, [], 1.0, tok=("sent", 0))
 
     nf, cm, colf, tc, hp, new, fa, jj, nhd, clb, tab, fav, f0, pu1, t1, nhs = [sm(i) for i in range(16)]
     nfb, fb, hasp, nhp, k0p, sn_, ra, rb = [sm(16 + i) for i in range(8)]
 
     def list_mask():
-        act(T.la[:], P4[:, 0:192], absf, ["P4"], ["la"])
-        act(P4[:, 192:384], T.la[:], relu, ["la"], ["P4"], bias=1.0, scale=-1.0)
+        act(T.la[:], P4[:, 0:192], absf, ["P4"], ["la"], scale=8192.0)
 
     def hints(t):
-        cp(su(2), colf, ["colf"], ["colu"])
-        ts(fb, nfb, -1.0, 32768.0, ALU.mult, ALU.add, ["nfb"], ["fb"])
-        tt(T.hs[:], T.ec[:].indirect(su(2)), T.mm[:], ALU.mult, EK + ["colu", "mm"], ["hs"])
-        tt(k0p, k0p, jj, ALU.min, ["k0p", "jj"], ["k0p"])
-        tt(sm(22, 2), sm(20, 2), sm(16, 2), ALU.add, ["k0p", "sn_", "nfb", "fb"], ["rab"])
-        tt(T.rowb[:], ra, rb, ALU.min, ["rab"], ["rowb"])
+        tt(T.hs[:], T.ec[:].indirect(su(2)), T.mm[:], ALU.mult, EK + ["colu", "mm"], ["hs"], "g")
 
     def hints_p():
         mm([(P4[:, 0:192], ID, T.kcn[:], True, False)]
            + [(P4[:, 16 * k:16 * k + 16], ID, T.rowb[:], False, k == 11) for k in range(12)], ["rowb", "m0", "kcn"], ["P4"])
-        mm(wrap(P7[:, 0:16], WH, T.hs, 0, 256, True, True), ["hs", "wh"], ["P7"])
+        mm([(P7[:, 0:16], ID, T.fbb[:], True, False)] + wrap(P7[:, 0:16], WH, T.hs, 0, 256, False, True), ["hs", "wh", "fbb", "m0"], ["P7"])
 
     def hints_b():
-        tt(hp, P7[:, 0:16], fb, ALU.add, ["P7", "fb"], ["hp"])
-        tt(new, hp, cm, ALU.min, ["hp", "cm"], ["new"])
+        tt(T.newh[:], P7[:, 0:16], cm, ALU.min, ["P7", "cm"], ["new"])
+
+    def list_bounds():
+        for o, w in ((0, ID), (192, NID)):
+            mm([(P4[:, o:o + 192], w, T.la[:], True, False)]
+               + [(P4[:, o + 16 * k:o + 16 * k + 16], T.idh[:], T.newh[:], False, k == 11) for k in range(12)], ["la", "new", "m0", "m1", "idh"], ["P4"])
 
     def list_update(t):
         b = t % 4; eb = T.ec[:, 192 * b:192 * b + 192]
-        yield tt(T.ld[:], new.indirect(T.bck[:]), eb, ALU.subtract, ["new", "bck", EK[b]], ["ld"])
-        yield tt(P4[:, 0:192], T.ld[:], P4[:, 192:384], ALU.mult, ["P4", "ld"], ["P4"])
-        yield tt(eb, eb, P4[:, 0:192], ALU.add, [EK[b], "P4"], [EK[b]])
+        yield tt(T.ld[:], eb, P4[:, 0:192], ALU.min, ["P4", EK[b]], ["ld"])
+        yield tt(eb, T.ld[:], P4[:, 192:384], ALU.max, ["ld", "P4"], [EK[b]])
         if t < 4:
             yield ts(T.eo[:, 192 * b:192 * b + 192], eb, 2048.0, None, ALU.add, None, [EK[b]], ["eo%d" % b])
 
@@ -293,8 +312,16 @@ def rank_program(g, core, T, topo):
         act(T.u0[:], P1[:, 0:192], ident, ["P1"], ["u0"])
         tt(T.uu[:], T.u0[:], P1[:, 192:384], ALU.mult, ["u0", "P1"], ["uu"])
         ts(T.d0[:], T.uu[:], 0.0, float(B), ALU.not_equal, ALU.mult, ["uu"], ["d0"])
-        ts(T.d1[:], T.uu[:], 0.0, float(B), ALU.is_equal, ALU.mult, ["uu"], ["d1"])
-        tt(T.d2[:], T.d0[:], P5[:, 272:464], ALU.add, ["d0", "P5"], ["d2"])
+        if LIVES:
+            act(T.sc[:], T.d0[:], ident, ["d0"], ["stale"], scale=1.0 / B)
+            act(T.d1[:], T.d0[:], ident, ["d0"], ["d1"], scale=-1.0, bias=float(B))
+        else:
+            ts(T.d1[:], T.uu[:], 0.0, float(B), ALU.is_equal, ALU.mult, ["uu"], ["d1"])
+        if LIVES > 1:
+            mm([(P2[:, 0:192], ID, T.kc2[:], True, False), (P2[:, 0:192], BID, T.sc[:], False, True)], ["stale", "kc2", "m0", "m2"], ["P2"])
+            act(T.d2[:], P2[:, 0:192], ident, ["P2"], ["d2"])
+        else:
+            tt(T.d2[:], T.d0[:], P5[:, 272:464], ALU.add, ["d0", "P5"], ["d2"])
 
     for t in range(RO):
         b = t % 4; lo = 256 * b
@@ -302,66 +329,81 @@ def rank_program(g, core, T, topo):
         zc = T.wx[:, zb:zb + 256]
         if t:
             arrive(t - 1)
-        mm([(P0[:, 0:192], NID, T.kcn[:], True, False)], ["m1", "kcn"], ["P0"])
+        mm([(P0[:, 0:128], NID, T.kcn[:, 0:128], True, False)], ["m1", "kcn"], ["P0"])
+        mm([(P3[:, 128:192], NID, T.kcn[:, 128:192], True, False)], ["m1", "kcn"], ["P3"])
         for a, e in CH:
             tt(T.xx[:, 256 * a:256 * e], T.mt[:, 0:W].indirect(T.eo[:, 192 * b + 16 * a:192 * b + 16 * e]),
-               T.zt[:, 1024 * b:1024 * b + 256 * (e - a)], ALU.subtract, ["M", "eo%d" % b, "zt%d" % b], XK[a:e])
+               T.zt[:, 1024 * b:1024 * b + 256 * (e - a)], ALU.subtract, ["M", "eo%d" % b, "zt%d" % b], XK[a:e], "g")
+            if a: ops[-1]["soft"].add(len(ops) - 2)
+        if t > 1:
+            for _ in list_update(t - 2): pass
+            if t > 5: list_out(t - 2)
         if t: hints(t - 1)
         for a, e in CH:
             act(T.wx[:, 256 * a:256 * e], T.xx[:, 256 * a:256 * e], absf, XK[a:e], AK[a:e])
+            if a: ops[-1]["soft"].add(lastw[AK[a - 1]])
+            elif t: ops[-1]["soft"].add(lastw["OA2"])
             if a == 0 and t: live()
             if e % 4 == 0:
                 j = e // 4 - 1
-                mm(wrap(P0[:, 64 * j:64 * j + 64], WD, T.wx, 1024 * j, 1024 * j + 1024, False, j == 2), AK[4 * j:4 * j + 4] + ["w0"], ["P0"])
+                mm(wrap((P0, P0, P3)[j][:, 64 * j:64 * j + 64], WD, T.wx, 1024 * j, 1024 * j + 1024, False, j > 0),
+                   AK[4 * j:4 * j + 4] + ["w0"], [("P0", "P0", "P3")[j]])
         if t:
             hints_p(); arrive_em(t - 1)
         else:
             cp(T.tf[0:64, :], T.ti[0:64, :], ["ti"], ["tf"])
-            add("p", lambda: P.transpose(P7[:, 0:64], T.tf[0:64, :], T.idf[0:64, 0:64]), ["tf", "idf"], ["P7"])
+            add("p", lambda: P.transpose(P7[:, 0:64], T.tf[0:64, :], T.idf[0:64, 0:64]), ["tf", "idf"], ["P7"], 0.3)
             owners(0, OGV0); late_constants(); live()
-        act(T.sc[:], T.d0[:], ident, ["d0"], ["stale"], scale=1.0 / B)
+        if not LIVES: act(T.sc[:], T.d0[:], ident, ["d0"], ["stale"], scale=1.0 / B)
         mm([(P6[:, 16 * s:192], ID, T.sc[:, 0:192 - 16 * s], s == 0, s == 11) for s in range(12)], ["stale", "m0"], ["P6"])
         if t: list_mask()
         act(T.lead[:], P6[:, 0:192], relu, ["P6"], ["lead"], bias=1.0, scale=-1.0)
         mm([(P6[:, 192:208], NID, T.kcn[:, 0:16], True, False)]
            + [(P6[:, 192:208], I16, T.lead[:, 16 * k:16 * k + 16], False, k == 11) for k in range(12)], ["lead", "m1", "m6", "kcn"], ["P6"])
-        tt(T.kb[:, 0, :], P0[:, 0:192], T.d0[:], ALU.add, ["P0", "d0"], ["kb0"])
-        tt(T.kb[:, 1, :], P0[:, 0:192], T.d1[:], ALU.add, ["P0", "d1"], ["kb1"])
-        tt(T.kb[:, 2, :], T.d2[:], P0[:, 0:192], ALU.subtract, ["P0", "d2"], ["kb2"])
-        tt(T.t1[:], T.kb[:, :, 0:96], T.kb[:, :, 96:192], ALU.min, ["kb0", "kb1", "kb2"], ["t1"])
-        tt(T.t2[:], T.t1[:, :, 0:48], T.t1[:, :, 48:96], ALU.min, ["t1"], ["t2"])
+        mm([(P6[:, 208:224], ID, T.ch[:], True, False)]
+           + [(P6[:, 208:224], I16, T.lead[:, 176:192], False, k == t) for k in range(t + 1)], ["lead", "m0", "m6", "ch"], ["P6"])
+        for pb, pk, a, e in ((P0, "P0", 0, 128), (P3, "P3", 128, 192)):
+            tt(T.kb[:, 0, a:e], pb[:, a:e], T.d0[:, a:e], ALU.add, [pk, "d0"], ["kb0" + pk])
+            tt(T.kb[:, 1, a:e], pb[:, a:e], T.d1[:, a:e], ALU.add, [pk, "d1"], ["kb1" + pk])
+            tt(T.kb[:, 2, a:e], T.d2[:, a:e], pb[:, a:e], ALU.subtract, [pk, "d2"], ["kb2" + pk])
+        tt(T.t1[:, :, 0:64], T.kb[:, :, 0:64], T.kb[:, :, 64:128], ALU.min, ["kb0P0", "kb1P0", "kb2P0"], ["t1"])
+        tt(T.t2[:, :, 0:32], T.t1[:, :, 0:32], T.t1[:, :, 32:64], ALU.min, ["t1"], ["t2"])
         tt(T.t3[:], T.t2[:, :, 0:16], T.t2[:, :, 16:32], ALU.min, ["t2"], ["t3"])
-        tt(T.rr[:], T.t3[:], T.t2[:, :, 32:48], ALU.min, ["t2", "t3"], ["rr"])
+        tt(T.t1[:, :, 64:96], T.kb[:, :, 128:160], T.kb[:, :, 160:192], ALU.min, ["kb0P3", "kb1P3", "kb2P3"], ["t1b"])
+        tt(T.t2[:, :, 32:48], T.t1[:, :, 64:80], T.t1[:, :, 80:96], ALU.min, ["t1b"], ["t2b"])
+        tt(T.rr[:], T.t3[:], T.t2[:, :, 32:48], ALU.min, ["t2b", "t3"], ["rr"])
         ts(T.rk[:], T.rr[:], 255, None, ALU.bitwise_and, None, ["rr"], ["rk"])
         ts(T.off[:], T.rk[:], 16.0, rcol, ALU.mult, ALU.add, ["rk", "pc"], ["off"])
         R0, K0, K1 = T.rr[:, 0, :], T.rk[:, 0, :], T.rk[:, 1, :]
         of, os_, om = T.off[:, 0:16], T.off[:, 16:32], T.off[:, 32:48]
         thb = T.thb[:, 16 * b:16 * b + 16]; tk = "th%d" % b
-        lu = list_update(t - 1) if t else iter(())
         mm([(P2[:, 0:384], ID, T.cwc[:, 16:400], True, False)], ["m0", "cwc", "cwc1"], ["P2"])
         mm([(P1[:, 0:16], ID, T.cwc[:, 0:16], True, False)], ["m0", "cwc0"], ["P1"])
-        act(T.nf_[:, 0:256], T.oa[:].indirect(of), ident, OAK + ["off"], ["nbf"])
-        act(T.nf_[:, 256:512], T.oa[:].indirect(om), ident, OAK + ["off"], ["nbm"])
+        gat(T.nf_[:, 0:256], T.oa[:].indirect(of), OAK + ["off"], ["nbf"])
+        gat(T.nf_[:, 256:512], T.oa[:].indirect(om), OAK + ["off"], ["nbm"])
         mm([(P0[:, 0:16], I16R, T.lanec[:, 0:16], True, False)] + wrap(P0[:, 0:16], WP, T.nf_, 0, 256, False, True),
            ["nbf", "w6", "m7", "lanec"], ["P0"])
-        mm(wrap(P3[:, 0:32], WN, T.nf_, 0, 512, True, True), ["nbf", "nbm", "w4"], ["P3"])
+        if EMSPLIT: mm(wrap(P3[:, 0:16], WN, T.nf_, 0, 256, True, True), ["nbf", "w4"], ["P3"])
+        else: mm(wrap(P3[:, 0:32], WN, T.nf_, 0, 512, True, True), ["nbf", "nbm", "w4"], ["P3"])
         mm([(P5[:, 16:272], RN, T.nf_[:, 0:256], True, True)], ["nbf", "m4"], ["P5"])
-        act(T.sz[:, 256 * t:256 * t + 256], T.wx[:, 0:3072].indirect(of), ident, AK + ["off"], ["sz%d" % t])
+        gat(T.sz[:, 256 * t:256 * t + 256], T.wx[:, 0:3072].indirect(of), AK + ["off"], ["sz%d" % t])
         send(t, T.lz[:, 256 * t:256 * t + 256], T.sz[:, 256 * t:256 * t + 256], "az%d" % t, ["sz%d" % t])
         act(nhp, P6[:, 192:208], relu, ["P6"], ["nhp"], bias=-256.0 * 191, scale=256.0)
         act(jj, P6[:, 192:208], ident, ["P6"], ["jj"])
-        act(nhs, nhp, sign, ["nhp"], ["nhs"])
         act(hasp, P6[:, 192:208], relu, ["P6"], ["hasp"], bias=256.0 * 192, scale=-256.0)
-        act(nhd, nhs, ident, ["nhs"], ["nhd"], scale=float((zb - HCOL) // 16))
         tt(nf, R0, thb, ALU.is_ge, ["rr", tk], ["nf"])
+        tt(fa, P6[:, 208:224], nf, ALU.mult, ["P6", "nf"], ["fa"])
         if t: arrive_k(t - 1)
         else:
             cp(T.eo[:, 192:768], T.ei[:, 192:768], ["ei1"], ["eo1", "eo2", "eo3"])
             ts(T.ec[:], T.ei[:], -2048.0, None, ALU.add, None, ["ei0", "ei1"], EK)
-        ts(nfb, nf, 32768.0, None, ALU.mult, None, ["nf"], ["nfb"])
+        act(nfb, nf, ident, ["nf"], ["nfb"], scale=32768.0)
+        act(fb, nf, ident, ["nf"], ["fb"], scale=-32768.0, bias=32768.0)
+        act(T.fbb[:], nf, ident, ["nf"], ["fbb"], scale=-32768.0, bias=32768.0)
         cp(su(0), P3[:, 0:16], ["P3"], ["efu"])
-        act(T.kg[:], T.kt[:, 0:W].indirect(su(0)), ident, ["K", "efu"], ["kg"])
+        gat(T.kg[:], T.kt[:, 0:W].indirect(su(0)), ["K", "efu"], ["kg"])
         tt(f0, P3[:, 0:16], nfb, ALU.add, ["P3", "nfb"], ["f0"])
+        if EMSPLIT: mm(wrap(P3[:, 16:32], WN, T.nf_, 256, 512, True, True), ["nbm", "w4"], ["P3"])
         cp(T.sn[:, 32 * t + 16:32 * t + 32], P3[:, 16:32], ["P3"], ["sm%d" % t])
         if t: hints_b()
         mm([(P2[:, 0:256], RN, T.kg[:], False, False)]
@@ -375,27 +417,29 @@ def rank_program(g, core, T, topo):
         ts(su(4), pu1, -MAGIC, 15.0, ALU.add, ALU.min, ["pu1"], ["pu"])
         tt(fav, f0, clb, ALU.add, ["f0", "clb"], ["fav"])
         tt(thb, thb, nfb, ALU.add, [tk, "nfb"], [tk])
-        tt(T.eq2[:], fav.indirect(su(4)), T.erow[:], ALU.is_equal, ["fav", "pu", "erow"], ["eq2"])
+        tt(T.eq2[:], fav.indirect(su(4)), T.erow[:], ALU.is_equal, ["fav", "pu", "erow"], ["eq2"], "g")
         mm(wrap(P0[:, 16:32], WBIG, T.eq2, 0, 256, True, True), ["eq2", "w1"], ["P0"])
         tt(cm, P1[:, 0:16], nfb, ALU.add, ["P1", "nfb"], ["cm"])
         ts(su(1), P1[:, 0:16], 2048.0, None, ALU.add, None, ["P1"], ["cu"])
-        tt(T.eq[:], cm.indirect(T.bcc[:]), T.crow[:], ALU.is_equal, ["cm", "bcc", "bcc1", "crow"], ["eq"])
+        tt(T.eq[:], cm.indirect(T.bcc[:]), T.crow[:], ALU.is_equal, ["cm", "bcc", "bcc1", "crow"], ["eq"], "g")
         mm(wrap(P1[:, 32:56], WBIG, T.eq, 0, 384, True, True), ["eq", "w1"], ["P1"])
         tt(t1, P0[:, 16:32], clb, ALU.min, ["P0", "clb"], ["t1_"])
-        tt(fa, nhd, T.ch[:], ALU.add, ["nhd", "ch"], ["fa"])
         tt(t1, t1, f0, ALU.add, ["t1_", "f0"], ["t1_"])
-        tt(fa, fa, nf, ALU.mult, ["fa", "nf"], ["fa"])
         tt(T.so[:, 0:16], t1, T.dm[:], ALU.min, ["t1_", "dm"], ["soa"])
         tt(fa, fa, K0, ALU.max, ["fa", "rk"], ["fa"])
         cp(T.sn[:, 32 * t:32 * t + 16], T.so[:, 0:16], ["soa"], ["sn%d" % t])
-        send(t, T.ln[:, 32 * t:32 * t + 32], T.sn[:, 32 * t:32 * t + 32], "an%d" % t, ["sn%d" % t, "sm%d" % t])
+        if EMSEND:
+            send(t, T.ln[:, 32 * t:32 * t + 16], T.sn[:, 32 * t:32 * t + 16], "an%d" % t, ["sn%d" % t])
+            send(t, T.ln[:, 32 * t + 16:32 * t + 32], T.sn[:, 32 * t + 16:32 * t + 32], "ae%d" % t, ["sm%d" % t])
+        else:
+            send(t, T.ln[:, 32 * t:32 * t + 32], T.sn[:, 32 * t:32 * t + 32], "an%d" % t, ["sn%d" % t, "sm%d" % t])
         if t == 0: later_constants()
-        act(T.keepv[:], T.ot[:, 0:W].indirect(su(1)), ident, ["O", "Oa", "cu", "keep%d" % (4 + b % 2), "keep%d" % (6 + b)], ["keepv"],
+        gat(T.keepv[:], T.ot[:, 0:W].indirect(su(1)), ["O", "Oa", "cu", "keep%d" % (4 + b % 2), "keep%d" % (6 + b)], ["keepv"],
             bias=T.cs[:, 6 + b:7 + b], scale=T.cs[:, 4 + b % 2:5 + b % 2])
-        act(T.sb[:], T.oa[:].indirect(os_), ident, OAK + ["off"], ["sb"])
+        gat(T.sb[:], T.oa[:].indirect(os_), OAK + ["off"], ["sb"])
         mm([(P7[:, 0:272], ID, T.hc[:], True, False), (P7[:, 16:272], R3, T.sb[:], False, False)]
            + wrap(P7[:, 0:16], WC, T.sb, 0, 256, False, True), ["sb", "w5", "m0", "m5", "hc", "hc0"], ["P7"])
-        act(T.xs[:], T.xx[:].indirect(os_), ident, XK + ["off"], ["xs"])
+        gat(T.xs[:], T.xx[:].indirect(os_), XK + ["off"], ["xs"])
         mm([(P6[:, 0:256], ID, T.qc[:], True, False), (P6[:, 0:256], ID, zc, False, False), (P6[:, 0:256], HID, T.xs[:], False, True)],
            ["xs", zk, "qc", "m0", "m3"], ["P6"])
         tt(tc, P1[:, 32:48], cm, ALU.add, ["P1", "cm"], ["tc"])
@@ -409,44 +453,66 @@ def rank_program(g, core, T, topo):
         act(T.wx[:, HCOL:HCOL + 256], T.ht[:], ident, ["ht"], ["H"], bias=-MAGIC)
         fill = [
             lambda: ts(su(3), fa, 16.0, rcol, ALU.mult, ALU.add, ["fa", "pc"], ["fo"]),
-            lambda: next(lu, None), lambda: next(lu, None), lambda: next(lu, None), lambda: next(lu, None),
-            lambda: tt(colf, P7[:, 0:16], K1, ALU.add, ["P7", "rk"], ["colf"]),
             lambda: tt(sm(20, 2), T.rk[:, 0:2, :], sm(18, 2), ALU.add, ["rk", "hasp", "nhp"], ["k0p", "sn_"]),
+            lambda: tt(k0p, k0p, jj, ALU.min, ["k0p", "jj"], ["k0p"]),
+            lambda: tt(sm(22, 2), sm(20, 2), sm(16, 2), ALU.add, ["k0p", "sn_", "nfb", "fb"], ["rab"]),
+            lambda: tt(T.rowb[:], ra, rb, ALU.min, ["rab"], ["rowb"]),
+            lambda: tt(colf, P7[:, 0:16], K1, ALU.add, ["P7", "rk"], ["colf"]),
+            lambda: cp(su(2), colf, ["colf"], ["colu"]),
         ]
+        if t: list_bounds()
         vb = 256 * (b % 2)
         for m in range(7, -1, -1):
             tt(T.ot[:].indirect(T.oc[:, 2 * m:2 * m + 2]), T.keepv[:, 32 * m:32 * m + 32], T.vl[:, vb + 32 * m:vb + 32 * m + 32], ALU.add,
-               ["oce", "oco", "keepv", "vl0", "vl1"], ["O", "Oa"])
+               ["oce", "oco", "keepv", "vl0", "vl1"], ["O", "Oa"], "s")
             if fill: fill.pop(0)()
-            if t == RO - 1 and m == LASTM:
-                arrive(t)
-                dma("y", [(T.ym[:], T.mt[:, 0:W])], ["M"], [])
+        if t == RO - 1:
+            arrive(t)
+            dma("y", [(T.ym[:], T.mt[:, 0:W])], ["M"], [], 3.5)
         if t < 4:
-            act(T.wx[:, Z1 + lo:Z1 + lo + 256], T.wx[:, 0:Z1].indirect(su(3)), ident, AK + ["H", "fo", "Z0"], ["Z1_%d" % b])
+            gat(T.wx[:, Z1 + lo:Z1 + lo + 256], T.wx[:, 0:Z1].indirect(su(3)), AK + ["H", "fo", "Z0"], ["Z1_%d" % b])
             dma("y", [(T.zt[:, 1024 * b + 256 * j:1024 * b + 256 * j + 256], T.wx[:, Z1 + lo:Z1 + lo + 256]) for j in range(4)],
                 ["Z1_%d" % b], ["zt%d" % b])
         else:
-            act(T.zo[:, lo:lo + 256], T.wx[:].indirect(su(3)), ident, AK + ["H", "fo", zk], ["zo%d" % b])
+            gat(T.zo[:, lo:lo + 256], T.wx[:].indirect(su(3)), AK + ["H", "fo", zk], ["zo%d" % b])
             dma("y", [(T.yz[:, lo:lo + 256], T.zo[:, lo:lo + 256])], ["zo%d" % b], [])
-        if t > 4: list_out(t - 1)
         if t == RO - 2: dma("y", [(T.yo[0:8, :], T.ot[0::16, 0:W])], ["O", "Oa"], [])
         if t == RO - 1: dma("y", [(T.yo[8:16, :], T.ot[1::16, 0:W])], ["O", "Oa"], [])
         if t == RO - 1:
             act(T.tho[:], T.thb[:], ident, ["th0", "th1", "th2", "th3"], ["tho"], scale=1.0 / 256)
-            add("p", lambda: P.transpose(P3[0:64, 0:128], T.tho[:], T.idf[:]), ["tho", "idf"], ["P3"])
+            add("p", lambda: P.transpose(P3[0:64, 0:128], T.tho[:], T.idf[:]), ["tho", "idf"], ["P3"], 0.3)
             arrive_em(t)
             act(T.tf[0:64, :], P3[0:64, 0:128], ident, ["P3"], ["tf"])
             dma("s", [(T.yt[q, :], T.tf[0:64, 16 * q:16 * q + 16]) for q in range(8)], ["tf"], [])
+            for _ in list_update(t - 1): pass
+            list_out(t - 1)
             hints(t); hints_p()
             arrive_k(t)
             dma("y", [(T.yk[:], T.kt[2::16, 0:W])], ["K"], [])
         if t + 1 < RO: owners(t + 1, OGV)
-    list_mask(); hints_b()
+    list_mask(); hints_b(); list_bounds()
     for _ in list_update(RO - 1): pass
     list_out(RO - 1)
 
     queue = {"v": V, "s": S, "p": P, "g": g, "y": g.sync}
     csem = {"v": "cv", "s": "cs", "p": "cp", "g": "cg"}
+    succ = [[] for _ in ops]
+    for n, o in enumerate(ops):
+        o["all"] = [(x, ops[x]["lat"] + WAKE) for x in o["d"]] + [(x, 0.0) for x in o["soft"]] + [(x, REM) for x in o["far"]]
+        for x, l in o["all"]: succ[x].append((n, l))
+    tail = [0.0] * len(ops)
+    for n in range(len(ops) - 1, -1, -1):
+        tail[n] = ops[n]["c"] + max([l + tail[y] for y, l in succ[n]] + [ops[n]["lat"]])
+    busy = {e: [] for e in queue}; begin = [0.0] * len(ops)
+    for n in sorted(range(len(ops)), key=lambda x: (-tail[x], x)):
+        o = ops[n]; t0 = max([begin[x] + ops[x]["c"] + l for x, l in o["all"]] + [0.0]); row = busy[o["e"]]; i = 0
+        while i < len(row) and row[i][0] < t0 + o["c"] - SLACK:
+            t0 = max(t0, row[i][1]); i += 1
+        row.insert(i, (t0, t0 + o["c"])); begin[n] = t0
+    order = sorted(range(len(ops)), key=lambda x: (begin[x], x))
+    pos = {n: i for i, n in enumerate(order)}
+    ops = [ops[n] for n in order]
+    for o in ops: o["d"] = [pos[x] for x in o["d"]]
     needed = set()
     for o in ops:
         best = {}

@@ -1,65 +1,57 @@
-from concourse.mybir import dt, AluOpType as ALU, ActivationFunctionType as AF
-from concourse.bass import DstId, RemoteDMATransfer
+from concourse.mybir import AluOpType as ALU, ActivationFunctionType as AF
 
-W, PB, RO, NR = 3840, 256, 8, 8
+W, RO, NR = 3840, 8, 8
 B = 1 << 21
+BIG = 32768.0
 MAGIC = 12582912.0
-HDT = "float16"
-CYC, GATHER, SCATTER, WAKE, REM, SLACK = 0.95e-3, 1.56, 3.8, 0.1, 3.0, 0.03
-EMSPLIT = True
-EMSEND = False
-LIVES = 1
-OGV0 = 64
-OGV = 0
-CH = ((0, 4), (4, 8), (8, 10), (10, 11), (11, 12))
-
-F, BF, I, U = "float32", "bfloat16", "int32", "uint16"
-SCRATCH = {
-    "mt": ("sbuf", [128, 4096], BF), "ot": ("sbuf", [128, 3872], F), "kt": ("sbuf", [128, 4096], F),
-    "xx": ("sbuf", [128, 3072], BF), "wx": ("sbuf", [128, 5376], BF), "oa": ("sbuf", [128, 3072], BF),
-    "zt": ("sbuf", [128, 4096], BF),
-    "zo": ("sbuf", [128, 1024], BF), "ec": ("sbuf", [128, 768], F), "eo": ("sbuf", [128, 768], U),
-    "ei": ("sbuf", [128, 768], I), "eout": ("sbuf", [128, 768], F),
-    "oi": ("sbuf", [128, 720], I), "stg": ("sbuf", [128, 2160], F), "sti": ("sbuf", [128, 720], I), "hb": ("sbuf", [128, 480], BF),
-    "ti": ("sbuf", [128, 128], I), "tf": ("sbuf", [128, 128], F), "thb": ("sbuf", [128, 64], F), "tho": ("sbuf", [128, 64], F),
-    "ip": ("sbuf", [128, 4], I), "pc": ("sbuf", [128, 16], F), "cs": ("sbuf", [128, 16], F),
-    "mk": ("sbuf", [128, 16], F), "mk2": ("sbuf", [128, 4], F),
-    "i143": ("sbuf", [128, 144], F), "b128": ("sbuf", [128, 128], F), "x240": ("sbuf", [128, 256], F),
-    "h256": ("sbuf", [128, 256], F), "r256": ("sbuf", [128, 256], F), "lc0": ("sbuf", [128, 384], F), "bo0": ("sbuf", [128, 4], F),
-    "d20": ("sbuf", [128, 16], F), "bc0": ("sbuf", [128, 8], F),
-    "ww": ("sbuf", [128, 7 * 144], BF), "wh": ("sbuf", [128, 144], HDT), "wm": ("sbuf", [128, 8 * 128], BF), "idf": ("sbuf", [128, 128], F),
-    "lanec": ("sbuf", [128, 384], BF), "kc2": ("sbuf", [128, 192], BF), "kcn": ("sbuf", [128, 192], BF),
-    "cwc": ("sbuf", [128, 400], BF), "hc": ("sbuf", [128, 272], BF), "qc": ("sbuf", [128, 256], BF),
-    "dm": ("sbuf", [128, 16], F), "ch": ("sbuf", [128, 16], BF), "bck": ("sbuf", [128, 12], U), "bcc": ("sbuf", [128, 24], U),
-    "vl": ("sbuf", [128, 512], F), "vt": ("sbuf", [128, 512], F),
-    "u0": ("sbuf", [128, 192], F), "uu": ("sbuf", [128, 192], F), "sc": ("sbuf", [128, 192], BF), "d0": ("sbuf", [128, 192], F),
-    "vq": ("sbuf", [128, 16], F),
-    "d1": ("sbuf", [128, 192], F), "d2": ("sbuf", [128, 192], F), "lead": ("sbuf", [128, 192], BF), "la": ("sbuf", [128, 192], BF),
-    "kb": ("sbuf", [128, 3, 192], F), "t1": ("sbuf", [128, 3, 96], F), "t2": ("sbuf", [128, 3, 48], F), "t3": ("sbuf", [128, 3, 16], F),
-    "rr": ("sbuf", [128, 3, 16], I), "rk": ("sbuf", [128, 3, 16], I), "off": ("sbuf", [128, 48], U),
-    "nf_": ("sbuf", [128, 512], BF),
-    "sb": ("sbuf", [128, 256], BF), "kg": ("sbuf", [128, 256], BF), "xs": ("sbuf", [128, 256], BF),
-    "crow": ("sbuf", [128, 384], F), "erow": ("sbuf", [128, 256], F), "keepv": ("sbuf", [128, 256], F),
-    "ma": ("sbuf", [128, 256], BF), "mm": ("sbuf", [128, 256], BF),
-    "ht": ("sbuf", [128, 256], F), "eq": ("sbuf", [128, 384], BF), "eq2": ("sbuf", [128, 256], BF),
-    "hs": ("sbuf", [128, 256], HDT), "emr": ("sbuf", [128, 256], F),
-    "sm": ("sbuf", [128, 28 * 16], F), "si": ("sbuf", [128, 16], I), "su": ("sbuf", [128, 5 * 16], U), "oc": ("sbuf", [128, 16], U),
-    "fbb": ("sbuf", [128, 16], BF), "newh": ("sbuf", [128, 16], HDT), "idh": ("sbuf", [128, 128], HDT),
-    "rowb": ("sbuf", [128, 16], BF), "so": ("sbuf", [128, 32], F), "ld": ("sbuf", [128, 192], F),
-    "sz": ("sbuf", [128, RO * 256], BF), "sn": ("sbuf", [128, RO * 32], U),
-    "lz": ("sbuf", [128, RO * 256], BF), "ln": ("sbuf", [128, RO * 32], U),
+CYC, FIX, GATHER, SCATTER, WAKE, REM, SLACK, DMAF = 0.85e-3, 0.01, 1.3, 3.0, 0.21, 2.3, 0.03, 0.45
+CH = ((0, 4), (4, 8), (8, 10), (10, 12))
+BC = ((0, 2), (2, 4), (4, 8), (8, 12))
+FILLG = 3
+AFFV = ("pq", "ph0", "ph1")
+CHAIN = {
+    "v": "X0<M X4<M ee<P1 X8<M X10<M d2<d0 ka0<P0 ka1<P0 ka2<P0 hs<E t0a<ka0 kb2<P3 kb1<P3 kb0<P3 t1a<t0a t0b<kb0 t3a<t1a t3b<t0b eo<E "
+         "rr<t3a rk<rr nf<rr off<rk Kf0<emr new<P7 efu<P3 efo<P3 f1<P3 rkb<rk clb<P0 pu1<P0 fav<f1 pu<pu1 eq2<fav cm<P1 sm<P1 eq<cm "
+         "so<P0 sn<so tc<P2 fa<P6 tco<P2 oce<tc oco<tco ra<P6 O<oce#1 fo<fa O<oce#1 colu<P7 rowb<ra O<oce#2 ld<P4+#1 O<oce#1 E<ld+#1 "
+         "O<oce OA0<O M<+",
+    "s": "A0<X0 A4<X4 d0<P5 A8<X8 A10<X10 emr<nt0 la<P4 lead<P6 nbf<OA0 sz<X0 nbm<OA0 kg<Kf0 erow<P5 kg2<Kf0 xs<X0 tq<P6 "
+         "sb<OA0 keepv<O H<P6 Z1_<X0 zo<X0 mm<P7 OA2<O OA4<O OA8<O",
+    "p": "P0<A0 P5<ee P0<A4 P3<A8 P6<d0 P0<m0#1 P2<m0 P6<lead P7<hs P3<nbf P0<nbf P5<nbf P1<kg P0<m0 P6<nf P0<eq2 P2<eq P5<thh+ "
+         "P1<m0 P7<sb P4<la#1 P6<xs P4<la P0<m1+ P3<m1+ P4<rowb+ P1<OA0 P1<OA2 P1<OA4 P1<OA8",
+    "y": "oi< ei0< zq< M< ki< Oa<s0 Or<s5 Kf1<s2 ti< Z0< ei1< Kf0<Kf1 O<s6",
+    "g": "ip< x240< i143< lh0< bo0< kcn< Of12<",
 }
+
+F, BF, HF, I, U = "float32", "bfloat16", "float16", "int32", "uint16"
+SCRATCH = {name: ("sbuf", [128] + list(cols), kind) for kind, bufs in (
+    (F, dict(ot=[3872], kt=[4096], nt=[W], ec=[768], eout=[768], stg=[2400], tf=[128], pc=[16], cs=[16], pw=[64], mk=[16], mk2=[8],
+             i143=[144], b128=[128], x240=[256], h256=[256], r256=[256], lc0=[16], lh0=[384], bo0=[4], d20=[16], bc0=[8], idf=[128],
+             dm=[16], vl=[512], vt=[256], vq=[16], d2=[192], kb=[3, 192], t1=[3, 96], t2=[3, 32], t3=[3, 32],
+             erow=[256], keepv=[256], emr=[256], sm=[256], ld=[192])),
+    (BF, dict(mt=[4096], xx=[5376], wx=[3072], oa=[3072], zt=[4096], zo=[1024], hb=[240], thh=[128], nfs=[128], rkb=[32], clb=[16],
+              tk=[112], tk0=[128], ww=[8 * 144], wm=[15 * 128], lanec=[16], lanh=[384], kc2=[192], kcn=[192],
+              ee=[384], d0=[192], lead=[192], la=[192], nf_=[256], sb=[256], mm=[256], r3=[256], eq=[384], eq2=[256], rowb=[16],
+              sz=[RO * 256], lz=[RO * 256])),
+    (HF, dict(wh=[288], idh=[128], kq=[640], xs=[256], hs=[256], newh=[16])),
+    (I, dict(ei=[768], oi=[720], sti=[720], ti=[128], ip=[8], rr=[3, 16], rk=[3, 16])),
+    (U, dict(eo=[768], bcc=[24], off=[48], su=[80], oc=[16], sn=[RO * 48], ln=[RO * 32])),
+) for name, cols in bufs.items()}
 for _i in range(8):
     SCRATCH["p%d" % _i] = ("psum", [128, 512], F)
 DSEMS = ["d%d" % i for i in range(48)]
-SEMAPHORES = ["cv", "cs", "cp", "cg", "sent"] + DSEMS + ["az%d" % t for t in range(RO)] + ["an%d" % t for t in range(RO)] + ["ae%d" % t for t in range(RO)]
+SEMAPHORES = ["cv", "cs", "cp", "cg", "sent"] + DSEMS + [x + str(t) for x in ("az", "an", "ae") for t in range(RO)]
+
+
+def label(s):
+    bare = lambda k: k.rstrip("0123456789")
+    return "<".join(bare(k) if bare(k) in ("sz", "sn", "sm", "nf", "E", "eo", "zt", "cm", "Z1_", "zo", "eout") else k for k in s.split("<"))
 
 
 def rank_program(g, core, T, topo):
     rank = T.rank_of(core)
     if rank is None:
         return
-    ops, lastw, readers, nd, own_send = [], {}, {}, [0], {}
+    ops, lastw, readers, nd, own_send, step = [], {}, {}, [0], {}, [0]
 
     def width(a):
         n = 1
@@ -67,8 +59,9 @@ def rank_program(g, core, T, topo):
         return n
 
     def cost(a, per, kind):
-        if kind: return 0.05 + width(a) * (GATHER if kind == "g" else SCATTER) * CYC
-        return 0.03 + max(64, width(a) * per) * CYC
+        if kind == "h": per = 0.5
+        elif kind: return 0.06 + width(a) * (GATHER if kind == "g" else SCATTER) * CYC
+        return FIX + max(64, width(a) * per) * CYC
 
     def deps(e, R, Wr):
         d, soft = set(), set()
@@ -82,31 +75,35 @@ def rank_program(g, core, T, topo):
 
     def add(e, fn, R, Wr, c, tok=None, ext=None, lat=0.0):
         d, soft = deps(e, R, Wr)
-        ops.append({"e": e, "fn": fn, "d": d, "soft": soft, "tok": tok, "ext": ext, "c": c, "lat": lat,
-                    "far": [own_send[x[0]] for x in ext or ()]})
+        ops.append({"e": e, "fn": fn, "d": d, "soft": soft, "tok": tok, "ext": ext, "c": c, "lat": lat, "step": step[0],
+                    "lab": label((Wr + [""])[0] + "<" + (R + [""])[0]), "far": [own_send[x[0]] for x in ext or ()]})
         n = len(ops) - 1
         for k in R: readers.setdefault(k, []).append(n)
         for k in Wr:
             lastw[k] = n; readers[k] = []
         return n
 
-    def dma(e, pairs, R, Wr, lat=0.8):
+    def dma(e, pairs, R, Wr, each=0.6):
         name = DSEMS[nd[0]]; nd[0] += 1
         q = g.sync if e == "y" else g.scalar
         def fn():
             for o, i in pairs: q.dma_start(o, i).then_inc(T.sem[name], 16)
-        return add(e, fn, R, Wr, 0.06 * len(pairs) + (lat if e == "y" else 0.0), tok=(name, 16 * len(pairs)), lat=2.0)
+        return add(e, fn, R, Wr, len(pairs) * (each * DMAF if e == "y" else 0.06), tok=(name, 16 * len(pairs)), lat=2.0)
 
     V, S, P = g.vector, g.scalar, g.tensor
+    ident, absf, relu = AF.Identity, AF.Abs, AF.Relu
     def ts(o, i, a, b, o0, o1, R, Wr, k=None):
         add("v", (lambda: V.tensor_scalar(o, i, a, None, o0)) if o1 is None else (lambda: V.tensor_scalar(o, i, a, b, o0, o1)), R, Wr, cost(o, 1, k))
     def tt(o, a, b, op, R, Wr, k=None):
         add("v", lambda: V.tensor_tensor(o, a, b, op), R, Wr, cost(b, 1 if any(x[0] == "P" for x in R) else 2, k))
     def cp(o, i, R, Wr, ext=None, k=None): add("v", lambda: V.tensor_copy(o, i), R, Wr, cost(i, 1, k), ext=ext)
-    def ms(o, c, Wr): add("v", lambda: V.memset(o, c), [], Wr, cost(o, 0.5, None))
     def act(o, i, f, R, Wr, bias=0.0, scale=1.0, ext=None, k=None):
         add("s", lambda: S.activation(o, i, f, bias=bias, scale=scale), R, Wr, cost(o, 1, k), ext=ext)
-    def gat(o, i, R, Wr, bias=0.0, scale=1.0, ext=None): act(o, i, AF.Identity, R, Wr, bias, scale, ext, "g")
+    def const(o, c, Wr): act(o, T.x240[:, 0:width(o)], ident, ["x240"], Wr, bias=c, scale=0.0)
+    def aff(o, i, scale, bias, R, Wr):
+        if Wr[0] in AFFV: ts(o, i, scale, bias, ALU.mult, ALU.add, R, Wr)
+        else: act(o, i, ident, R, Wr, bias, scale)
+    def gat(o, i, R, Wr, bias=0.0, scale=1.0, ext=None, f=ident): act(o, i, f, R, Wr, bias, scale, ext, "g")
     def iota(o, pat, base, cm, Wr, isint=False):
         add("g", (lambda: g.iota(o, pat, base, cm)) if isint else (lambda: g.iota(o, pat, base, cm, allow_small_or_imprecise_dtypes=True)), [], Wr,
             0.13 + 2 * width(o) * CYC)
@@ -114,155 +111,162 @@ def rank_program(g, core, T, topo):
         def fn():
             for x in lst: last = P.matmul(*x)
             return last
-        add("p", fn, R, Wr, sum(max(64, width(x[2])) for x in lst) * CYC / 2)
-    def wrap(out, w, src, lo, hi, start, stop):
-        return [(out, w(r), src[:, lo + r:hi:16], start and r == 0, stop and r == 15) for r in range(16)]
+        add("p", fn, R, Wr, sum(max(64, width(x[2])) for x in lst) * CYC / 2, lat=0.1)
+    def group(lst, start=True, stop=True):
+        return [x + (start and n == 0, stop and n == len(lst) - 1) for n, x in enumerate(lst)]
+    def wrap(out, w, src, lo, hi):
+        return [(out, w(r), src[:, lo + r:hi:16]) for r in range(16)]
     def wset(i): return lambda r: T.ww[:, 144 * i + 15 - r:144 * i + 143 - r]
-    WD, WBIG, WU0, WU1, WN, WC, WP = [wset(i) for i in range(7)]
+    WD, WBIG, WQ, W2, WN, WC, WP, WNS = [wset(i) for i in range(8)]
     WH = lambda r: T.wh[:, 15 - r:143 - r]
-    ID, NID, BID, HID, RN, R3, I16, I16R = [T.wm[:, 128 * i:128 * i + 128] for i in range(8)]
-    pcol, rcol, p16, r2, r240, dcol, dcol2 = [T.pc[:, i:i + 1] for i in range(7)]
+    WH16 = lambda r: T.wh[:, 159 - r:287 - r]
+    ID, NID, IB, H0, RN, R3, I16, I16R, I256, IBIG, NBIG, I128, I2, H1 = [T.wm[:, 128 * i:128 * i + 128] for i in range(14)]
+    IDH = T.idh[:]
+    pcol, rcol, p16, r2, p7, r240, dcol, dcol2, rsq, pq, ph0, ph1, rs0 = [T.pc[:, i:i + 1] for i in range(13)]
     mk = lambda f: T.mk[:, f:f + 1]
     mk2 = lambda f: T.mk2[:, f:f + 1]
+    cs = lambda f: T.cs[:, f:f + 1]
     sm = lambda i, n=1: T.sm[:, 16 * i:16 * (i + n)]
     su = lambda i: T.su[:, 16 * i:16 * i + 16]
     st = lambda a, b: T.stg[:, 240 * a:240 * b]
+    tk = lambda i: T.tk[:, 16 * i:16 * i + 16]
     P0, P1, P2, P3, P4, P5, P6, P7 = [T["p%d" % i] for i in range(8)]
     HCOL, Z0, Z1 = 3072, 3328, 4352
-    AK = ["A%d" % k for k in range(12)]; XK = ["X%d" % k for k in range(12)]; OAK = ["OA0", "OA1", "OA2"]
-    EK = ["E%d" % b for b in range(4)]; Z0K = ["Z0"]
-    ident, absf, relu, sign = AF.Identity, AF.Abs, AF.Relu, AF.Sign
+    AK = ["A%d" % k for k in range(12)]; XK = ["X%d" % k for k in range(12)]; OAK = ["OA%d" % k for k in range(12)]
+    EK = ["E%d" % b for b in range(4)]; OF = ["Of%d" % j for j in range(15)]; OT = ["O", "Oa", "Or"]; KT = ["Kf0", "Kf1"]
 
-    dma("y", [(T.oi[:, 0:240], T.own[0:8, :]), (T.oi[:, 240:480], T.own[8:16, :])], [], ["oi"])
+    dma("y", [(T.oi[:, 0:240], T.own[0:8, :]), (T.oi[:, 240:480], T.own[8:16, :])], [], ["oi"], 0.8)
     dma("y", [(T.ei[:, 0:192], T.ends[:, 0:192])], [], ["ei0"])
-    dma("y", [(T.zt[:, 256 * j:256 * j + 256], T.st[:, 0:256]) for j in range(4)], [], ["zt0"])
-    dma("y", [(T.mt[:, 0:W], T.msg[:])], [], ["M"], 3.5)
+    dma("y", [(T.zt[:, 0:256], T.st[:, 0:256])], [], ["zq"])
+    dma("y", [(T.mt[:, 0:W], T.msg[:])], [], ["M"], 4.9)
+    dma("y", [(T.oi[:, 480:720], T.enc[:])], [], ["ki"], 0.8)
+    dma("y", [(T.ti[0:64, 16 * q:16 * q + 16], T.th[q, :]) for q in range(8)], [], ["ti"], 0.1)
+    dma("y", [(T.xx[:, Z0:Z0 + 1024], T.st[:])], [], ["Z0"], 1.4)
+    dma("y", [(T.ei[:, 192:768], T.ends[:, 192:768])], [], ["ei1"], 1.55)
+    cp(T.zt[:, 256:512], T.zt[:, 0:256], ["zq"], ["zq1"], k="h")
+    cp(T.zt[:, 512:1024], T.zt[:, 0:512], ["zq", "zq1"], ["zt0"], k="h")
     iota(T.ip[:, 0:1], [[0, 1]], 0, 1, ["ip"], True)
-    iota(T.x240[:], [[1, 256]], 0, 0, ["x240"])
-    iota(T.i143[:], [[1, 144]], -15, 0, ["i143"])
-    iota(T.bo0[:], [[-256, 4]], -128, 0, ["bo0"])
-    iota(T.lc0[:], [[0, 24], [-16, 16]], 128, 0, ["lc0"])
-    iota(T.kcn[:], [[-1, 192]], 0, 0, ["kcn"])
-    iota(T.kc2[:], [[2, 192]], 0, 0, ["kc2"])
-    iota(T.b128[:], [[16, 8], [0, 16]], 0, 0, ["b128"])
-    iota(T.d20[:], [[16, 16]], W, 0, ["d20"])
-    iota(T.r256[:], [[0, 16], [1, 16]], 0, 0, ["r256"])
-    iota(T.h256[:], [[1, 16], [0, 16]], 0, 0, ["h256"])
-    iota(T.hc[:, 0:16], [[-1, 16]], 0, 0, ["hc0"])
-    iota(T.ch[:], [[1, 16]], 192, 0, ["ch"])
-    iota(T.bc0[:], [[2, 8]], 0, 0, ["bc0"])
-    ms(T.wx[:, 0:960], 0.0, AK[:4])
-    for j in range(4):
-        act(T.ot[:, 960 * j:960 * j + 960], T.wx[:, 0:960], AF.Copy, AK[:4], ["Of%d" % j])
-    OF = ["Of%d" % j for j in range(4)]; KF = ["Kf%d" % j for j in range(4)]
-    dma("s", [(T.oi[:, 480:720], T.enc[:])], [], ["ki"])
-    dma("s", [(T.ti[0:64, 16 * q:16 * q + 16], T.th[q, :]) for q in range(8)], [], ["ti"])
-    for j in range(4):
-        act(T.kt[:, 960 * j:960 * j + 960], T.wx[:, 0:960], AF.Copy, AK[:4], ["Kf%d" % j])
+    for o, pat, base, key in (
+            (T.x240[:], [[1, 256]], 0, "x240"), (T.i143[:], [[1, 144]], -15, "i143"), (T.bo0[:], [[-256, 4]], -128, "bo0"),
+            (T.lc0[:], [[-16, 16]], 128, "lc0"), (T.lh0[:], [[0, 12], [-8, 32]], 128, "lh0"), (T.kcn[:], [[-1, 192]], 0, "kcn"),
+            (T.kc2[:], [[2, 192]], 0, "kc2"), (T.b128[:], [[16, 8], [0, 16]], 0, "b128"),
+            (T.d20[:], [[16, 16]], W, "d20"), (T.r256[:], [[0, 16], [1, 16]], 0, "r256"), (T.h256[:], [[1, 16], [0, 16]], 0, "h256"),
+            (T.bc0[:], [[2, 8]], 0, "bc0"), (T.tk0[:, 0:16], [[1, 16]], 0, "tq0"), (T.tk0[:, 48:64], [[1, 16]], 192, "tq1")):
+        iota(o, pat, base, 0, [key])
     ts(T.ip[:, 1:2], T.ip[:, 0:1], 15, None, ALU.bitwise_and, None, ["ip"], ["ip1"])
     ts(T.ip[:, 2:3], T.ip[:, 0:1], 112, None, ALU.bitwise_and, None, ["ip"], ["ip2"])
     ts(T.ip[:, 3:4], T.ip[:, 0:1], 1, 7, ALU.arith_shift_right, ALU.bitwise_and, ["ip"], ["ip3"])
-    cp(T.pc[:, 0:4], T.ip[:], ["ip", "ip1", "ip2", "ip3"], ["pc"])
+    ts(T.ip[:, 4:5], T.ip[:, 0:1], 7, None, ALU.bitwise_and, None, ["ip"], ["ip4"])
+    cp(T.pc[:, 0:5], T.ip[:, 0:5], ["ip", "ip1", "ip2", "ip3", "ip4"], ["pc"])
+    for j in range(15 - FILLG):
+        aff(T.ot[:, 256 * j:256 * j + 256], T.x240[:], 1.0, 256.0 * j, ["x240"], [OF[j]])
+    iota(T.ot[:, W - 256 * FILLG:W], [[1, 256 * FILLG]], W - 256 * FILLG, 0, OF[15 - FILLG:])
     ts(r240, rcol, 240.0, None, ALU.mult, None, ["pc"], ["r240"])
     ts(st(3, 4), T.x240[:, 0:240], r240, None, ALU.add, None, ["x240", "r240"], ["s3"])
     ts(T.mk[:], T.x240[:, 0:16], rcol, None, ALU.is_equal, None, ["x240", "pc"], ["mk"])
-    cp(T.hb[:, 240:480], st(3, 4), ["s3"], ["hb1"])
-    ts(T.mk2[:], T.x240[:, 0:4], r2, None, ALU.is_equal, None, ["x240", "pc"], ["mk2"])
-    tt(st(5, 6), st(3, 4), T.hb[:, 240:480], ALU.subtract, ["s3", "hb1"], ["s5"])
+    cp(T.hb[:], st(3, 4), ["s3"], ["hb1"])
+    ts(T.mk2[:, 0:4], T.x240[:, 0:4], r2, None, ALU.is_equal, None, ["x240", "pc"], ["mk2"])
+    tt(st(5, 6), st(3, 4), T.hb[:], ALU.subtract, ["s3", "hb1"], ["s5"])
+    dma("y", [(T.ot[3::16, 0:W], st(5, 6))], ["s5"] + OF, ["Or"], 0.75)
     cp(st(0, 2), T.oi[:, 0:480], ["oi"], ["s0"])
     ts(T.sti[:, 0:240], T.oi[:, 0:240], 8, None, ALU.arith_shift_right, None, ["oi"], ["sti0"])
     ts(T.sti[:, 240:480], T.oi[:, 0:240], 4, 15, ALU.arith_shift_right, ALU.bitwise_and, ["oi"], ["sti1"])
     ts(T.sti[:, 480:720], T.oi[:, 0:240], 15, None, ALU.bitwise_and, None, ["oi"], ["sti2"])
-    dma("y", [(T.ot[f::16, 0:W], st(s, s + 1)) for f, s in ((2, 3), (3, 5), (0, 0), (1, 1))], ["s0", "s3", "s5"] + OF, ["Oa"])
+    dma("y", [(T.ot[f::16, 0:W], st(f, f + 1)) for f in (0, 1)], ["s0"] + OF, ["Oa"], 0.75)
     ts(st(6, 7), T.sti[:, 0:240], 192.0, None, ALU.mult, None, ["sti0"], ["s6"])
     cp(st(7, 9), T.sti[:, 240:720], ["sti1", "sti2"], ["s7"])
-    dma("y", [(T.ot[f::16, 0:W], st(s, s + 1)) for f, s in ((4, 6), (5, 7), (6, 8))], ["s6", "s7"] + OF, ["O"])
-    dma("y", [(T.wx[:, Z0:Z0 + 1024], T.st[:])], [], Z0K)
-    dma("y", [(T.ei[:, 192:768], T.ends[:, 192:768])], [], ["ei1"])
+    act(st(9, 10), st(8, 9), AF.Square, ["s7"], ["s9"])
     cp(T.eo[:, 0:192], T.ei[:, 0:192], ["ei0"], ["eo0"])
     ts(T.cs[:, 0:4], T.bo0[:], mk2(0), None, ALU.mult, None, ["bo0", "mk2"], ["bo"])
-    def weights(i, w, w2=None):
-        ts(T.ww[:, 144 * i:144 * i + 144], T.i143[:], p16, w, ALU.is_equal, ALU.mult, ["i143", "pc", "mk", "mk2", "wp"], ["w%d" % i])
-    def diag(i, w):
-        ts(T.wm[:, 128 * i:128 * i + 128], T.x240[:, 0:128], pcol, w, ALU.is_equal, ALU.mult, ["x240", "pc"], ["m%d" % i])
-    weights(2, mk(0)); weights(3, mk(1)); weights(0, 256.0)
-    diag(0, 1.0); diag(1, -1.0)
-    if LIVES > 1: diag(2, float(B))
+    def scaled(i, j, w, R=()):
+        aff(T.ww[:, 144 * i:144 * i + 144], T.ww[:, 144 * j:144 * j + 144], w, 0.0, ["w%d" % j] + list(R), ["w%d" % i])
+    ts(T.ww[:, 0:144], T.i143[:], p16, 256.0, ALU.is_equal, ALU.mult, ["i143", "pc"], ["w0"])
+    ts(T.lanh[:], T.lh0[:], p7, None, ALU.subtract, None, ["lh0", "pc"], ["lanh"])
+    aff(pq, rcol, 8.0, p16, ["pc"], ["pq"])
+    ts(T.ww[:, 288:432], T.i143[:], pq, mk2(0), ALU.is_equal, ALU.mult, ["i143", "pq", "mk2"], ["w2"])
+    aff(ph0, p7, 1.0, p16, ["pc"], ["ph0"])
+    aff(ph1, ph0, 1.0, 8.0, ["ph0"], ["ph1"])
+    ts(H0, T.x240[:, 0:128], ph0, None, ALU.is_equal, None, ["x240", "ph0"], ["m3"])
+    ts(H1, T.x240[:, 0:128], ph1, None, ALU.is_equal, None, ["x240", "ph1"], ["m13"])
+    ts(ID, T.x240[:, 0:128], pcol, None, ALU.is_equal, None, ["x240", "pc"], ["m0"])
     ts(T.lanec[:], T.lc0[:], rcol, None, ALU.subtract, None, ["lc0", "pc"], ["lanec"])
-    mm([(P5[:, 272:464], ID, T.kc2[:], True, True)], ["m0", "kc2"], ["P5"])
-    ts(T.idf[:], T.x240[:, 0:128], pcol, None, ALU.is_equal, None, ["x240", "pc"], ["idf"])
-    ts(T.cs[:, 12:13], mk2(0), 1.0 / 16, None, ALU.mult, None, ["mk2"], ["wp"])
-    diag(3, 0.5); diag(6, 16.0); diag(7, 1.0 / 16)
-    weights(4, mk2(1)); weights(6, T.cs[:, 12:13]); weights(5, mk2(2)); weights(1, 4096.0)
+    for i, w in ((1, -1.0), (2, 1.0 / B), (6, 16.0), (7, 1.0 / 16), (8, 256.0), (9, BIG), (10, -BIG), (11, 128.0), (12, 2.0)):
+        aff(T.wm[:, 128 * i:128 * i + 128], ID, w, 0.0, ["m0"], ["m%d" % i])
+    for o, key in ((T.idf[:], "idf"), (IDH, "idh")): aff(o, ID, 1.0, 0.0, ["m0"], [key])
+    mm(group([(P5[:, 272:464], ID, T.kc2[:])]), ["kc2", "m0"], ["P5"])
+    aff(cs(12), mk2(0), 1.0 / 4096, 0.0, ["mk2"], ["wp"])
+    aff(T.mk2[:, 4:8], T.mk2[:, 0:4], 1.0 / 256, 0.0, ["mk2"], ["mkq"])
+    scaled(4, 0, mk2(5), ["mkq"]); scaled(6, 0, cs(12), ["wp"]); scaled(5, 0, mk2(6), ["mkq"])
+    scaled(7, 4, 1.0 / 4096); scaled(3, 0, 1.0 / 128)
 
     def late_constants():
         cp(st(2, 3), T.oi[:, 480:720], ["ki"], ["s2"])
-        cp(T.hb[:, 0:240], st(2, 3), ["s2"], ["hb0"])
-        tt(st(4, 5), st(2, 3), T.hb[:, 0:240], ALU.subtract, ["s2", "hb0"], ["s4"])
-        dma("y", [(T.kt[f::16, 0:W], st(s, s + 1)) for f, s in ((2, 2), (3, 4))], ["s2", "s4"] + KF, ["K"])
+        dma("y", [(T.kt[0::16, 0:W], st(2, 3))], ["s2"], ["Kf1"], 0.75)
+        dma("y", [(T.kt[f::16, 0:W], T.kt[0::16, 0:W]) for f in range(1, 16)], ["Kf1"], ["Kf0"], 0.55)
+        for j in range(4): iota(T.nt[:, 960 * j:960 * j + 960], [[1, 960]], 960 * j, 0, ["nt%d" % j])
+        ts(T.pw[:, 0:16], T.x240[:, 0:16], rcol, -0.5, ALU.is_lt, ALU.mult, ["x240", "pc"], ["pw0"])
+        ts(T.pw[:, 0:16], T.pw[:, 0:16], 1.0, None, ALU.add, None, ["pw0"], ["pw0"])
+        const(T.pw[:, 16:32], 0.0, ["pw1"])
+        add("v", lambda: V.tensor_tensor_scan(T.pw[:, 32:48], T.pw[:, 0:16], T.pw[:, 16:32], float(1 << 19), ALU.mult, ALU.add), ["pw0", "pw1"], ["pw2"], 0.1)
+        scaled(1, 0, T.pw[:, 47:48], ["pw2"])
         for b in range(1, 4):
-            dma("y", [(T.zt[:, 1024 * b + 256 * j:1024 * b + 256 * j + 256], T.st[:, 256 * b:256 * b + 256]) for j in range(4)], [], ["zt%d" % b])
-        ts(T.thb[:], P7[:, 0:64], 256.0, None, ALU.mult, None, ["P7"], ["th0", "th1", "th2", "th3"])
-        ts(T.vq[:], T.lanec[:, 0:16], -1.0 / 16, None, ALU.mult, None, ["lanec"], ["vq"])
-        ts(T.dm[:], T.d20[:], rcol, None, ALU.add, None, ["d20", "pc"], ["dm"])
-        ts(dcol, rcol, float(W), None, ALU.add, None, ["pc"], ["dcol"])
-        ts(dcol2, rcol, float(W + 16), None, ALU.add, None, ["pc"], ["dcol2"])
-        ms(T.qc[:], -0.25, ["qc"])
-        ms(T.cwc[:, 0:16], -2048.0, ["cwc0"])
-        ms(T.cwc[:, 272:400], -2048.0, ["cwc1"])
-        ts(T.eq2[:], T.r256[:], rcol, 8192.0, ALU.is_le, ALU.mult, ["r256", "pc"], ["eq2"])
-        ts(T.hc[:, 16:272], T.r256[:], 0.0, rcol, ALU.mult, ALU.subtract, ["r256", "pc"], ["hc"])
-        ts(T.cwc[:, 16:272], T.eq2[:], -2048.0, None, ALU.add, None, ["eq2"], ["cwc"])
-        ts(T.wm[:, 512:640], T.b128[:], p16, mk2(1), ALU.is_equal, ALU.mult, ["b128", "pc", "mk2"], ["m4"])
-        ts(T.wm[:, 640:768], T.b128[:], p16, mk(6), ALU.is_equal, ALU.mult, ["b128", "pc", "mk"], ["m5"])
-        ts(T.wh[:], T.i143[:], p16, None, ALU.is_equal, None, ["i143", "pc"], ["wh"])
-        cp(T.idh[:], ID, ["m0"], ["idh"])
+            dma("y", [(T.zt[:, 1024 * b + 256 * j:1024 * b + 256 * j + 256], T.st[:, 256 * b:256 * b + 256]) for j in range(4)], [], ["zt%d" % b], 0.5)
+        cp(T.thh[:, 0:64], P7[:, 0:64], ["P7"], ["thh"])
+        tt(T.thh[:, 64:128], P7[:, 0:64], T.thh[:, 0:64], ALU.subtract, ["P7", "thh"], ["thl"])
+        aff(T.vq[:], T.lanec[:], -1.0 / 16, 7.53125, ["lanec"], ["vq"])
+        ts(T.dm[:], T.d20[:], rcol, 1.0 / 4096, ALU.add, ALU.mult, ["d20", "pc"], ["dm"])
+        aff(dcol, rcol, 1.0, float(W), ["pc"], ["dcol"])
+        aff(dcol2, rcol, 1.0, float(W + 16), ["pc"], ["dcol2"])
+        aff(rs0, rcol, rcol, 0.0, ["pc"], ["rsq0"])
+        aff(rsq, rs0, -1.0, 1.0, ["rsq0"], ["rsq"])
+        for i, c in ((0, 7.53125), (2, -3.0625), (3, 1.0), (5, 0.0), (6, 2048.0)): const(tk(i), c, ["tk%d" % i])
+        aff(tk(1), T.dm[:], 1.0, -W / 4096.0, ["dm"], ["tk1"])
+        ts(tk(4), T.pw[:, 16:32], T.pw[:, 47:48], -512.0, ALU.add, ALU.mult, ["pw1", "pw2"], ["tk4"])
+        aff(cs(14), mk2(1), 16.0, 0.0, ["mk2"], ["cs14"])
+        aff(cs(15), mk(2), -BIG, 0.0, ["mk"], ["cs15"])
+        for i, (a, e, c) in enumerate(((16, 48, 0.0), (64, 80, 0.0), (80, 112, 1.0), (112, 128, -1.0))): const(T.tk0[:, a:e], c, ["tq%d" % (i + 2)])
+        ts(T.r3[:, 0:128], T.b128[:], p16, None, ALU.is_equal, None, ["b128", "pc"], ["r3a"])
+        aff(RN, T.r3[:, 0:128], mk2(1), 0.0, ["r3a", "mk2"], ["m4"])
+        aff(cs(13), mk(6), -2.0, 0.0, ["mk"], ["cs13"])
+        aff(T.r3[:, 128:256], T.r256[:, 0:128], cs(13), mk(7), ["r256", "cs13", "mk"], ["r3b"])
+        tt(R3, T.r3[:, 0:128], T.r3[:, 128:256], ALU.mult, ["r3a", "r3b"], ["m5"])
+        act(T.wh[:, 0:144], T.ww[:, 0:144], ident, ["w0"], ["wh"], scale=1.0 / 256)
+        act(T.wh[:, 144:288], T.ww[:, 0:144], ident, ["w0"], ["wh16"], scale=1.0 / 4096)
         cp(T.bcc[:, 0:16], T.x240[:, 0:16], ["x240"], ["bcc"])
         cp(T.bcc[:, 16:24], T.bc0[:], ["bc0"], ["bcc1"])
         act(T.vl[:, 0:256], T.x240[:], ident, ["x240", "mk"], ["vl0"], scale=mk(0))
         act(T.vl[:, 256:512], T.x240[:], ident, ["x240", "mk"], ["vl1"], scale=mk(1))
-        act(T.vt[:, 0:256], T.h256[:], ident, ["h256", "mk"], ["vt0"], scale=mk(5))
-        act(T.vt[:, 256:512], T.r256[:], ident, ["r256", "mk"], ["vt1"], scale=mk(6))
-        ts(T.cs[:, 10:11], mk(0), mk2(2), mk(6), ALU.add, ALU.add, ["mk", "mk2"], ["cs10"])
-        ts(T.cs[:, 5:6], mk(1), -1.0, 1.0, ALU.mult, ALU.add, ["mk"], ["keep5"])
-        ms(T.cs[:, 6:7], 0.0, ["keep6"])
-        ts(T.cs[:, 11:12], mk(4), 384.0, None, ALU.mult, None, ["mk"], ["cs11"])
-        ts(T.cs[:, 7:8], mk(1), 256.0, None, ALU.mult, None, ["mk"], ["keep7"])
-        ts(T.cs[:, 9:10], mk(1), 768.0, None, ALU.mult, None, ["mk"], ["keep9"])
-        ts(T.cs[:, 4:5], T.cs[:, 10:11], -1.0, 1.0, ALU.mult, ALU.add, ["cs10"], ["keep4"])
-        ts(T.cs[:, 8:9], mk(0), 512.0, T.cs[:, 11:12], ALU.mult, ALU.add, ["mk", "cs11"], ["keep8"])
+        act(T.vt[:], T.r256[:], AF.Square, ["r256"], ["vt"])
+        dma("y", [(T.vl[f::16, 0:256], x[f::16, :]) for f, x in ((5, T.h256), (6, T.r256), (7, T.vt))], ["h256", "r256", "vt"], ["vl0"], 0.06)
+        ts(cs(10), mk(0), mk2(2), mk2(3), ALU.add, ALU.add, ["mk", "mk2"], ["cs10"])
+        aff(cs(4), cs(10), -1.0, 1.0, ["cs10"], ["keep4"])
+        aff(cs(5), mk(1), -1.0, 1.0, ["mk"], ["keep5"])
+        const(cs(6), 0.0, ["keep6"])
+        aff(cs(7), mk(1), 256.0, 0.0, ["mk"], ["keep7"])
+        aff(cs(11), mk(4), 384.0, 0.0, ["mk"], ["cs11"])
+        aff(cs(8), mk(0), 512.0, cs(11), ["mk", "cs11"], ["keep8"])
+        aff(cs(9), mk(1), 768.0, 0.0, ["mk"], ["keep9"])
 
-    def later_constants():
-        tt(T.vl[:, 0:256], T.vl[:, 0:256], T.vt[:, 0:256], ALU.add, ["vl0", "vt0"], ["vl0"])
-        tt(T.vl[:, 0:256], T.vl[:, 0:256], T.vt[:, 256:512], ALU.add, ["vl0", "vt1"], ["vl0"])
-
-    def owners(t, ogv):
+    def owners(t):
         b = t % 4
-        mm([(P1[:, 0:384], ID, T.lanec[:], True, False)], ["m0", "lanec"], ["P1"])
-        def part(e, lo, hi, key):
-            o, i = T.oa[:, 16 * lo:16 * hi], T.ot[:, 0:W].indirect(T.eo[:, 192 * b + lo:192 * b + hi])
-            R = ["O", "Oa", "eo%d" % b, "bo"]
-            if e == "s": gat(o, i, R, [key], bias=T.cs[:, b:b + 1])
-            else: ts(o, i, T.cs[:, b:b + 1], None, ALU.add, None, R, [key], "g")
-        if ogv: part("v", 192 - ogv, 192, "OA3")
-        for j in ((2, 0, 1) if ogv == 64 else (0, 1, 2)):
-            if 64 * j < 192 - ogv:
-                part("s", 64 * j, min(64 * j + 64, 192 - ogv), OAK[j])
-                if j: ops[-1]["soft"].add(lastw[OAK[j - 1]])
-            mm(wrap(P1[:, 64 * j:64 * j + 64], WU0, T.oa, 1024 * j, 1024 * j + 1024, False, False)
-               + wrap(P1[:, 192 + 64 * j:256 + 64 * j], WU1, T.oa, 1024 * j, 1024 * j + 1024, False, j == (1 if ogv == 64 else 2)),
-               [OAK[j], "w2", "w3"] + (["OA3"] if j == 2 else []), ["P1"])
-    OAK = OAK + ["OA3"]
+        mm(group([(P1[:, 0:384], ID, T.lanh[:])], True, False), ["m0", "lanh"], ["P1"])
+        for a, e in BC:
+            o, i = T.oa[:, 256 * a:256 * e], T.ot[:, 0:W].indirect(T.eo[:, 192 * b + 16 * a:192 * b + 16 * e])
+            R = OT + ["eo%d" % b, "bo"]
+            if a == 0: ts(o, i, cs(b), None, ALU.add, None, R, OAK[a:e], "g")
+            else: gat(o, i, R, OAK[a:e], bias=cs(b))
+            mm(group([(P1[:, 32 * a:32 * e], WQ(r), T.oa[:, 256 * a + r:256 * e:8]) for r in range(8)], False, e == 12), OAK[a:e] + ["w2"], ["P1"])
 
-    def arrive(t):
-        cp(T.mt[:].indirect(T.ln[:, 32 * t:32 * t + 16]), T.lz[:, 256 * t:256 * t + 256], [], ["M"],
-           ext=[("az%d" % t, cnt_in[t]), ("an%d" % t, cnt_in[t])], k="s")
+    def live():
+        ts(T.ee[:], P1[:, 0:384], 0.0, None, ALU.is_equal, None, ["P1"], ["ee"])
+        mm(group([(P5[:, 0:192], H0, T.ee[:, 0:384:2]), (P5[:, 0:192], H1, T.ee[:, 1:384:2])]), ["ee", "m3", "m13"], ["P5"])
+        act(T.d0[:], P5[:, 0:192], relu, ["P5"], ["d0"], bias=float(B), scale=-float(B))
+        tt(T.d2[:], T.d0[:], P5[:, 272:464], ALU.add, ["d0", "P5"], ["d2"])
 
-    def arrive_em(t):
-        gat(T.emr[:], T.ot[:, 0:W].indirect(T.ln[:, 32 * t + 16:32 * t + 32]), ["O", "Oa"], ["emr"], ext=[(("ae%d" if EMSEND else "an%d") % t, cnt_in[t])])
-
-    def arrive_k(t):
-        cp(T.kt[:].indirect(T.ln[:, 32 * t:32 * t + 16]), T.emr[:], ["emr"], ["K"], ext=[("an%d" % t, cnt_in[t])], k="s")
+    def threshold(t):
+        b = t % 4; o = P5[:, 464:480]
+        mm(group([(o, I256, T.thh[:, 16 * b:16 * b + 16]), (o, I256, T.thh[:, 64 + 16 * b:80 + 16 * b])]
+                 + ([(o, IBIG, nfs(t - 4))] if t > 3 else [])), ["thh", "thl", "m8", "m9"] + (["nf%d" % (t - 4)] if t > 3 else []), ["P5"])
 
     dst = [T.cores[(rank + 1 + t % (NR - 1)) % NR] for t in range(RO)]
     src = [T.cores[(rank - 1 - t % (NR - 1)) % NR] for t in range(RO)]
@@ -274,8 +278,20 @@ def rank_program(g, core, T, topo):
         sent[0] += len(topo.engines(core, dst[t]))
         own_send[sem] = add("g", lambda: g.remote_dma(o, i, T.sem[sem], T.sem.sent, pid, rid, m), R, [], 1.0, tok=("sent", 0))
 
-    nf, cm, colf, tc, hp, new, fa, jj, nhd, clb, tab, fav, f0, pu1, t1, nhs = [sm(i) for i in range(16)]
-    nfb, fb, hasp, nhp, k0p, sn_, ra, rb = [sm(16 + i) for i in range(8)]
+    def arrive(t):
+        cp(T.mt[:].indirect(T.ln[:, 32 * t:32 * t + 16]), T.lz[:, 256 * t:256 * t + 256], [], ["M"],
+           ext=[("az%d" % t, cnt_in[t]), ("an%d" % t, cnt_in[t])], k="s")
+
+    def arrive_em(t):
+        gat(T.emr[:], T.nt[:].indirect(T.ln[:, 32 * t + 16:32 * t + 32]), ["nt%d" % j for j in range(4)], ["emr"], ext=[("ae%d" % t, cnt_in[t])])
+
+    def arrive_k(t):
+        cp(T.kt[:].indirect(T.ln[:, 32 * t:32 * t + 16]), T.emr[:], ["emr"], KT, ext=[("an%d" % t, cnt_in[t])], k="s")
+
+    tc, fa, f1, fav, pu1, so, ra = [sm(i) for i in range(1, 8)]
+    tq = sm(10, 2)
+    cms = lambda t: sm(12 + t % 2)
+    nfs = lambda t: T.nfs[:, 16 * t:16 * t + 16]
 
     def list_mask():
         act(T.la[:], P4[:, 0:192], absf, ["P4"], ["la"], scale=8192.0)
@@ -283,228 +299,204 @@ def rank_program(g, core, T, topo):
     def hints(t):
         tt(T.hs[:], T.ec[:].indirect(su(2)), T.mm[:], ALU.mult, EK + ["colu", "mm"], ["hs"], "g")
 
-    def hints_p():
-        mm([(P4[:, 0:192], ID, T.kcn[:], True, False)]
-           + [(P4[:, 16 * k:16 * k + 16], ID, T.rowb[:], False, k == 11) for k in range(12)], ["rowb", "m0", "kcn"], ["P4"])
-        mm([(P7[:, 0:16], ID, T.fbb[:], True, False)] + wrap(P7[:, 0:16], WH, T.hs, 0, 256, False, True), ["hs", "wh", "fbb", "m0"], ["P7"])
+    def hints_p(t):
+        mm(group([(P4[:, 0:192], ID, T.kcn[:])] + [(P4[:, 16 * k:16 * k + 16], ID, T.rowb[:]) for k in range(12)]), ["rowb", "m0", "kcn"], ["P4"])
+        mm(group([(P7[:, 0:16], IBIG, tk(3)), (P7[:, 0:16], NBIG, nfs(t))] + wrap(P7[:, 0:16], WH, T.hs, 0, 256)),
+           ["hs", "wh", "tk3", "nf%d" % t, "m9", "m10"], ["P7"])
 
-    def hints_b():
-        tt(T.newh[:], P7[:, 0:16], cm, ALU.min, ["P7", "cm"], ["new"])
+    def hints_b(t):
+        tt(T.newh[:], P7[:, 0:16], cms(t), ALU.min, ["P7", "cm%d" % (t % 2)], ["new"])
 
     def list_bounds():
         for o, w in ((0, ID), (192, NID)):
-            mm([(P4[:, o:o + 192], w, T.la[:], True, False)]
-               + [(P4[:, o + 16 * k:o + 16 * k + 16], T.idh[:], T.newh[:], False, k == 11) for k in range(12)], ["la", "new", "m0", "m1", "idh"], ["P4"])
+            mm(group([(P4[:, o:o + 192], w, T.la[:])] + [(P4[:, o + 16 * k:o + 16 * k + 16], IDH, T.newh[:]) for k in range(12)]),
+               ["la", "new", "m0", "m1", "idh"], ["P4"])
 
     def list_update(t):
         b = t % 4; eb = T.ec[:, 192 * b:192 * b + 192]
-        yield tt(T.ld[:], eb, P4[:, 0:192], ALU.min, ["P4", EK[b]], ["ld"])
-        yield tt(eb, T.ld[:], P4[:, 192:384], ALU.max, ["ld", "P4"], [EK[b]])
+        tt(T.ld[:], eb, P4[:, 0:192], ALU.min, ["P4", EK[b]], ["ld"])
+        tt(eb, T.ld[:], P4[:, 192:384], ALU.max, ["ld", "P4"], [EK[b]])
         if t < 4:
-            yield ts(T.eo[:, 192 * b:192 * b + 192], eb, 2048.0, None, ALU.add, None, [EK[b]], ["eo%d" % b])
-
-    def list_out(t):
-        b = t % 4
-        act(T.eout[:, 192 * b:192 * b + 192], T.ec[:, 192 * b:192 * b + 192], ident, [EK[b]], ["eout%d" % b], bias=2048.0)
-        dma("y", [(T.ye[:, 192 * b:192 * b + 192], T.eout[:, 192 * b:192 * b + 192])], ["eout%d" % b], [])
-
-    def live():
-        act(T.u0[:], P1[:, 0:192], ident, ["P1"], ["u0"])
-        tt(T.uu[:], T.u0[:], P1[:, 192:384], ALU.mult, ["u0", "P1"], ["uu"])
-        ts(T.d0[:], T.uu[:], 0.0, float(B), ALU.not_equal, ALU.mult, ["uu"], ["d0"])
-        if LIVES:
-            act(T.sc[:], T.d0[:], ident, ["d0"], ["stale"], scale=1.0 / B)
-            act(T.d1[:], T.d0[:], ident, ["d0"], ["d1"], scale=-1.0, bias=float(B))
+            ts(T.eo[:, 192 * b:192 * b + 192], eb, 2048.0, None, ALU.add, None, [EK[b]], ["eo%d" % b])
         else:
-            ts(T.d1[:], T.uu[:], 0.0, float(B), ALU.is_equal, ALU.mult, ["uu"], ["d1"])
-        if LIVES > 1:
-            mm([(P2[:, 0:192], ID, T.kc2[:], True, False), (P2[:, 0:192], BID, T.sc[:], False, True)], ["stale", "kc2", "m0", "m2"], ["P2"])
-            act(T.d2[:], P2[:, 0:192], ident, ["P2"], ["d2"])
-        else:
-            tt(T.d2[:], T.d0[:], P5[:, 272:464], ALU.add, ["d0", "P5"], ["d2"])
+            act(T.eout[:, 192 * b:192 * b + 192], eb, ident, [EK[b]], ["eout%d" % b], bias=2048.0)
+            dma("y", [(T.ye[:, 192 * b:192 * b + 192], T.eout[:, 192 * b:192 * b + 192])], ["eout%d" % b], [])
 
     for t in range(RO):
-        b = t % 4; lo = 256 * b
+        b = t % 4; lo = 256 * b; step[0] = t
         zb = (Z0 if t < 4 else Z1) + lo; zk = "Z0" if t < 4 else "Z1_%d" % b
-        zc = T.wx[:, zb:zb + 256]
         if t:
-            arrive(t - 1)
-        mm([(P0[:, 0:128], NID, T.kcn[:, 0:128], True, False)], ["m1", "kcn"], ["P0"])
-        mm([(P3[:, 128:192], NID, T.kcn[:, 128:192], True, False)], ["m1", "kcn"], ["P3"])
+            arrive(t - 1); threshold(t)
+        else:
+            step[0] = -1; owners(0); step[0] = 0
+            dma("y", [(T.ot[f::16, 0:W], st(f + 2, f + 3)) for f in (4, 5, 6, 7)], ["s6", "s7", "s9"] + OF, ["O"], 0.75)
+        live()
+        mm(group([(P0[:, 0:128], NID, T.kcn[:, 0:128])], True, False), ["m1", "kcn"], ["P0"])
+        mm(group([(P3[:, 128:192], NID, T.kcn[:, 128:192])], True, False), ["m1", "kcn"], ["P3"])
         for a, e in CH:
             tt(T.xx[:, 256 * a:256 * e], T.mt[:, 0:W].indirect(T.eo[:, 192 * b + 16 * a:192 * b + 16 * e]),
                T.zt[:, 1024 * b:1024 * b + 256 * (e - a)], ALU.subtract, ["M", "eo%d" % b, "zt%d" % b], XK[a:e], "g")
-            if a: ops[-1]["soft"].add(len(ops) - 2)
-        if t > 1:
-            for _ in list_update(t - 2): pass
-            if t > 5: list_out(t - 2)
+        if t > 1: list_update(t - 2)
         if t: hints(t - 1)
         for a, e in CH:
             act(T.wx[:, 256 * a:256 * e], T.xx[:, 256 * a:256 * e], absf, XK[a:e], AK[a:e])
-            if a: ops[-1]["soft"].add(lastw[AK[a - 1]])
-            elif t: ops[-1]["soft"].add(lastw["OA2"])
-            if a == 0 and t: live()
             if e % 4 == 0:
-                j = e // 4 - 1
-                mm(wrap((P0, P0, P3)[j][:, 64 * j:64 * j + 64], WD, T.wx, 1024 * j, 1024 * j + 1024, False, j > 0),
+                j = a // 4
+                mm(group(wrap((P0, P0, P3)[j][:, 64 * j:64 * j + 64], WD, T.wx, 1024 * j, 1024 * j + 1024), False, j > 0),
                    AK[4 * j:4 * j + 4] + ["w0"], [("P0", "P0", "P3")[j]])
         if t:
-            hints_p(); arrive_em(t - 1)
+            hints_p(t - 1); arrive_em(t - 1)
         else:
             cp(T.tf[0:64, :], T.ti[0:64, :], ["ti"], ["tf"])
             add("p", lambda: P.transpose(P7[:, 0:64], T.tf[0:64, :], T.idf[0:64, 0:64]), ["tf", "idf"], ["P7"], 0.3)
-            owners(0, OGV0); late_constants(); live()
-        if not LIVES: act(T.sc[:], T.d0[:], ident, ["d0"], ["stale"], scale=1.0 / B)
-        mm([(P6[:, 16 * s:192], ID, T.sc[:, 0:192 - 16 * s], s == 0, s == 11) for s in range(12)], ["stale", "m0"], ["P6"])
+            late_constants(); threshold(0)
+        mm(group([(P6[:, 16 * s:192], IB, T.d0[:, 0:192 - 16 * s]) for s in range(12)]), ["d0", "m2"], ["P6"])
         if t: list_mask()
         act(T.lead[:], P6[:, 0:192], relu, ["P6"], ["lead"], bias=1.0, scale=-1.0)
-        mm([(P6[:, 192:208], NID, T.kcn[:, 0:16], True, False)]
-           + [(P6[:, 192:208], I16, T.lead[:, 16 * k:16 * k + 16], False, k == 11) for k in range(12)], ["lead", "m1", "m6", "kcn"], ["P6"])
-        mm([(P6[:, 208:224], ID, T.ch[:], True, False)]
-           + [(P6[:, 208:224], I16, T.lead[:, 176:192], False, k == t) for k in range(t + 1)], ["lead", "m0", "m6", "ch"], ["P6"])
-        for pb, pk, a, e in ((P0, "P0", 0, 128), (P3, "P3", 128, 192)):
-            tt(T.kb[:, 0, a:e], pb[:, a:e], T.d0[:, a:e], ALU.add, [pk, "d0"], ["kb0" + pk])
-            tt(T.kb[:, 1, a:e], pb[:, a:e], T.d1[:, a:e], ALU.add, [pk, "d1"], ["kb1" + pk])
-            tt(T.kb[:, 2, a:e], T.d2[:, a:e], pb[:, a:e], ALU.subtract, [pk, "d2"], ["kb2" + pk])
-        tt(T.t1[:, :, 0:64], T.kb[:, :, 0:64], T.kb[:, :, 64:128], ALU.min, ["kb0P0", "kb1P0", "kb2P0"], ["t1"])
-        tt(T.t2[:, :, 0:32], T.t1[:, :, 0:32], T.t1[:, :, 32:64], ALU.min, ["t1"], ["t2"])
-        tt(T.t3[:], T.t2[:, :, 0:16], T.t2[:, :, 16:32], ALU.min, ["t2"], ["t3"])
-        tt(T.t1[:, :, 64:96], T.kb[:, :, 128:160], T.kb[:, :, 160:192], ALU.min, ["kb0P3", "kb1P3", "kb2P3"], ["t1b"])
-        tt(T.t2[:, :, 32:48], T.t1[:, :, 64:80], T.t1[:, :, 80:96], ALU.min, ["t1b"], ["t2b"])
-        tt(T.rr[:], T.t3[:], T.t2[:, :, 32:48], ALU.min, ["t2b", "t3"], ["rr"])
+        TA, TB, TC, TD = [P6[:, 192 + 16 * i:208 + 16 * i] for i in range(4)]
+        nh = T.lead[:, 176:192]
+        mm(group([(P6[:, 192:256], ID, T.tk0[:, 0:64]), (P6[:, 192:256], IBIG, T.tk0[:, 64:128])]
+                 + [(TA, I16, T.lead[:, 16 * k:16 * k + 16]) for k in range(12)] + [(TB, NBIG, nh), (TC, IBIG, nh)]
+                 + [(TD, I16, nh) for k in range(t + 1)], True, False),
+           ["lead", "m0", "m6", "m9", "m10"] + ["tq%d" % i for i in range(6)], ["P6"])
+        for pb, pk, x, y, n in ((P0, "P0", 0, 128, "ka"), (P3, "P3", 128, 192, "kb")):
+            tt(T.kb[:, 0, x:y], pb[:, x:y], T.d0[:, x:y], ALU.add, [pk, "d0"], [n + "0"])
+            tt(T.kb[:, 1, x:y], pb[:, x:y], T.d0[:, x:y], ALU.subtract, [pk, "d0"], [n + "1"])
+            tt(T.kb[:, 2, x:y], T.d2[:, x:y], pb[:, x:y], ALU.subtract, [pk, "d2"], [n + "2"])
+        tt(T.t1[:, :, 0:64], T.kb[:, :, 0:64], T.kb[:, :, 64:128], ALU.min, ["ka0", "ka1", "ka2"], ["t0a"])
+        tt(T.t2[:], T.t1[:, :, 0:32], T.t1[:, :, 32:64], ALU.min, ["t0a"], ["t1a"])
+        tt(T.t3[:, :, 0:16], T.t2[:, :, 0:16], T.t2[:, :, 16:32], ALU.min, ["t1a"], ["t3a"])
+        tt(T.t1[:, :, 64:96], T.kb[:, :, 128:160], T.kb[:, :, 160:192], ALU.min, ["kb0", "kb1", "kb2"], ["t0b"])
+        tt(T.t3[:, :, 16:32], T.t1[:, :, 64:80], T.t1[:, :, 80:96], ALU.min, ["t0b"], ["t3b"])
+        tt(T.rr[:], T.t3[:, :, 0:16], T.t3[:, :, 16:32], ALU.min, ["t3a", "t3b"], ["rr"])
         ts(T.rk[:], T.rr[:], 255, None, ALU.bitwise_and, None, ["rr"], ["rk"])
         ts(T.off[:], T.rk[:], 16.0, rcol, ALU.mult, ALU.add, ["rk", "pc"], ["off"])
-        R0, K0, K1 = T.rr[:, 0, :], T.rk[:, 0, :], T.rk[:, 1, :]
         of, os_, om = T.off[:, 0:16], T.off[:, 16:32], T.off[:, 32:48]
-        thb = T.thb[:, 16 * b:16 * b + 16]; tk = "th%d" % b
-        mm([(P2[:, 0:384], ID, T.cwc[:, 16:400], True, False)], ["m0", "cwc", "cwc1"], ["P2"])
-        mm([(P1[:, 0:16], ID, T.cwc[:, 0:16], True, False)], ["m0", "cwc0"], ["P1"])
-        gat(T.nf_[:, 0:256], T.oa[:].indirect(of), OAK + ["off"], ["nbf"])
-        gat(T.nf_[:, 256:512], T.oa[:].indirect(om), OAK + ["off"], ["nbm"])
-        mm([(P0[:, 0:16], I16R, T.lanec[:, 0:16], True, False)] + wrap(P0[:, 0:16], WP, T.nf_, 0, 256, False, True),
-           ["nbf", "w6", "m7", "lanec"], ["P0"])
-        if EMSPLIT: mm(wrap(P3[:, 0:16], WN, T.nf_, 0, 256, True, True), ["nbf", "w4"], ["P3"])
-        else: mm(wrap(P3[:, 0:32], WN, T.nf_, 0, 512, True, True), ["nbf", "nbm", "w4"], ["P3"])
-        mm([(P5[:, 16:272], RN, T.nf_[:, 0:256], True, True)], ["nbf", "m4"], ["P5"])
-        gat(T.sz[:, 256 * t:256 * t + 256], T.wx[:, 0:3072].indirect(of), AK + ["off"], ["sz%d" % t])
+        nf, nk = nfs(t), "nf%d" % t
+        tt(nf, T.rr[:, 0, :], P5[:, 464:480], ALU.is_ge, ["rr", "P5"], [nk])
+        ts(T.rkb[:], T.rk[:, 0:2, :], 1.0, None, ALU.mult, None, ["rk"], ["rkb"])
+        mm(group([(TA, IBIG, nf), (TB, IBIG, nf), (TC, NBIG, nf), (TD, IBIG, nf), (P6[:, 208:240], ID, T.rkb[:])], False, True),
+           [nk, "rkb", "m0", "m9", "m10"], ["P6"])
+        mm(group([(P0[:, 0:16], I16R, T.lanec[:]), (P0[:, 0:16], ID, tk(0))], True, False), ["m0", "m7", "lanec", "tk0"], ["P0"])
+        gat(T.nf_[:], T.oa[:].indirect(of), OAK + ["off"], ["nbf"])
+        gat(T.kq[:, 0:256], T.oa[:].indirect(om), OAK + ["off", "cs14", "cs15"], ["nbm"], scale=cs(14), bias=cs(15))
+        mm(group(wrap(P3[:, 0:16], WNS, T.nf_, 0, 256) + [(P3[:, 0:16], I2, nf)]), ["nbf", "w7", "m12", nk], ["P3"])
+        mm(group(wrap(P0[:, 0:16], WP, T.nf_, 0, 256), False, True), ["nbf", "w6"], ["P0"])
+        mm(group([(P5[:, 16:272], RN, T.nf_[:])]), ["nbf", "m4"], ["P5"])
+        gat(T.sz[:, 256 * t:256 * t + 256], T.xx[:, 0:3072].indirect(of), XK + ["off"], ["sz%d" % t], f=absf)
         send(t, T.lz[:, 256 * t:256 * t + 256], T.sz[:, 256 * t:256 * t + 256], "az%d" % t, ["sz%d" % t])
-        act(nhp, P6[:, 192:208], relu, ["P6"], ["nhp"], bias=-256.0 * 191, scale=256.0)
-        act(jj, P6[:, 192:208], ident, ["P6"], ["jj"])
-        act(hasp, P6[:, 192:208], relu, ["P6"], ["hasp"], bias=256.0 * 192, scale=-256.0)
-        tt(nf, R0, thb, ALU.is_ge, ["rr", tk], ["nf"])
-        tt(fa, P6[:, 208:224], nf, ALU.mult, ["P6", "nf"], ["fa"])
         if t: arrive_k(t - 1)
         else:
-            cp(T.eo[:, 192:768], T.ei[:, 192:768], ["ei1"], ["eo1", "eo2", "eo3"])
-            ts(T.ec[:], T.ei[:], -2048.0, None, ALU.add, None, ["ei0", "ei1"], EK)
-        act(nfb, nf, ident, ["nf"], ["nfb"], scale=32768.0)
-        act(fb, nf, ident, ["nf"], ["fb"], scale=-32768.0, bias=32768.0)
-        act(T.fbb[:], nf, ident, ["nf"], ["fbb"], scale=-32768.0, bias=32768.0)
-        cp(su(0), P3[:, 0:16], ["P3"], ["efu"])
-        gat(T.kg[:], T.kt[:, 0:W].indirect(su(0)), ["K", "efu"], ["kg"])
-        tt(f0, P3[:, 0:16], nfb, ALU.add, ["P3", "nfb"], ["f0"])
-        if EMSPLIT: mm(wrap(P3[:, 16:32], WN, T.nf_, 256, 512, True, True), ["nbm", "w4"], ["P3"])
-        cp(T.sn[:, 32 * t + 16:32 * t + 32], P3[:, 16:32], ["P3"], ["sm%d" % t])
-        if t: hints_b()
-        mm([(P2[:, 0:256], RN, T.kg[:], False, False)]
-           + [(P2[:, 256 + 16 * m:272 + 16 * m], RN, T.kg[:, 32 * m + 16:32 * m + 32], False, m == 7) for m in range(8)], ["kg", "m4"], ["P2"])
-        mm(wrap(P1[:, 0:16], WN, T.kg, 0, 256, False, True), ["kg", "w4"], ["P1"])
-        act(T.erow[:], P5[:, 16:272], ident, ["P5"], ["erow"])
-        act(T.crow[:], P2[:, 0:384], ident, ["P2"], ["crow"])
-        tt(clb, P0[:, 0:16], T.vq[:], ALU.is_lt, ["P0", "vq"], ["clb"])
-        ts(pu1, P0[:, 0:16], 7.53125, MAGIC, ALU.add, ALU.add, ["P0"], ["pu1"])
-        ts(clb, clb, 4096.0, None, ALU.mult, None, ["clb"], ["clb"])
+            for q in range(4):
+                if q: cp(T.eo[:, 192 * q:192 * q + 192], T.ei[:, 192 * q:192 * q + 192], ["ei1"], ["eo%d" % q])
+                ts(T.ec[:, 192 * q:192 * q + 192], T.ei[:, 192 * q:192 * q + 192], -2048.0, None, ALU.add, None, ["ei1" if q else "ei0"], [EK[q]])
+        ts(su(0), P3[:, 0:16], 4096.0, W - 1.0, ALU.mult, ALU.min, ["P3"], ["efu"])
+        ts(T.su[:, 16:24], P3[:, 1:16:2], 4096.0, W - 1.0, ALU.mult, ALU.min, ["P3"], ["efo"])
+        gat(T.kq[:, 256:512], T.kt[:, 0:W].indirect(su(0)), KT + ["efu"], ["kg"], bias=-2048.0)
+        gat(T.kq[:, 512:640], T.kt[:, 0:W].indirect(T.su[:, 16:24]), KT + ["efo"], ["kg2"], bias=-2048.0)
+        tt(f1, P3[:, 0:16], T.dm[:], ALU.min, ["P3", "dm"], ["f1"])
+        if t: hints_b(t - 1)
+        mm(group(wrap(P1[:, 0:32], WH16, T.kq, 0, 512) + [(P1[:, 16:32], IBIG, nf)]), ["kg", "nbm", "wh16", "m9", nk], ["P1"])
+        cm, ck = cms(t), "cm%d" % (t % 2)
+        act(T.erow[:], P5[:, 16:272], ident, ["P5"], ["erow"], scale=1.0 / 4096)
+        ts(pu1, P0[:, 0:16], MAGIC, None, ALU.add, None, ["P0"], ["pu1"])
+        tt(T.clb[:], P0[:, 0:16], T.vq[:], ALU.is_lt, ["P0", "vq"], ["clb"])
         ts(su(4), pu1, -MAGIC, 15.0, ALU.add, ALU.min, ["pu1"], ["pu"])
-        tt(fav, f0, clb, ALU.add, ["f0", "clb"], ["fav"])
-        tt(thb, thb, nfb, ALU.add, [tk, "nfb"], [tk])
+        tt(fav, f1, T.clb[:], ALU.add, ["f1", "clb"], ["fav"])
+        mm(group([(P0[:, 16:32], ID, tk(1)), (P0[:, 16:32], ID, tk(2)), (P0[:, 16:32], I2, T.clb[:])], True, False),
+           ["m0", "m12", "tk1", "tk2", "clb"], ["P0"])
         tt(T.eq2[:], fav.indirect(su(4)), T.erow[:], ALU.is_equal, ["fav", "pu", "erow"], ["eq2"], "g")
-        mm(wrap(P0[:, 16:32], WBIG, T.eq2, 0, 256, True, True), ["eq2", "w1"], ["P0"])
-        tt(cm, P1[:, 0:16], nfb, ALU.add, ["P1", "nfb"], ["cm"])
-        ts(su(1), P1[:, 0:16], 2048.0, None, ALU.add, None, ["P1"], ["cu"])
-        tt(T.eq[:], cm.indirect(T.bcc[:]), T.crow[:], ALU.is_equal, ["cm", "bcc", "bcc1", "crow"], ["eq"], "g")
-        mm(wrap(P1[:, 32:56], WBIG, T.eq, 0, 384, True, True), ["eq", "w1"], ["P1"])
-        tt(t1, P0[:, 16:32], clb, ALU.min, ["P0", "clb"], ["t1_"])
-        tt(t1, t1, f0, ALU.add, ["t1_", "f0"], ["t1_"])
-        tt(T.so[:, 0:16], t1, T.dm[:], ALU.min, ["t1_", "dm"], ["soa"])
-        tt(fa, fa, K0, ALU.max, ["fa", "rk"], ["fa"])
-        cp(T.sn[:, 32 * t:32 * t + 16], T.so[:, 0:16], ["soa"], ["sn%d" % t])
-        if EMSEND:
-            send(t, T.ln[:, 32 * t:32 * t + 16], T.sn[:, 32 * t:32 * t + 16], "an%d" % t, ["sn%d" % t])
-            send(t, T.ln[:, 32 * t + 16:32 * t + 32], T.sn[:, 32 * t + 16:32 * t + 32], "ae%d" % t, ["sm%d" % t])
-        else:
-            send(t, T.ln[:, 32 * t:32 * t + 32], T.sn[:, 32 * t:32 * t + 32], "an%d" % t, ["sn%d" % t, "sm%d" % t])
-        if t == 0: later_constants()
-        gat(T.keepv[:], T.ot[:, 0:W].indirect(su(1)), ["O", "Oa", "cu", "keep%d" % (4 + b % 2), "keep%d" % (6 + b)], ["keepv"],
-            bias=T.cs[:, 6 + b:7 + b], scale=T.cs[:, 4 + b % 2:5 + b % 2])
-        gat(T.sb[:], T.oa[:].indirect(os_), OAK + ["off"], ["sb"])
-        mm([(P7[:, 0:272], ID, T.hc[:], True, False), (P7[:, 16:272], R3, T.sb[:], False, False)]
-           + wrap(P7[:, 0:16], WC, T.sb, 0, 256, False, True), ["sb", "w5", "m0", "m5", "hc", "hc0"], ["P7"])
-        gat(T.xs[:], T.xx[:].indirect(os_), XK + ["off"], ["xs"])
-        mm([(P6[:, 0:256], ID, T.qc[:], True, False), (P6[:, 0:256], ID, zc, False, False), (P6[:, 0:256], HID, T.xs[:], False, True)],
-           ["xs", zk, "qc", "m0", "m3"], ["P6"])
-        tt(tc, P1[:, 32:48], cm, ALU.add, ["P1", "cm"], ["tc"])
-        tco = T.sm[:, 16 * 3 + 1:16 * 4:2]; tce = T.sm[:, 16 * 3:16 * 4:2]
-        tt(tco, tco, P1[:, 48:56], ALU.add, ["P1", "tc"], ["tco"])
+        mm(group(wrap(P0[:, 16:32], W2, T.eq2, 0, 256), False, True), ["eq2", "w3"], ["P0"])
+        tt(so, P0[:, 16:32], f1, ALU.max, ["P0", "f1"], ["so"])
+        ts(T.sn[:, 48 * t:48 * t + 16], so, 4096.0, None, ALU.mult, None, ["so"], ["sn%d" % t])
+        send(t, T.ln[:, 32 * t:32 * t + 16], T.sn[:, 48 * t:48 * t + 16], "an%d" % t, ["sn%d" % t])
+        cp(cm, P1[:, 16:32], ["P1"], [ck])
+        ts(T.sn[:, 48 * t + 16:48 * t + 48], P1[:, 0:32], 2048.0, W - 1.0, ALU.add, ALU.min, ["P1"], ["sm%d" % t])
+        send(t, T.ln[:, 32 * t + 16:32 * t + 32], T.sn[:, 48 * t + 16:48 * t + 32], "ae%d" % t, ["sm%d" % t])
+        mm(group([(P2[:, 0:24], ID, T.tk[:, 64:88]), (P2[:, 0:16], ID, tk(6))], True, False), ["m0", "tk4", "tk5", "tk6"], ["P2"])
+        tt(T.eq[:], cm.indirect(T.bcc[:]), T.kq[:, 256:640], ALU.is_equal, [ck, "bcc", "bcc1", "kg", "kg2"], ["eq"], "g")
+        mm(group(wrap(P2[:, 0:24], WBIG, T.eq, 0, 384), False, True), ["eq", "w1"], ["P2"])
+        gat(T.keepv[:], T.ot[:, 0:W].indirect(T.sn[:, 48 * t + 32:48 * t + 48]), OT + ["sm%d" % t, "keep%d" % (4 + b % 2), "keep%d" % (6 + b)], ["keepv"],
+            bias=cs(6 + b), scale=cs(4 + b % 2))
+        tt(tc, P2[:, 0:16], cm, ALU.max, ["P2", ck], ["tc"])
+        tco = T.sm[:, 17:32:2]; tce = T.sm[:, 16:32:2]
+        tt(tco, tco, P2[:, 16:24], ALU.add, ["P2", "tc"], ["tco"])
         ts(T.oc[:, 0:16:2], tce, 2048.0, dcol, ALU.add, ALU.min, ["tc", "dcol"], ["oce"])
         ts(T.oc[:, 1:16:2], tco, 2048.0, dcol2, ALU.add, ALU.min, ["tco", "dcol2"], ["oco"])
-        act(T.ma[:], P7[:, 16:272], absf, ["P7"], ["ma"])
-        act(T.mm[:], T.ma[:], relu, ["ma"], ["mm"], bias=1.0, scale=-1.0)
-        act(T.ht[:], P6[:, 0:256], ident, ["P6"], ["ht"], bias=MAGIC)
-        act(T.wx[:, HCOL:HCOL + 256], T.ht[:], ident, ["ht"], ["H"], bias=-MAGIC)
-        fill = [
-            lambda: ts(su(3), fa, 16.0, rcol, ALU.mult, ALU.add, ["fa", "pc"], ["fo"]),
-            lambda: tt(sm(20, 2), T.rk[:, 0:2, :], sm(18, 2), ALU.add, ["rk", "hasp", "nhp"], ["k0p", "sn_"]),
-            lambda: tt(k0p, k0p, jj, ALU.min, ["k0p", "jj"], ["k0p"]),
-            lambda: tt(sm(22, 2), sm(20, 2), sm(16, 2), ALU.add, ["k0p", "sn_", "nfb", "fb"], ["rab"]),
-            lambda: tt(T.rowb[:], ra, rb, ALU.min, ["rab"], ["rowb"]),
-            lambda: tt(colf, P7[:, 0:16], K1, ALU.add, ["P7", "rk"], ["colf"]),
-            lambda: cp(su(2), colf, ["colf"], ["colu"]),
-        ]
+        act(tq, P6[:, 192:224], ident, ["P6"], ["tq"])
+        tt(fa, TD, T.rk[:, 0, :], ALU.max, ["P6", "rk"], ["fa"])
+        tt(ra, TC, sm(11), ALU.min, ["P6", "tq"], ["ra"])
+        tt(T.rowb[:], ra, sm(10), ALU.min, ["ra", "tq"], ["rowb"])
+        ts(su(3), fa, 16.0, rcol, ALU.mult, ALU.add, ["fa", "pc"], ["fo"])
+        gat(T.sb[:], T.oa[:].indirect(os_), OAK + ["off"], ["sb"])
+        if t == 0:
+            mm(group(wrap(P7[:, 0:16], WN, T.sb, 0, 256)), ["w4", "sb"], ["P7"])
+            cp(su(2), P7[:, 0:16], ["w4", "P7"], ["colu"])
+            gat(T.sb[:], T.ot[:, 0:W].indirect(su(2)), OT + ["colu"], ["sb"])
+        mm(group([(P7[:, 16:272], R3, T.sb[:])]) + group([(P7[:, 0:16], ID, T.kcn[:, 0:16]), (P7[:, 0:16], ID, T.rkb[:, 16:32])]
+                 + wrap(P7[:, 0:16], WC, T.sb, 0, 256)), ["sb", "w5", "m0", "m5", "kcn", "rkb"], ["P7"])
+        cp(su(2), P7[:, 0:16], ["P7"], ["colu"])
+        act(T.mm[:], P7[:, 16:272], relu, ["P7", "rsq"], ["mm"], bias=rsq, scale=-1.0)
+        gat(T.xs[:], T.xx[:, 0:3072].indirect(os_), XK + ["off"], ["xs"], bias=1535.75, scale=0.5)
+        mm(group([(P6[:, 0:256], ID, T.xx[:, zb:zb + 256]), (P6[:, 0:256], IDH, T.xs[:])]), ["xs", zk, "m0", "idh"], ["P6"])
+        act(T.xx[:, HCOL:HCOL + 256], P6[:, 0:256], ident, ["P6"], ["H"], bias=-1536.0)
         if t: list_bounds()
         vb = 256 * (b % 2)
         for m in range(7, -1, -1):
             tt(T.ot[:].indirect(T.oc[:, 2 * m:2 * m + 2]), T.keepv[:, 32 * m:32 * m + 32], T.vl[:, vb + 32 * m:vb + 32 * m + 32], ALU.add,
-               ["oce", "oco", "keepv", "vl0", "vl1"], ["O", "Oa"], "s")
-            if fill: fill.pop(0)()
+               ["oce", "oco", "keepv", "vl0", "vl1"], OT, "s")
         if t == RO - 1:
+            step[0] = RO
             arrive(t)
-            dma("y", [(T.ym[:], T.mt[:, 0:W])], ["M"], [], 3.5)
+            dma("y", [(T.ym[:], T.mt[:, 0:W])], ["M"], [], 4.9)
         if t < 4:
-            gat(T.wx[:, Z1 + lo:Z1 + lo + 256], T.wx[:, 0:Z1].indirect(su(3)), AK + ["H", "fo", "Z0"], ["Z1_%d" % b])
-            dma("y", [(T.zt[:, 1024 * b + 256 * j:1024 * b + 256 * j + 256], T.wx[:, Z1 + lo:Z1 + lo + 256]) for j in range(4)],
+            gat(T.xx[:, Z1 + lo:Z1 + lo + 256], T.xx[:, 0:Z1].indirect(su(3)), XK + ["H", "fo", "Z0"], ["Z1_%d" % b], f=absf)
+            dma("y", [(T.zt[:, 1024 * b + 256 * j:1024 * b + 256 * j + 256], T.xx[:, Z1 + lo:Z1 + lo + 256]) for j in range(4)],
                 ["Z1_%d" % b], ["zt%d" % b])
         else:
-            gat(T.zo[:, lo:lo + 256], T.wx[:].indirect(su(3)), AK + ["H", "fo", zk], ["zo%d" % b])
+            gat(T.zo[:, lo:lo + 256], T.xx[:].indirect(su(3)), XK + ["H", "fo", zk], ["zo%d" % b], f=absf)
             dma("y", [(T.yz[:, lo:lo + 256], T.zo[:, lo:lo + 256])], ["zo%d" % b], [])
-        if t == RO - 2: dma("y", [(T.yo[0:8, :], T.ot[0::16, 0:W])], ["O", "Oa"], [])
-        if t == RO - 1: dma("y", [(T.yo[8:16, :], T.ot[1::16, 0:W])], ["O", "Oa"], [])
-        if t == RO - 1:
-            act(T.tho[:], T.thb[:], ident, ["th0", "th1", "th2", "th3"], ["tho"], scale=1.0 / 256)
-            add("p", lambda: P.transpose(P3[0:64, 0:128], T.tho[:], T.idf[:]), ["tho", "idf"], ["P3"], 0.3)
-            arrive_em(t)
-            act(T.tf[0:64, :], P3[0:64, 0:128], ident, ["P3"], ["tf"])
-            dma("s", [(T.yt[q, :], T.tf[0:64, 16 * q:16 * q + 16]) for q in range(8)], ["tf"], [])
-            for _ in list_update(t - 1): pass
-            list_out(t - 1)
-            hints(t); hints_p()
-            arrive_k(t)
-            dma("y", [(T.yk[:], T.kt[2::16, 0:W])], ["K"], [])
-        if t + 1 < RO: owners(t + 1, OGV)
-    list_mask(); hints_b(); list_bounds()
-    for _ in list_update(RO - 1): pass
-    list_out(RO - 1)
+        if t >= RO - 2: dma("y", [(T.yo[8 * (t % 2):8 * (t % 2) + 8, :], T.ot[t % 2::16, 0:W])], OT, [])
+        if t + 1 < RO: owners(t + 1)
+    mm(group([(P3[0:64, 0:128], T.thh[:, 0:64], ID), (P3[0:64, 0:128], T.thh[:, 64:128], ID),
+              (P3[0:64, 0:128], T.nfs[:, 0:64], I128), (P3[0:64, 0:128], T.nfs[:, 64:128], I128)]),
+       ["thh", "thl", "m0", "m11"] + ["nf%d" % i for i in range(RO)], ["P3"])
+    arrive_em(RO - 1)
+    act(T.tf[0:64, :], P3[0:64, 0:128], ident, ["P3"], ["tf"])
+    dma("s", [(T.yt[q, :], T.tf[0:64, 16 * q:16 * q + 16]) for q in range(8)], ["tf"], [])
+    list_update(RO - 2)
+    hints(RO - 1); hints_p(RO - 1)
+    arrive_k(RO - 1)
+    dma("y", [(T.yk[:], T.kt[0::16, 0:W])], KT, [])
+    list_mask(); hints_b(RO - 1); list_bounds()
+    list_update(RO - 1)
 
     queue = {"v": V, "s": S, "p": P, "g": g, "y": g.sync}
     csem = {"v": "cv", "s": "cs", "p": "cp", "g": "cg"}
+    named = {}
+    for n, o in enumerate(ops): named.setdefault((o["e"], o["step"], o["lab"]), []).append(n)
+    for e, names in CHAIN.items():
+        row = []
+        for t in range(RO):
+            for x in names.split():
+                x, _, k = x.partition("#"); calls = named.get((e, t + x.count("+"), x.rstrip("+")), [])
+                k = int(k) if k else len(calls)
+                row += calls[:k]; del calls[:k]
+        for a, b in zip(row, row[1:]): ops[b]["soft"].add(a)
     succ = [[] for _ in ops]
     for n, o in enumerate(ops):
         o["all"] = [(x, ops[x]["lat"] + WAKE) for x in o["d"]] + [(x, 0.0) for x in o["soft"]] + [(x, REM) for x in o["far"]]
         for x, l in o["all"]: succ[x].append((n, l))
+    left = [len(o["all"]) for o in ops]; forward = [n for n, k in enumerate(left) if not k]
+    for n in forward:
+        for y, l in succ[n]:
+            left[y] -= 1
+            if not left[y]: forward.append(y)
     tail = [0.0] * len(ops)
-    for n in range(len(ops) - 1, -1, -1):
+    for n in reversed(forward):
         tail[n] = ops[n]["c"] + max([l + tail[y] for y, l in succ[n]] + [ops[n]["lat"]])
     busy = {e: [] for e in queue}; begin = [0.0] * len(ops)
-    for n in sorted(range(len(ops)), key=lambda x: (-tail[x], x)):
+    for n in sorted(forward, key=lambda x: (-tail[x], x)):
         o = ops[n]; t0 = max([begin[x] + ops[x]["c"] + l for x, l in o["all"]] + [0.0]); row = busy[o["e"]]; i = 0
         while i < len(row) and row[i][0] < t0 + o["c"] - SLACK:
             t0 = max(t0, row[i][1]); i += 1

from concourse.mybir import AluOpType as ALU, ActivationFunctionType as AF

W, RO, NR = 3840, 8, 8
B = 1 << 21
BIG = 32768.0
MAGIC = 12582912.0
CYC, FIX, GATHER, SCATTER, WAKE, REM, SLACK, DMAF = 0.85e-3, 0.01, 1.3, 3.0, 0.21, 2.3, 0.03, 0.45
CH = ((0, 4), (4, 8), (8, 10), (10, 12))
BC = ((0, 2), (2, 4), (4, 8), (8, 12))
FILLG = 3
AFFV = ("pq", "ph0", "ph1")
CHAIN = {
    "v": "X0<M X4<M ee<P1 X8<M X10<M d2<d0 ka0<P0 ka1<P0 ka2<P0 hs<E t0a<ka0 kb2<P3 kb1<P3 kb0<P3 t1a<t0a t0b<kb0 t3a<t1a t3b<t0b eo<E "
         "rr<t3a rk<rr nf<rr off<rk Kf0<emr new<P7 efu<P3 efo<P3 f1<P3 rkb<rk clb<P0 pu1<P0 fav<f1 pu<pu1 eq2<fav cm<P1 sm<P1 eq<cm "
         "so<P0 sn<so tc<P2 fa<P6 tco<P2 oce<tc oco<tco ra<P6 O<oce#1 fo<fa O<oce#1 colu<P7 rowb<ra O<oce#2 ld<P4+#1 O<oce#1 E<ld+#1 "
         "O<oce OA0<O M<+",
    "s": "A0<X0 A4<X4 d0<P5 A8<X8 A10<X10 emr<nt0 la<P4 lead<P6 nbf<OA0 sz<X0 nbm<OA0 kg<Kf0 erow<P5 kg2<Kf0 xs<X0 tq<P6 "
         "sb<OA0 keepv<O H<P6 Z1_<X0 zo<X0 mm<P7 OA2<O OA4<O OA8<O",
    "p": "P0<A0 P5<ee P0<A4 P3<A8 P6<d0 P0<m0#1 P2<m0 P6<lead P7<hs P3<nbf P0<nbf P5<nbf P1<kg P0<m0 P6<nf P0<eq2 P2<eq P5<thh+ "
         "P1<m0 P7<sb P4<la#1 P6<xs P4<la P0<m1+ P3<m1+ P4<rowb+ P1<OA0 P1<OA2 P1<OA4 P1<OA8",
    "y": "oi< ei0< zq< M< ki< Oa<s0 Or<s5 Kf1<s2 ti< Z0< ei1< Kf0<Kf1 O<s6",
    "g": "ip< x240< i143< lh0< bo0< kcn< Of12<",
}

F, BF, HF, I, U = "float32", "bfloat16", "float16", "int32", "uint16"
SCRATCH = {name: ("sbuf", [128] + list(cols), kind) for kind, bufs in (
    (F, dict(ot=[3872], kt=[4096], nt=[W], ec=[768], eout=[768], stg=[2400], tf=[128], pc=[16], cs=[16], pw=[64], mk=[16], mk2=[8],
             i143=[144], b128=[128], x240=[256], h256=[256], r256=[256], lc0=[16], lh0=[384], bo0=[4], d20=[16], bc0=[8], idf=[128],
             dm=[16], vl=[512], vt=[256], vq=[16], d2=[192], kb=[3, 192], t1=[3, 96], t2=[3, 32], t3=[3, 32],
             erow=[256], keepv=[256], emr=[256], sm=[256], ld=[192])),
    (BF, dict(mt=[4096], xx=[5376], wx=[3072], oa=[3072], zt=[4096], zo=[1024], hb=[240], thh=[128], nfs=[128], rkb=[32], clb=[16],
              tk=[112], tk0=[128], ww=[8 * 144], wm=[15 * 128], lanec=[16], lanh=[384], kc2=[192], kcn=[192],
              ee=[384], d0=[192], lead=[192], la=[192], nf_=[256], sb=[256], mm=[256], r3=[256], eq=[384], eq2=[256], rowb=[16],
              sz=[RO * 256], lz=[RO * 256])),
    (HF, dict(wh=[288], idh=[128], kq=[640], xs=[256], hs=[256], newh=[16])),
    (I, dict(ei=[768], oi=[720], sti=[720], ti=[128], ip=[8], rr=[3, 16], rk=[3, 16])),
    (U, dict(eo=[768], bcc=[24], off=[48], su=[80], oc=[16], sn=[RO * 48], ln=[RO * 32])),
) for name, cols in bufs.items()}
for _i in range(8):
    SCRATCH["p%d" % _i] = ("psum", [128, 512], F)
DSEMS = ["d%d" % i for i in range(48)]
SEMAPHORES = ["cv", "cs", "cp", "cg", "sent"] + DSEMS + [x + str(t) for x in ("az", "an", "ae") for t in range(RO)]


def label(s):
    bare = lambda k: k.rstrip("0123456789")
    return "<".join(bare(k) if bare(k) in ("sz", "sn", "sm", "nf", "E", "eo", "zt", "cm", "Z1_", "zo", "eout") else k for k in s.split("<"))


def rank_program(g, core, T, topo):
    rank = T.rank_of(core)
    if rank is None:
        return
    ops, lastw, readers, nd, own_send, step = [], {}, {}, [0], {}, [0]

    def width(a):
        n = 1
        for x in a.shape[1:]: n *= x
        return n

    def cost(a, per, kind):
        if kind == "h": per = 0.5
        elif kind: return 0.06 + width(a) * (GATHER if kind == "g" else SCATTER) * CYC
        return FIX + max(64, width(a) * per) * CYC

    def deps(e, R, Wr):
        d, soft = set(), set()
        for k in R:
            if k in lastw: d.add(lastw[k])
            if k[0] == "P": d.update(x for x in readers.get(k, ()) if ops[x]["e"] != e)
        for k in Wr:
            for x in ([lastw[k]] if k in lastw else []) + readers.get(k, []):
                (d if e != "p" or ops[x]["e"] != e else soft).add(x)
        return d, soft

    def add(e, fn, R, Wr, c, tok=None, ext=None, lat=0.0):
        d, soft = deps(e, R, Wr)
        ops.append({"e": e, "fn": fn, "d": d, "soft": soft, "tok": tok, "ext": ext, "c": c, "lat": lat, "step": step[0],
                    "lab": label((Wr + [""])[0] + "<" + (R + [""])[0]), "far": [own_send[x[0]] for x in ext or ()]})
        n = len(ops) - 1
        for k in R: readers.setdefault(k, []).append(n)
        for k in Wr:
            lastw[k] = n; readers[k] = []
        return n

    def dma(e, pairs, R, Wr, each=0.6):
        name = DSEMS[nd[0]]; nd[0] += 1
        q = g.sync if e == "y" else g.scalar
        def fn():
            for o, i in pairs: q.dma_start(o, i).then_inc(T.sem[name], 16)
        return add(e, fn, R, Wr, len(pairs) * (each * DMAF if e == "y" else 0.06), tok=(name, 16 * len(pairs)), lat=2.0)

    V, S, P = g.vector, g.scalar, g.tensor
    ident, absf, relu = AF.Identity, AF.Abs, AF.Relu
    def ts(o, i, a, b, o0, o1, R, Wr, k=None):
        add("v", (lambda: V.tensor_scalar(o, i, a, None, o0)) if o1 is None else (lambda: V.tensor_scalar(o, i, a, b, o0, o1)), R, Wr, cost(o, 1, k))
    def tt(o, a, b, op, R, Wr, k=None):
        add("v", lambda: V.tensor_tensor(o, a, b, op), R, Wr, cost(b, 1 if any(x[0] == "P" for x in R) else 2, k))
    def cp(o, i, R, Wr, ext=None, k=None): add("v", lambda: V.tensor_copy(o, i), R, Wr, cost(i, 1, k), ext=ext)
    def act(o, i, f, R, Wr, bias=0.0, scale=1.0, ext=None, k=None):
        add("s", lambda: S.activation(o, i, f, bias=bias, scale=scale), R, Wr, cost(o, 1, k), ext=ext)
    def const(o, c, Wr): act(o, T.x240[:, 0:width(o)], ident, ["x240"], Wr, bias=c, scale=0.0)
    def aff(o, i, scale, bias, R, Wr):
        if Wr[0] in AFFV: ts(o, i, scale, bias, ALU.mult, ALU.add, R, Wr)
        else: act(o, i, ident, R, Wr, bias, scale)
    def gat(o, i, R, Wr, bias=0.0, scale=1.0, ext=None, f=ident): act(o, i, f, R, Wr, bias, scale, ext, "g")
    def iota(o, pat, base, cm, Wr, isint=False):
        add("g", (lambda: g.iota(o, pat, base, cm)) if isint else (lambda: g.iota(o, pat, base, cm, allow_small_or_imprecise_dtypes=True)), [], Wr,
            0.13 + 2 * width(o) * CYC)
    def mm(lst, R, Wr):
        def fn():
            for x in lst: last = P.matmul(*x)
            return last
        add("p", fn, R, Wr, sum(max(64, width(x[2])) for x in lst) * CYC / 2, lat=0.1)
    def group(lst, start=True, stop=True):
        return [x + (start and n == 0, stop and n == len(lst) - 1) for n, x in enumerate(lst)]
    def wrap(out, w, src, lo, hi):
        return [(out, w(r), src[:, lo + r:hi:16]) for r in range(16)]
    def wset(i): return lambda r: T.ww[:, 144 * i + 15 - r:144 * i + 143 - r]
    WD, WBIG, WQ, W2, WN, WC, WP, WNS = [wset(i) for i in range(8)]
    WH = lambda r: T.wh[:, 15 - r:143 - r]
    WH16 = lambda r: T.wh[:, 159 - r:287 - r]
    ID, NID, IB, H0, RN, R3, I16, I16R, I256, IBIG, NBIG, I128, I2, H1 = [T.wm[:, 128 * i:128 * i + 128] for i in range(14)]
    IDH = T.idh[:]
    pcol, rcol, p16, r2, p7, r240, dcol, dcol2, rsq, pq, ph0, ph1, rs0 = [T.pc[:, i:i + 1] for i in range(13)]
    mk = lambda f: T.mk[:, f:f + 1]
    mk2 = lambda f: T.mk2[:, f:f + 1]
    cs = lambda f: T.cs[:, f:f + 1]
    sm = lambda i, n=1: T.sm[:, 16 * i:16 * (i + n)]
    su = lambda i: T.su[:, 16 * i:16 * i + 16]
    st = lambda a, b: T.stg[:, 240 * a:240 * b]
    tk = lambda i: T.tk[:, 16 * i:16 * i + 16]
    P0, P1, P2, P3, P4, P5, P6, P7 = [T["p%d" % i] for i in range(8)]
    HCOL, Z0, Z1 = 3072, 3328, 4352
    AK = ["A%d" % k for k in range(12)]; XK = ["X%d" % k for k in range(12)]; OAK = ["OA%d" % k for k in range(12)]
    EK = ["E%d" % b for b in range(4)]; OF = ["Of%d" % j for j in range(15)]; OT = ["O", "Oa", "Or"]; KT = ["Kf0", "Kf1"]

    dma("y", [(T.oi[:, 0:240], T.own[0:8, :]), (T.oi[:, 240:480], T.own[8:16, :])], [], ["oi"], 0.8)
    dma("y", [(T.ei[:, 0:192], T.ends[:, 0:192])], [], ["ei0"])
    dma("y", [(T.zt[:, 0:256], T.st[:, 0:256])], [], ["zq"])
    dma("y", [(T.mt[:, 0:W], T.msg[:])], [], ["M"], 4.9)
    dma("y", [(T.oi[:, 480:720], T.enc[:])], [], ["ki"], 0.8)
    dma("y", [(T.ti[0:64, 16 * q:16 * q + 16], T.th[q, :]) for q in range(8)], [], ["ti"], 0.1)
    dma("y", [(T.xx[:, Z0:Z0 + 1024], T.st[:])], [], ["Z0"], 1.4)
    dma("y", [(T.ei[:, 192:768], T.ends[:, 192:768])], [], ["ei1"], 1.55)
    cp(T.zt[:, 256:512], T.zt[:, 0:256], ["zq"], ["zq1"], k="h")
    cp(T.zt[:, 512:1024], T.zt[:, 0:512], ["zq", "zq1"], ["zt0"], k="h")
    iota(T.ip[:, 0:1], [[0, 1]], 0, 1, ["ip"], True)
    for o, pat, base, key in (
            (T.x240[:], [[1, 256]], 0, "x240"), (T.i143[:], [[1, 144]], -15, "i143"), (T.bo0[:], [[-256, 4]], -128, "bo0"),
            (T.lc0[:], [[-16, 16]], 128, "lc0"), (T.lh0[:], [[0, 12], [-8, 32]], 128, "lh0"), (T.kcn[:], [[-1, 192]], 0, "kcn"),
            (T.kc2[:], [[2, 192]], 0, "kc2"), (T.b128[:], [[16, 8], [0, 16]], 0, "b128"),
            (T.d20[:], [[16, 16]], W, "d20"), (T.r256[:], [[0, 16], [1, 16]], 0, "r256"), (T.h256[:], [[1, 16], [0, 16]], 0, "h256"),
            (T.bc0[:], [[2, 8]], 0, "bc0"), (T.tk0[:, 0:16], [[1, 16]], 0, "tq0"), (T.tk0[:, 48:64], [[1, 16]], 192, "tq1")):
        iota(o, pat, base, 0, [key])
    ts(T.ip[:, 1:2], T.ip[:, 0:1], 15, None, ALU.bitwise_and, None, ["ip"], ["ip1"])
    ts(T.ip[:, 2:3], T.ip[:, 0:1], 112, None, ALU.bitwise_and, None, ["ip"], ["ip2"])
    ts(T.ip[:, 3:4], T.ip[:, 0:1], 1, 7, ALU.arith_shift_right, ALU.bitwise_and, ["ip"], ["ip3"])
    ts(T.ip[:, 4:5], T.ip[:, 0:1], 7, None, ALU.bitwise_and, None, ["ip"], ["ip4"])
    cp(T.pc[:, 0:5], T.ip[:, 0:5], ["ip", "ip1", "ip2", "ip3", "ip4"], ["pc"])
    for j in range(15 - FILLG):
        aff(T.ot[:, 256 * j:256 * j + 256], T.x240[:], 1.0, 256.0 * j, ["x240"], [OF[j]])
    iota(T.ot[:, W - 256 * FILLG:W], [[1, 256 * FILLG]], W - 256 * FILLG, 0, OF[15 - FILLG:])
    ts(r240, rcol, 240.0, None, ALU.mult, None, ["pc"], ["r240"])
    ts(st(3, 4), T.x240[:, 0:240], r240, None, ALU.add, None, ["x240", "r240"], ["s3"])
    ts(T.mk[:], T.x240[:, 0:16], rcol, None, ALU.is_equal, None, ["x240", "pc"], ["mk"])
    cp(T.hb[:], st(3, 4), ["s3"], ["hb1"])
    ts(T.mk2[:, 0:4], T.x240[:, 0:4], r2, None, ALU.is_equal, None, ["x240", "pc"], ["mk2"])
    tt(st(5, 6), st(3, 4), T.hb[:], ALU.subtract, ["s3", "hb1"], ["s5"])
    dma("y", [(T.ot[3::16, 0:W], st(5, 6))], ["s5"] + OF, ["Or"], 0.75)
    cp(st(0, 2), T.oi[:, 0:480], ["oi"], ["s0"])
    ts(T.sti[:, 0:240], T.oi[:, 0:240], 8, None, ALU.arith_shift_right, None, ["oi"], ["sti0"])
    ts(T.sti[:, 240:480], T.oi[:, 0:240], 4, 15, ALU.arith_shift_right, ALU.bitwise_and, ["oi"], ["sti1"])
    ts(T.sti[:, 480:720], T.oi[:, 0:240], 15, None, ALU.bitwise_and, None, ["oi"], ["sti2"])
    dma("y", [(T.ot[f::16, 0:W], st(f, f + 1)) for f in (0, 1)], ["s0"] + OF, ["Oa"], 0.75)
    ts(st(6, 7), T.sti[:, 0:240], 192.0, None, ALU.mult, None, ["sti0"], ["s6"])
    cp(st(7, 9), T.sti[:, 240:720], ["sti1", "sti2"], ["s7"])
    act(st(9, 10), st(8, 9), AF.Square, ["s7"], ["s9"])
    cp(T.eo[:, 0:192], T.ei[:, 0:192], ["ei0"], ["eo0"])
    ts(T.cs[:, 0:4], T.bo0[:], mk2(0), None, ALU.mult, None, ["bo0", "mk2"], ["bo"])
    def scaled(i, j, w, R=()):
        aff(T.ww[:, 144 * i:144 * i + 144], T.ww[:, 144 * j:144 * j + 144], w, 0.0, ["w%d" % j] + list(R), ["w%d" % i])
    ts(T.ww[:, 0:144], T.i143[:], p16, 256.0, ALU.is_equal, ALU.mult, ["i143", "pc"], ["w0"])
    ts(T.lanh[:], T.lh0[:], p7, None, ALU.subtract, None, ["lh0", "pc"], ["lanh"])
    aff(pq, rcol, 8.0, p16, ["pc"], ["pq"])
    ts(T.ww[:, 288:432], T.i143[:], pq, mk2(0), ALU.is_equal, ALU.mult, ["i143", "pq", "mk2"], ["w2"])
    aff(ph0, p7, 1.0, p16, ["pc"], ["ph0"])
    aff(ph1, ph0, 1.0, 8.0, ["ph0"], ["ph1"])
    ts(H0, T.x240[:, 0:128], ph0, None, ALU.is_equal, None, ["x240", "ph0"], ["m3"])
    ts(H1, T.x240[:, 0:128], ph1, None, ALU.is_equal, None, ["x240", "ph1"], ["m13"])
    ts(ID, T.x240[:, 0:128], pcol, None, ALU.is_equal, None, ["x240", "pc"], ["m0"])
    ts(T.lanec[:], T.lc0[:], rcol, None, ALU.subtract, None, ["lc0", "pc"], ["lanec"])
    for i, w in ((1, -1.0), (2, 1.0 / B), (6, 16.0), (7, 1.0 / 16), (8, 256.0), (9, BIG), (10, -BIG), (11, 128.0), (12, 2.0)):
        aff(T.wm[:, 128 * i:128 * i + 128], ID, w, 0.0, ["m0"], ["m%d" % i])
    for o, key in ((T.idf[:], "idf"), (IDH, "idh")): aff(o, ID, 1.0, 0.0, ["m0"], [key])
    mm(group([(P5[:, 272:464], ID, T.kc2[:])]), ["kc2", "m0"], ["P5"])
    aff(cs(12), mk2(0), 1.0 / 4096, 0.0, ["mk2"], ["wp"])
    aff(T.mk2[:, 4:8], T.mk2[:, 0:4], 1.0 / 256, 0.0, ["mk2"], ["mkq"])
    scaled(4, 0, mk2(5), ["mkq"]); scaled(6, 0, cs(12), ["wp"]); scaled(5, 0, mk2(6), ["mkq"])
    scaled(7, 4, 1.0 / 4096); scaled(3, 0, 1.0 / 128)

    def late_constants():
        cp(st(2, 3), T.oi[:, 480:720], ["ki"], ["s2"])
        dma("y", [(T.kt[0::16, 0:W], st(2, 3))], ["s2"], ["Kf1"], 0.75)
        dma("y", [(T.kt[f::16, 0:W], T.kt[0::16, 0:W]) for f in range(1, 16)], ["Kf1"], ["Kf0"], 0.55)
        for j in range(4): iota(T.nt[:, 960 * j:960 * j + 960], [[1, 960]], 960 * j, 0, ["nt%d" % j])
        ts(T.pw[:, 0:16], T.x240[:, 0:16], rcol, -0.5, ALU.is_lt, ALU.mult, ["x240", "pc"], ["pw0"])
        ts(T.pw[:, 0:16], T.pw[:, 0:16], 1.0, None, ALU.add, None, ["pw0"], ["pw0"])
        const(T.pw[:, 16:32], 0.0, ["pw1"])
        add("v", lambda: V.tensor_tensor_scan(T.pw[:, 32:48], T.pw[:, 0:16], T.pw[:, 16:32], float(1 << 19), ALU.mult, ALU.add), ["pw0", "pw1"], ["pw2"], 0.1)
        scaled(1, 0, T.pw[:, 47:48], ["pw2"])
        for b in range(1, 4):
            dma("y", [(T.zt[:, 1024 * b + 256 * j:1024 * b + 256 * j + 256], T.st[:, 256 * b:256 * b + 256]) for j in range(4)], [], ["zt%d" % b], 0.5)
        cp(T.thh[:, 0:64], P7[:, 0:64], ["P7"], ["thh"])
        tt(T.thh[:, 64:128], P7[:, 0:64], T.thh[:, 0:64], ALU.subtract, ["P7", "thh"], ["thl"])
        aff(T.vq[:], T.lanec[:], -1.0 / 16, 7.53125, ["lanec"], ["vq"])
        ts(T.dm[:], T.d20[:], rcol, 1.0 / 4096, ALU.add, ALU.mult, ["d20", "pc"], ["dm"])
        aff(dcol, rcol, 1.0, float(W), ["pc"], ["dcol"])
        aff(dcol2, rcol, 1.0, float(W + 16), ["pc"], ["dcol2"])
        aff(rs0, rcol, rcol, 0.0, ["pc"], ["rsq0"])
        aff(rsq, rs0, -1.0, 1.0, ["rsq0"], ["rsq"])
        for i, c in ((0, 7.53125), (2, -3.0625), (3, 1.0), (5, 0.0), (6, 2048.0)): const(tk(i), c, ["tk%d" % i])
        aff(tk(1), T.dm[:], 1.0, -W / 4096.0, ["dm"], ["tk1"])
        ts(tk(4), T.pw[:, 16:32], T.pw[:, 47:48], -512.0, ALU.add, ALU.mult, ["pw1", "pw2"], ["tk4"])
        aff(cs(14), mk2(1), 16.0, 0.0, ["mk2"], ["cs14"])
        aff(cs(15), mk(2), -BIG, 0.0, ["mk"], ["cs15"])
        for i, (a, e, c) in enumerate(((16, 48, 0.0), (64, 80, 0.0), (80, 112, 1.0), (112, 128, -1.0))): const(T.tk0[:, a:e], c, ["tq%d" % (i + 2)])
        ts(T.r3[:, 0:128], T.b128[:], p16, None, ALU.is_equal, None, ["b128", "pc"], ["r3a"])
        aff(RN, T.r3[:, 0:128], mk2(1), 0.0, ["r3a", "mk2"], ["m4"])
        aff(cs(13), mk(6), -2.0, 0.0, ["mk"], ["cs13"])
        aff(T.r3[:, 128:256], T.r256[:, 0:128], cs(13), mk(7), ["r256", "cs13", "mk"], ["r3b"])
        tt(R3, T.r3[:, 0:128], T.r3[:, 128:256], ALU.mult, ["r3a", "r3b"], ["m5"])
        act(T.wh[:, 0:144], T.ww[:, 0:144], ident, ["w0"], ["wh"], scale=1.0 / 256)
        act(T.wh[:, 144:288], T.ww[:, 0:144], ident, ["w0"], ["wh16"], scale=1.0 / 4096)
        cp(T.bcc[:, 0:16], T.x240[:, 0:16], ["x240"], ["bcc"])
        cp(T.bcc[:, 16:24], T.bc0[:], ["bc0"], ["bcc1"])
        act(T.vl[:, 0:256], T.x240[:], ident, ["x240", "mk"], ["vl0"], scale=mk(0))
        act(T.vl[:, 256:512], T.x240[:], ident, ["x240", "mk"], ["vl1"], scale=mk(1))
        act(T.vt[:], T.r256[:], AF.Square, ["r256"], ["vt"])
        dma("y", [(T.vl[f::16, 0:256], x[f::16, :]) for f, x in ((5, T.h256), (6, T.r256), (7, T.vt))], ["h256", "r256", "vt"], ["vl0"], 0.06)
        ts(cs(10), mk(0), mk2(2), mk2(3), ALU.add, ALU.add, ["mk", "mk2"], ["cs10"])
        aff(cs(4), cs(10), -1.0, 1.0, ["cs10"], ["keep4"])
        aff(cs(5), mk(1), -1.0, 1.0, ["mk"], ["keep5"])
        const(cs(6), 0.0, ["keep6"])
        aff(cs(7), mk(1), 256.0, 0.0, ["mk"], ["keep7"])
        aff(cs(11), mk(4), 384.0, 0.0, ["mk"], ["cs11"])
        aff(cs(8), mk(0), 512.0, cs(11), ["mk", "cs11"], ["keep8"])
        aff(cs(9), mk(1), 768.0, 0.0, ["mk"], ["keep9"])

    def owners(t):
        b = t % 4
        mm(group([(P1[:, 0:384], ID, T.lanh[:])], True, False), ["m0", "lanh"], ["P1"])
        for a, e in BC:
            o, i = T.oa[:, 256 * a:256 * e], T.ot[:, 0:W].indirect(T.eo[:, 192 * b + 16 * a:192 * b + 16 * e])
            R = OT + ["eo%d" % b, "bo"]
            if a == 0: ts(o, i, cs(b), None, ALU.add, None, R, OAK[a:e], "g")
            else: gat(o, i, R, OAK[a:e], bias=cs(b))
            mm(group([(P1[:, 32 * a:32 * e], WQ(r), T.oa[:, 256 * a + r:256 * e:8]) for r in range(8)], False, e == 12), OAK[a:e] + ["w2"], ["P1"])

    def live():
        ts(T.ee[:], P1[:, 0:384], 0.0, None, ALU.is_equal, None, ["P1"], ["ee"])
        mm(group([(P5[:, 0:192], H0, T.ee[:, 0:384:2]), (P5[:, 0:192], H1, T.ee[:, 1:384:2])]), ["ee", "m3", "m13"], ["P5"])
        act(T.d0[:], P5[:, 0:192], relu, ["P5"], ["d0"], bias=float(B), scale=-float(B))
        tt(T.d2[:], T.d0[:], P5[:, 272:464], ALU.add, ["d0", "P5"], ["d2"])

    def threshold(t):
        b = t % 4; o = P5[:, 464:480]
        mm(group([(o, I256, T.thh[:, 16 * b:16 * b + 16]), (o, I256, T.thh[:, 64 + 16 * b:80 + 16 * b])]
                 + ([(o, IBIG, nfs(t - 4))] if t > 3 else [])), ["thh", "thl", "m8", "m9"] + (["nf%d" % (t - 4)] if t > 3 else []), ["P5"])

    dst = [T.cores[(rank + 1 + t % (NR - 1)) % NR] for t in range(RO)]
    src = [T.cores[(rank - 1 - t % (NR - 1)) % NR] for t in range(RO)]
    cnt_in = [len(topo.engines(s, core)) for s in src]
    sent = [0]

    def send(t, o, i, sem, R):
        rid, pid, _ = topo.addr(dst[t]); m = topo.mask(core, dst[t])
        sent[0] += len(topo.engines(core, dst[t]))
        own_send[sem] = add("g", lambda: g.remote_dma(o, i, T.sem[sem], T.sem.sent, pid, rid, m), R, [], 1.0, tok=("sent", 0))

    def arrive(t):
        cp(T.mt[:].indirect(T.ln[:, 32 * t:32 * t + 16]), T.lz[:, 256 * t:256 * t + 256], [], ["M"],
           ext=[("az%d" % t, cnt_in[t]), ("an%d" % t, cnt_in[t])], k="s")

    def arrive_em(t):
        gat(T.emr[:], T.nt[:].indirect(T.ln[:, 32 * t + 16:32 * t + 32]), ["nt%d" % j for j in range(4)], ["emr"], ext=[("ae%d" % t, cnt_in[t])])

    def arrive_k(t):
        cp(T.kt[:].indirect(T.ln[:, 32 * t:32 * t + 16]), T.emr[:], ["emr"], KT, ext=[("an%d" % t, cnt_in[t])], k="s")

    tc, fa, f1, fav, pu1, so, ra = [sm(i) for i in range(1, 8)]
    tq = sm(10, 2)
    cms = lambda t: sm(12 + t % 2)
    nfs = lambda t: T.nfs[:, 16 * t:16 * t + 16]

    def list_mask():
        act(T.la[:], P4[:, 0:192], absf, ["P4"], ["la"], scale=8192.0)

    def hints(t):
        tt(T.hs[:], T.ec[:].indirect(su(2)), T.mm[:], ALU.mult, EK + ["colu", "mm"], ["hs"], "g")

    def hints_p(t):
        mm(group([(P4[:, 0:192], ID, T.kcn[:])] + [(P4[:, 16 * k:16 * k + 16], ID, T.rowb[:]) for k in range(12)]), ["rowb", "m0", "kcn"], ["P4"])
        mm(group([(P7[:, 0:16], IBIG, tk(3)), (P7[:, 0:16], NBIG, nfs(t))] + wrap(P7[:, 0:16], WH, T.hs, 0, 256)),
           ["hs", "wh", "tk3", "nf%d" % t, "m9", "m10"], ["P7"])

    def hints_b(t):
        tt(T.newh[:], P7[:, 0:16], cms(t), ALU.min, ["P7", "cm%d" % (t % 2)], ["new"])

    def list_bounds():
        for o, w in ((0, ID), (192, NID)):
            mm(group([(P4[:, o:o + 192], w, T.la[:])] + [(P4[:, o + 16 * k:o + 16 * k + 16], IDH, T.newh[:]) for k in range(12)]),
               ["la", "new", "m0", "m1", "idh"], ["P4"])

    def list_update(t):
        b = t % 4; eb = T.ec[:, 192 * b:192 * b + 192]
        tt(T.ld[:], eb, P4[:, 0:192], ALU.min, ["P4", EK[b]], ["ld"])
        tt(eb, T.ld[:], P4[:, 192:384], ALU.max, ["ld", "P4"], [EK[b]])
        if t < 4:
            ts(T.eo[:, 192 * b:192 * b + 192], eb, 2048.0, None, ALU.add, None, [EK[b]], ["eo%d" % b])
        else:
            act(T.eout[:, 192 * b:192 * b + 192], eb, ident, [EK[b]], ["eout%d" % b], bias=2048.0)
            dma("y", [(T.ye[:, 192 * b:192 * b + 192], T.eout[:, 192 * b:192 * b + 192])], ["eout%d" % b], [])

    for t in range(RO):
        b = t % 4; lo = 256 * b; step[0] = t
        zb = (Z0 if t < 4 else Z1) + lo; zk = "Z0" if t < 4 else "Z1_%d" % b
        if t:
            arrive(t - 1); threshold(t)
        else:
            step[0] = -1; owners(0); step[0] = 0
            dma("y", [(T.ot[f::16, 0:W], st(f + 2, f + 3)) for f in (4, 5, 6, 7)], ["s6", "s7", "s9"] + OF, ["O"], 0.75)
        live()
        mm(group([(P0[:, 0:128], NID, T.kcn[:, 0:128])], True, False), ["m1", "kcn"], ["P0"])
        mm(group([(P3[:, 128:192], NID, T.kcn[:, 128:192])], True, False), ["m1", "kcn"], ["P3"])
        for a, e in CH:
            tt(T.xx[:, 256 * a:256 * e], T.mt[:, 0:W].indirect(T.eo[:, 192 * b + 16 * a:192 * b + 16 * e]),
               T.zt[:, 1024 * b:1024 * b + 256 * (e - a)], ALU.subtract, ["M", "eo%d" % b, "zt%d" % b], XK[a:e], "g")
        if t > 1: list_update(t - 2)
        if t: hints(t - 1)
        for a, e in CH:
            act(T.wx[:, 256 * a:256 * e], T.xx[:, 256 * a:256 * e], absf, XK[a:e], AK[a:e])
            if e % 4 == 0:
                j = a // 4
                mm(group(wrap((P0, P0, P3)[j][:, 64 * j:64 * j + 64], WD, T.wx, 1024 * j, 1024 * j + 1024), False, j > 0),
                   AK[4 * j:4 * j + 4] + ["w0"], [("P0", "P0", "P3")[j]])
        if t:
            hints_p(t - 1); arrive_em(t - 1)
        else:
            cp(T.tf[0:64, :], T.ti[0:64, :], ["ti"], ["tf"])
            add("p", lambda: P.transpose(P7[:, 0:64], T.tf[0:64, :], T.idf[0:64, 0:64]), ["tf", "idf"], ["P7"], 0.3)
            late_constants(); threshold(0)
        mm(group([(P6[:, 16 * s:192], IB, T.d0[:, 0:192 - 16 * s]) for s in range(12)]), ["d0", "m2"], ["P6"])
        if t: list_mask()
        act(T.lead[:], P6[:, 0:192], relu, ["P6"], ["lead"], bias=1.0, scale=-1.0)
        TA, TB, TC, TD = [P6[:, 192 + 16 * i:208 + 16 * i] for i in range(4)]
        nh = T.lead[:, 176:192]
        mm(group([(P6[:, 192:256], ID, T.tk0[:, 0:64]), (P6[:, 192:256], IBIG, T.tk0[:, 64:128])]
                 + [(TA, I16, T.lead[:, 16 * k:16 * k + 16]) for k in range(12)] + [(TB, NBIG, nh), (TC, IBIG, nh)]
                 + [(TD, I16, nh) for k in range(t + 1)], True, False),
           ["lead", "m0", "m6", "m9", "m10"] + ["tq%d" % i for i in range(6)], ["P6"])
        for pb, pk, x, y, n in ((P0, "P0", 0, 128, "ka"), (P3, "P3", 128, 192, "kb")):
            tt(T.kb[:, 0, x:y], pb[:, x:y], T.d0[:, x:y], ALU.add, [pk, "d0"], [n + "0"])
            tt(T.kb[:, 1, x:y], pb[:, x:y], T.d0[:, x:y], ALU.subtract, [pk, "d0"], [n + "1"])
            tt(T.kb[:, 2, x:y], T.d2[:, x:y], pb[:, x:y], ALU.subtract, [pk, "d2"], [n + "2"])
        tt(T.t1[:, :, 0:64], T.kb[:, :, 0:64], T.kb[:, :, 64:128], ALU.min, ["ka0", "ka1", "ka2"], ["t0a"])
        tt(T.t2[:], T.t1[:, :, 0:32], T.t1[:, :, 32:64], ALU.min, ["t0a"], ["t1a"])
        tt(T.t3[:, :, 0:16], T.t2[:, :, 0:16], T.t2[:, :, 16:32], ALU.min, ["t1a"], ["t3a"])
        tt(T.t1[:, :, 64:96], T.kb[:, :, 128:160], T.kb[:, :, 160:192], ALU.min, ["kb0", "kb1", "kb2"], ["t0b"])
        tt(T.t3[:, :, 16:32], T.t1[:, :, 64:80], T.t1[:, :, 80:96], ALU.min, ["t0b"], ["t3b"])
        tt(T.rr[:], T.t3[:, :, 0:16], T.t3[:, :, 16:32], ALU.min, ["t3a", "t3b"], ["rr"])
        ts(T.rk[:], T.rr[:], 255, None, ALU.bitwise_and, None, ["rr"], ["rk"])
        ts(T.off[:], T.rk[:], 16.0, rcol, ALU.mult, ALU.add, ["rk", "pc"], ["off"])
        of, os_, om = T.off[:, 0:16], T.off[:, 16:32], T.off[:, 32:48]
        nf, nk = nfs(t), "nf%d" % t
        tt(nf, T.rr[:, 0, :], P5[:, 464:480], ALU.is_ge, ["rr", "P5"], [nk])
        ts(T.rkb[:], T.rk[:, 0:2, :], 1.0, None, ALU.mult, None, ["rk"], ["rkb"])
        mm(group([(TA, IBIG, nf), (TB, IBIG, nf), (TC, NBIG, nf), (TD, IBIG, nf), (P6[:, 208:240], ID, T.rkb[:])], False, True),
           [nk, "rkb", "m0", "m9", "m10"], ["P6"])
        mm(group([(P0[:, 0:16], I16R, T.lanec[:]), (P0[:, 0:16], ID, tk(0))], True, False), ["m0", "m7", "lanec", "tk0"], ["P0"])
        gat(T.nf_[:], T.oa[:].indirect(of), OAK + ["off"], ["nbf"])
        gat(T.kq[:, 0:256], T.oa[:].indirect(om), OAK + ["off", "cs14", "cs15"], ["nbm"], scale=cs(14), bias=cs(15))
        mm(group(wrap(P3[:, 0:16], WNS, T.nf_, 0, 256) + [(P3[:, 0:16], I2, nf)]), ["nbf", "w7", "m12", nk], ["P3"])
        mm(group(wrap(P0[:, 0:16], WP, T.nf_, 0, 256), False, True), ["nbf", "w6"], ["P0"])
        mm(group([(P5[:, 16:272], RN, T.nf_[:])]), ["nbf", "m4"], ["P5"])
        gat(T.sz[:, 256 * t:256 * t + 256], T.xx[:, 0:3072].indirect(of), XK + ["off"], ["sz%d" % t], f=absf)
        send(t, T.lz[:, 256 * t:256 * t + 256], T.sz[:, 256 * t:256 * t + 256], "az%d" % t, ["sz%d" % t])
        if t: arrive_k(t - 1)
        else:
            for q in range(4):
                if q: cp(T.eo[:, 192 * q:192 * q + 192], T.ei[:, 192 * q:192 * q + 192], ["ei1"], ["eo%d" % q])
                ts(T.ec[:, 192 * q:192 * q + 192], T.ei[:, 192 * q:192 * q + 192], -2048.0, None, ALU.add, None, ["ei1" if q else "ei0"], [EK[q]])
        ts(su(0), P3[:, 0:16], 4096.0, W - 1.0, ALU.mult, ALU.min, ["P3"], ["efu"])
        ts(T.su[:, 16:24], P3[:, 1:16:2], 4096.0, W - 1.0, ALU.mult, ALU.min, ["P3"], ["efo"])
        gat(T.kq[:, 256:512], T.kt[:, 0:W].indirect(su(0)), KT + ["efu"], ["kg"], bias=-2048.0)
        gat(T.kq[:, 512:640], T.kt[:, 0:W].indirect(T.su[:, 16:24]), KT + ["efo"], ["kg2"], bias=-2048.0)
        tt(f1, P3[:, 0:16], T.dm[:], ALU.min, ["P3", "dm"], ["f1"])
        if t: hints_b(t - 1)
        mm(group(wrap(P1[:, 0:32], WH16, T.kq, 0, 512) + [(P1[:, 16:32], IBIG, nf)]), ["kg", "nbm", "wh16", "m9", nk], ["P1"])
        cm, ck = cms(t), "cm%d" % (t % 2)
        act(T.erow[:], P5[:, 16:272], ident, ["P5"], ["erow"], scale=1.0 / 4096)
        ts(pu1, P0[:, 0:16], MAGIC, None, ALU.add, None, ["P0"], ["pu1"])
        tt(T.clb[:], P0[:, 0:16], T.vq[:], ALU.is_lt, ["P0", "vq"], ["clb"])
        ts(su(4), pu1, -MAGIC, 15.0, ALU.add, ALU.min, ["pu1"], ["pu"])
        tt(fav, f1, T.clb[:], ALU.add, ["f1", "clb"], ["fav"])
        mm(group([(P0[:, 16:32], ID, tk(1)), (P0[:, 16:32], ID, tk(2)), (P0[:, 16:32], I2, T.clb[:])], True, False),
           ["m0", "m12", "tk1", "tk2", "clb"], ["P0"])
        tt(T.eq2[:], fav.indirect(su(4)), T.erow[:], ALU.is_equal, ["fav", "pu", "erow"], ["eq2"], "g")
        mm(group(wrap(P0[:, 16:32], W2, T.eq2, 0, 256), False, True), ["eq2", "w3"], ["P0"])
        tt(so, P0[:, 16:32], f1, ALU.max, ["P0", "f1"], ["so"])
        ts(T.sn[:, 48 * t:48 * t + 16], so, 4096.0, None, ALU.mult, None, ["so"], ["sn%d" % t])
        send(t, T.ln[:, 32 * t:32 * t + 16], T.sn[:, 48 * t:48 * t + 16], "an%d" % t, ["sn%d" % t])
        cp(cm, P1[:, 16:32], ["P1"], [ck])
        ts(T.sn[:, 48 * t + 16:48 * t + 48], P1[:, 0:32], 2048.0, W - 1.0, ALU.add, ALU.min, ["P1"], ["sm%d" % t])
        send(t, T.ln[:, 32 * t + 16:32 * t + 32], T.sn[:, 48 * t + 16:48 * t + 32], "ae%d" % t, ["sm%d" % t])
        mm(group([(P2[:, 0:24], ID, T.tk[:, 64:88]), (P2[:, 0:16], ID, tk(6))], True, False), ["m0", "tk4", "tk5", "tk6"], ["P2"])
        tt(T.eq[:], cm.indirect(T.bcc[:]), T.kq[:, 256:640], ALU.is_equal, [ck, "bcc", "bcc1", "kg", "kg2"], ["eq"], "g")
        mm(group(wrap(P2[:, 0:24], WBIG, T.eq, 0, 384), False, True), ["eq", "w1"], ["P2"])
        gat(T.keepv[:], T.ot[:, 0:W].indirect(T.sn[:, 48 * t + 32:48 * t + 48]), OT + ["sm%d" % t, "keep%d" % (4 + b % 2), "keep%d" % (6 + b)], ["keepv"],
            bias=cs(6 + b), scale=cs(4 + b % 2))
        tt(tc, P2[:, 0:16], cm, ALU.max, ["P2", ck], ["tc"])
        tco = T.sm[:, 17:32:2]; tce = T.sm[:, 16:32:2]
        tt(tco, tco, P2[:, 16:24], ALU.add, ["P2", "tc"], ["tco"])
        ts(T.oc[:, 0:16:2], tce, 2048.0, dcol, ALU.add, ALU.min, ["tc", "dcol"], ["oce"])
        ts(T.oc[:, 1:16:2], tco, 2048.0, dcol2, ALU.add, ALU.min, ["tco", "dcol2"], ["oco"])
        act(tq, P6[:, 192:224], ident, ["P6"], ["tq"])
        tt(fa, TD, T.rk[:, 0, :], ALU.max, ["P6", "rk"], ["fa"])
        tt(ra, TC, sm(11), ALU.min, ["P6", "tq"], ["ra"])
        tt(T.rowb[:], ra, sm(10), ALU.min, ["ra", "tq"], ["rowb"])
        ts(su(3), fa, 16.0, rcol, ALU.mult, ALU.add, ["fa", "pc"], ["fo"])
        gat(T.sb[:], T.oa[:].indirect(os_), OAK + ["off"], ["sb"])
        if t == 0:
            mm(group(wrap(P7[:, 0:16], WN, T.sb, 0, 256)), ["w4", "sb"], ["P7"])
            cp(su(2), P7[:, 0:16], ["w4", "P7"], ["colu"])
            gat(T.sb[:], T.ot[:, 0:W].indirect(su(2)), OT + ["colu"], ["sb"])
        mm(group([(P7[:, 16:272], R3, T.sb[:])]) + group([(P7[:, 0:16], ID, T.kcn[:, 0:16]), (P7[:, 0:16], ID, T.rkb[:, 16:32])]
                 + wrap(P7[:, 0:16], WC, T.sb, 0, 256)), ["sb", "w5", "m0", "m5", "kcn", "rkb"], ["P7"])
        cp(su(2), P7[:, 0:16], ["P7"], ["colu"])
        act(T.mm[:], P7[:, 16:272], relu, ["P7", "rsq"], ["mm"], bias=rsq, scale=-1.0)
        gat(T.xs[:], T.xx[:, 0:3072].indirect(os_), XK + ["off"], ["xs"], bias=1535.75, scale=0.5)
        mm(group([(P6[:, 0:256], ID, T.xx[:, zb:zb + 256]), (P6[:, 0:256], IDH, T.xs[:])]), ["xs", zk, "m0", "idh"], ["P6"])
        act(T.xx[:, HCOL:HCOL + 256], P6[:, 0:256], ident, ["P6"], ["H"], bias=-1536.0)
        if t: list_bounds()
        vb = 256 * (b % 2)
        for m in range(7, -1, -1):
            tt(T.ot[:].indirect(T.oc[:, 2 * m:2 * m + 2]), T.keepv[:, 32 * m:32 * m + 32], T.vl[:, vb + 32 * m:vb + 32 * m + 32], ALU.add,
               ["oce", "oco", "keepv", "vl0", "vl1"], OT, "s")
        if t == RO - 1:
            step[0] = RO
            arrive(t)
            dma("y", [(T.ym[:], T.mt[:, 0:W])], ["M"], [], 4.9)
        if t < 4:
            gat(T.xx[:, Z1 + lo:Z1 + lo + 256], T.xx[:, 0:Z1].indirect(su(3)), XK + ["H", "fo", "Z0"], ["Z1_%d" % b], f=absf)
            dma("y", [(T.zt[:, 1024 * b + 256 * j:1024 * b + 256 * j + 256], T.xx[:, Z1 + lo:Z1 + lo + 256]) for j in range(4)],
                ["Z1_%d" % b], ["zt%d" % b])
        else:
            gat(T.zo[:, lo:lo + 256], T.xx[:].indirect(su(3)), XK + ["H", "fo", zk], ["zo%d" % b], f=absf)
            dma("y", [(T.yz[:, lo:lo + 256], T.zo[:, lo:lo + 256])], ["zo%d" % b], [])
        if t >= RO - 2: dma("y", [(T.yo[8 * (t % 2):8 * (t % 2) + 8, :], T.ot[t % 2::16, 0:W])], OT, [])
        if t + 1 < RO: owners(t + 1)
    mm(group([(P3[0:64, 0:128], T.thh[:, 0:64], ID), (P3[0:64, 0:128], T.thh[:, 64:128], ID),
              (P3[0:64, 0:128], T.nfs[:, 0:64], I128), (P3[0:64, 0:128], T.nfs[:, 64:128], I128)]),
       ["thh", "thl", "m0", "m11"] + ["nf%d" % i for i in range(RO)], ["P3"])
    arrive_em(RO - 1)
    act(T.tf[0:64, :], P3[0:64, 0:128], ident, ["P3"], ["tf"])
    dma("s", [(T.yt[q, :], T.tf[0:64, 16 * q:16 * q + 16]) for q in range(8)], ["tf"], [])
    list_update(RO - 2)
    hints(RO - 1); hints_p(RO - 1)
    arrive_k(RO - 1)
    dma("y", [(T.yk[:], T.kt[0::16, 0:W])], KT, [])
    list_mask(); hints_b(RO - 1); list_bounds()
    list_update(RO - 1)

    queue = {"v": V, "s": S, "p": P, "g": g, "y": g.sync}
    csem = {"v": "cv", "s": "cs", "p": "cp", "g": "cg"}
    named = {}
    for n, o in enumerate(ops): named.setdefault((o["e"], o["step"], o["lab"]), []).append(n)
    for e, names in CHAIN.items():
        row = []
        for t in range(RO):
            for x in names.split():
                x, _, k = x.partition("#"); calls = named.get((e, t + x.count("+"), x.rstrip("+")), [])
                k = int(k) if k else len(calls)
                row += calls[:k]; del calls[:k]
        for a, b in zip(row, row[1:]): ops[b]["soft"].add(a)
    succ = [[] for _ in ops]
    for n, o in enumerate(ops):
        o["all"] = [(x, ops[x]["lat"] + WAKE) for x in o["d"]] + [(x, 0.0) for x in o["soft"]] + [(x, REM) for x in o["far"]]
        for x, l in o["all"]: succ[x].append((n, l))
    left = [len(o["all"]) for o in ops]; forward = [n for n, k in enumerate(left) if not k]
    for n in forward:
        for y, l in succ[n]:
            left[y] -= 1
            if not left[y]: forward.append(y)
    tail = [0.0] * len(ops)
    for n in reversed(forward):
        tail[n] = ops[n]["c"] + max([l + tail[y] for y, l in succ[n]] + [ops[n]["lat"]])
    busy = {e: [] for e in queue}; begin = [0.0] * len(ops)
    for n in sorted(forward, key=lambda x: (-tail[x], x)):
        o = ops[n]; t0 = max([begin[x] + ops[x]["c"] + l for x, l in o["all"]] + [0.0]); row = busy[o["e"]]; i = 0
        while i < len(row) and row[i][0] < t0 + o["c"] - SLACK:
            t0 = max(t0, row[i][1]); i += 1
        row.insert(i, (t0, t0 + o["c"])); begin[n] = t0
    order = sorted(range(len(ops)), key=lambda x: (begin[x], x))
    pos = {n: i for i, n in enumerate(order)}
    ops = [ops[n] for n in order]
    for o in ops: o["d"] = [pos[x] for x in o["d"]]
    needed = set()
    for o in ops:
        best = {}
        for x in o["d"]:
            if ops[x]["tok"] is None: best[ops[x]["e"]] = max(best.get(ops[x]["e"], -1), x)
        o["d"] = [x for x in o["d"] if ops[x]["tok"] is not None] + list(best.values())
    seen = {e: {} for e in queue}
    for o in ops:
        keep = []
        for x in o["d"]:
            if ops[x]["tok"] is None:
                if seen[o["e"]].get(ops[x]["e"], -1) >= x: continue
                seen[o["e"]][ops[x]["e"]] = x; needed.add(x)
            keep.append(x)
        o["d"] = keep
    count = {e: 0 for e in csem}
    waited = {e: {} for e in queue}
    done = set()
    for n, o in enumerate(ops):
        e = o["e"]
        for name, val in [ops[x]["tok"] for x in o["d"]] + list(o["ext"] or []):
            if waited[e].get(name, 0) < val:
                queue[e].wait_ge(T.sem[name], val); waited[e][name] = val; done.add(name)
        ins = o["fn"]()
        if n in needed:
            count[e] += 1
            ins.then_inc(T.sem[csem[e]], 1)
            o["tok"] = (csem[e], count[e])
    for o in ops:
        if o["tok"] is not None and o["tok"][0] in DSEMS and o["tok"][0] not in done:
            g.sync.wait_ge(T.sem[o["tok"][0]], o["tok"][1])
    g.wait_ge(T.sem.sent, sent[0])
